import numpy as np, ml_dtypes
CORES = [35,38,43,46]
N = 4
BF = ml_dtypes.bfloat16
V, H, LB, K, T, TH = 4096, 2048, 12, 256, 5, 5
ODD = (np.arange(16) & 1)[:, None]
def before(w):
    return np.concatenate([np.zeros_like(w[..., :1, :]), w[..., :-1, :]], axis=-2) * ODD
def follow(rng, cyc):
    F = rng.integers(0, V, (8, 16, V))
    for g in range(8):
        for k in range(16):
            e = np.roll(cyc[g], -(k + 1))
            F[g, k, cyc[g]] = (e + np.roll(cyc[g], -1)) & (V - 1) if k & 1 else e
    return F
def chain(cyc, b):
    return np.take_along_axis(cyc[:, None, :], (b[:, None, :] - np.arange(16)[None, :, None]) % cyc.shape[1], 2)
def spoil(rng, F, share):
    return np.where(rng.random(F.shape) < share, rng.integers(0, V, F.shape), F)
def pack(F, x, w):
    return {"fld": (F[..., :H] + V * F[..., H:]).reshape(N, 128, H).astype(np.int32), "rec": np.ascontiguousarray(x).reshape(N, 128, V).astype(np.float32).astype(BF),
            "wnd": np.ascontiguousarray(w).reshape(N, 128, K).astype(np.int32)}
def setup_inputs(rng):
    cyc = np.argsort(rng.random((8, V)), axis=-1); F = np.stack([follow(rng, cyc)] * N)
    F = spoil(rng, F, rng.choice(np.array([0.12, 0.35, 0.55, 0.68]), (N, 8, 1, 1)))
    w = np.stack([chain(cyc, rng.integers(0, V, (8, K))) for r in range(N)])
    w = spoil(rng, w, rng.choice(np.array([0.0, 0.0, 0.06, 0.06, 0.06, 0.2, 0.2, 1.0]), (N, 8, 1, K)))
    return pack(F, rng.integers(0, 16, (N, 8, 16, V)), w)
def setup_inputs_spread(rng):
    cyc = np.argsort(rng.random((8, V)), axis=-1); F = np.stack([follow(rng, cyc)] * N)
    low = np.minimum((V * rng.random(F.shape) ** 4).astype(np.int64), V - 1)
    F = np.where(rng.random(F.shape) < 0.85 * rng.random((N, 8, 1, 1)) ** 1.5, low, F)
    w = np.stack([chain(cyc, np.minimum((V * rng.random((8, K)) ** 3).astype(np.int64), V - 1)) for r in range(N)])
    w = spoil(rng, w, 0.5 * rng.random((N, 8, 1, K)) ** 3)
    x = np.minimum((16 * rng.random(F.shape) ** np.exp2(rng.integers(-2, 4, (N, 8, 1, V)))).astype(np.int64), 15)
    return pack(F, x, w)
def setup_inputs_ends(rng):
    e = V - 1
    F = e * np.tile(rng.integers(0, 2, (N, 8, 16, H)), (1, 1, 1, 2))
    x = 15 * np.where(rng.random((N, 8, 1, V)) < 0.5, rng.integers(0, 2, (N, 8, 1, V)), rng.integers(0, 2, (N, 8, 16, V)))
    w = e * (rng.random((N, 8, 16, K)) < rng.choice(np.array([0.1, 0.5, 0.9]), (N, 8, 1, K))).astype(np.int64)
    F[:, 4:, :, 0] = 0; F[:, 4:, :, H] = 0; F[:, 4:, :, H - 1] = e; F[:, 4:, :, e] = e
    for c in (0, 1, e):
        x[:, 4, :, c] = 0; x[:, 5, :, c] = 15
    for g in (6, 7):
        x[:, g, :, 0] = 0; x[:, g, :, 1] = 0; x[:, g, :, e] = 15
    x[:, 6, 8:, 1] = 15
    pat = np.zeros((7, 16), np.int64)
    pat[0, 15] = 1; pat[1, 14] = 1; pat[2, 2] = 1; pat[2, 15] = 1; pat[3] = np.array([0, 1] * 7 + [1, 0]); pat[4] = np.array([0, 1] + [1, 0] * 7); pat[5] = 1
    pt = rng.integers(0, 7, (N, 4, K))
    pt[:, 0:2, K - 1] = 4; pt[:, 0:2, 0] = 4; pt[:, 2, K - 1] = 3; pt[:, 2, 1] = 3; pt[:, 3, K - 1] = 0; pt[:, 3, 0] = 2; pt[:, 3, 1] = 6
    pt[N - 1, 3] = 6; pt[N - 1, 3, K - 1] = 0
    w[:, 4:] = e * np.moveaxis(pat[pt], 3, 2)
    return pack(F, x, w)
def setup_inputs_corners(rng):
    R = V // 8; inner = 1 + np.argsort(rng.random((8, V - 2)), axis=-1)
    out = np.concatenate([np.tile(np.array([0, V - 1]), (8, 1)), inner[:, :R - 2]], axis=1); cyc = np.ascontiguousarray(inner[:, R - 2:])
    F = np.stack([follow(rng, cyc)] * N); x = rng.integers(0, 16, (N, 8, 16, V)); s0 = int(rng.integers(0, N)); q = [(s0 + i) % N for i in range(N)]
    b = np.argsort(rng.random((N, 8, V - R)), axis=-1)[..., :K]
    w = np.stack([chain(cyc, b[r]) for r in range(N)])
    for r in (q[1], q[3]):
        F[r] = spoil(rng, F[r], 0.58)
        F[r, :, :, ::16] = 16 * rng.integers(0, V // 16, (8, 16, V // 16)) + np.arange(16)[None, :, None]
        w[r] = 16 * rng.integers(0, V // 16 - 1, (8, 16, K))
    g = int(rng.integers(0, 8)); m = int(rng.integers(0, V))
    w[q[1], g, :, int(rng.integers(0, K))] = V - 16; F[q[1], g, 0::2, V - 16] = m; F[q[1], g, 1::2, V - 16] = (m + V - 16) & (V - 1)
    for r in [q[2]] + q[4:]:
        x[r] = 7 + rng.integers(0, 2, (8, 16, V))
        for h in range(8):
            x[r, h][:, out[h, ::2]] = 0; x[r, h][:, out[h, 1::2]] = 15
        w[r, 3] = cyc[3, b[r, 3]][None, :]; F[r, 3, 0::2] = np.arange(V); F[r, 3, 1::2] = (2 * np.arange(V)) & (V - 1)
        v = rng.choice(np.array([1, TH - 1, TH, TH + 1, 15, 16]), (8, 1, K)); o = np.argsort(rng.random((8, 16, K)), axis=1)
        y = np.take_along_axis(out[:, None, :], (rng.integers(0, R, (8, 1, K)) + o) % R, 2)
        new = (y + before(w[r])) & (V - 1); old = np.take_along_axis(F[r], w[r], 2)
        np.put_along_axis(F[r], w[r], np.where(o >= v, new, old), 2)
    return pack(F, x, w)
def setup_inputs_crowd(rng):
    cyc = np.argsort(rng.random((8, V)), axis=-1); F = np.stack([follow(rng, cyc)] * N)
    a = int(rng.integers(0, N)); e = (a - 1) % N; p = (a + 1) % N; q = (a + 2) % N
    share = np.tile(np.array([0.0, 0.0, 0.1, 0.0, 0.0, 0.1, 0.1, 0.3]).reshape(1, 8, 1, 1), (N, 1, 1, 1))
    for r in (e, a, p, q): share[r, 7] = 0.0
    share[p] = 0.0; share[q] = 0.0
    F = spoil(rng, F, share)
    x = rng.integers(0, 8, (N, 8, 16, V)); x[:, 7] = rng.integers(0, 16, (N, 16, V))
    b = rng.integers(64, V - 64, (N, 8, K))
    b[:, 3] = 64 + np.argsort(rng.random((N, V - 128)), axis=-1)[:, :K]
    b[:, 7] = H + 64 + np.argsort(rng.random((N, H - 128)), axis=-1)[:, :K]; b[a, 7] = b[a, 7] - H
    w = np.stack([chain(cyc, b[r]) for r in range(N)])
    for g in (0, 1, 2, 4, 5, 6):
        bad = cyc[g, :3]; o = int(cyc[g, 4]); x[:, g, :, o] = 15
        for c in bad: F[:, g, 0::2, c] = o
        for r in range(N):
            if r == p: continue
            k = 2 * rng.integers(0, 8, K); c = bad[rng.integers(0, 3, K)] if g == 6 else np.full(K, bad[0]); j = np.arange(K)
            if g in (4, 5): j = np.delete(j, int(rng.integers(0, K)))
            w[r, g, k[j], j] = c[j]
    o = int(cyc[3, 4]); x[:, 3, :, o] = 15; k0 = int(rng.integers(0, 16))
    for r in range(N):
        k = (k0 + 5 * r) % 16
        F[r, 3, k, w[r, 3, k]] = (o + before(w[r, 3])[k]) & (V - 1)
    out = cyc[7, 8:40]
    for r, whose, t in ((a, e, 1), (q, a, 2)):
        x[r, 7] = 7 + rng.integers(0, 2, (16, V)); x[r, 7][:, out[::2]] = 0; x[r, 7][:, out[1::2]] = 15
        then = chain(cyc[7:], b[whose, 7][None, :] + t)[0]
        v = rng.choice(np.array([TH - 1, TH, TH, TH + 1]), (1, K)); turn = np.argsort(rng.random((16, K)), axis=0)
        y = out[(rng.integers(0, 32, (1, K)) + turn) % 32]
        new = (y + before(then)) & (V - 1); old = np.take_along_axis(F[r, 7], then, 1)
        np.put_along_axis(F[r, 7], then, np.where(turn >= v, new, old), 1)
    for g in (2, 5): w[a, g] = rng.integers(0, V, (16, K))
    w[q, 7, :, int(rng.integers(0, K))] = rng.integers(0, V, 16)
    return pack(F, x, w)
def setup_inputs_ties(rng):
    cyc = np.argsort(rng.random((8, V)), axis=-1); F = np.stack([follow(rng, cyc)] * N)
    r0 = int(rng.integers(0, N)); r1 = (r0 + 1) % N; r2 = (r0 + 2) % N
    sf = rng.choice(np.array([0.05, 0.2, 0.45]), (N, 8, 1, 1)); sw = rng.choice(np.array([0.0, 0.05, 0.2]), (N, 8, 1, K))
    for s in (sf, sw):
        s[r1] = 0.0; s[r2] = 0.0; s[r0, 6:] = 0.0
    F = spoil(rng, F, sf)
    b = rng.integers(0, V, (N, 8, K))
    b[:, 6:] = H + 64 + np.argsort(rng.random((N, 2, H - 128)), axis=-1)[..., :K]; b[r0, 6:] = b[r0, 6:] - H
    w = np.stack([chain(cyc, b[r]) for r in range(N)]); w = spoil(rng, w, sw)
    kind = rng.integers(0, 4, (N, 8, 1, V)); kind[:, 0] = 0
    x = np.take_along_axis(rng.integers(0, 16, (N, 8, 16, 4)), kind, 3)
    w[r1, int(rng.integers(0, 6)), :, int(rng.integers(0, K))] = rng.integers(0, V, 16)
    two = chain(cyc[7:], b[r1, 7, rng.permutation(K)[:2]][None, :] + 1)[0]
    np.put_along_axis(F[r2, 7], two, rng.integers(0, V, (16, 2)), 1)
    for r, g, t in ((r1, 7, 1), (r2, 6, 2)):
        out = cyc[g, 8:40]
        x[r, g] = (7 + rng.integers(0, 2, (16, 4)))[:, kind[r, g, 0]]; x[r, g][:, out[::2]] = 0; x[r, g][:, out[1::2]] = 15
        then = chain(cyc[g:g + 1], b[r0, g][None, :] + t)[0]
        v = rng.choice(np.array([TH - 1, TH, TH, TH + 1]), (1, K)); turn = np.argsort(rng.random((16, K)), axis=0)
        y = out[(rng.integers(0, 32, (1, K)) + turn) % 32]
        new = (y + before(then)) & (V - 1); old = np.take_along_axis(F[r, g], then, 1)
        np.put_along_axis(F[r, g], then, np.where(turn >= v, new, old), 1)
    return pack(F, x, w)
def check_inputs(d):
    bad = []
    for k, hi in (("fld", V * V - 1), ("rec", 15), ("wnd", V - 1)):
        v = np.asarray(d[k]).astype(np.float64)
        if not (np.all(v >= 0) and np.all(v <= hi)): bad.append("range of " + k)
    v = np.asarray(d["rec"]).astype(np.float64)
    if not np.all(v == np.floor(v)): bad.append("whole numbers in rec")
    return bad
def reference(fld, rec, wnd):
    pk = fld.astype(np.int64).reshape(N, 8, 16, H); F = np.concatenate([pk & (V - 1), pk >> LB], axis=3)
    X = rec.astype(np.float32).astype(np.int64).reshape(N, 8, 16, V)
    here = [a for a in wnd.astype(np.int64).reshape(N, 8, 16, K)]
    A = np.zeros(N, np.int64); wt = (2 * np.arange(16) + 1)[None, :, None]
    for t in range(T):
        left = []
        for q in range(N):
            w = here[q]; pv = before(w)
            e = (np.take_along_axis(F[q], w, 2) - pv) & (V - 1)
            x = np.take_along_axis(X[q], e.reshape(8, 1, 16 * K), 2).reshape(8, 16, 16, K)
            M = np.add.reduce(x, axis=2) >> 4
            d = np.add.reduce(np.abs(x - M[:, :, None, :]), axis=1)
            lo = np.argmin(d, axis=1)[:, None, :]; hi = np.argmax(d, axis=1)[:, None, :]
            n = np.take_along_axis(e, lo, 1)
            s = np.add.reduce((e == n).astype(np.int64), axis=1)
            go = s >= TH + (A[q] & 1)
            want = go & (np.take_along_axis(e, hi, 1) != n)[:, 0]
            col = np.take_along_axis(w, hi, 1)[:, 0]; val = ((n + np.take_along_axis(pv, hi, 1)) & (V - 1))[:, 0]
            for g in range(8):
                i = np.flatnonzero(want[g]); c, first = np.unique(col[g, i], return_index=True); i = i[first]
                F[q, g, hi[g, 0, i], c] = val[g, i]
            u = np.add.reduce(M * wt, axis=1); z = ((u * u >> 5) + 37 * u) & (V - 1)
            A[q] = np.count_nonzero(~go)
            left.append(np.where(go[:, None, :], np.concatenate([n, w[:, :15]], axis=1), np.concatenate([z[:, None, :], w[:, 14::-1]], axis=1)))
        here = left if t == T - 1 else [left[(q - 1) % N] for q in range(N)]
    return {"yf": (F[..., :H] + V * F[..., H:]).reshape(N, 128, H).astype(np.float32), "yw": np.stack(here).reshape(N, 128, K).astype(np.float32)}

@@ -1,0 +1,694 @@
+from concourse.mybir import AluOpType as A, ActivationFunctionType as F
+
+V, H, K, NV = 4096, 2048, 256, 5
+MAG = 1.5 * 2.0 ** 36
+LCH = 4
+PC = [(0, 32, 0), (32, 32, 0), (64, 64, 0), (128, 64, 0), (192, 64, 6)]
+AF = 4
+MV = [1, 1]
+UNP = ()
+EARLY = 200
+KD = [list(range(0, 8)), list(range(0, 8))]
+ORDER = ("A G0 T0 P0 G1 T1 N0 P1 Xa0 F0 G2 T2 N1 Xa1 F1 G3 F2 P2 F3 G4 N2 N4 Xa2 Xa3 G5 P3 S0 Xa6 S1 Xv7 N3 Xa4 Xv5 W4 W0123 K0 M0 S3 S2 "
+         "M1 K1 Z0 Z1 Z2 Z3 V0a V0b D0a B0a D0b B0b E0v E0a R0 V1a V1b D1a B1a D1b B1b H E1v E1a R1")
+FIRST = ("B1b N2 N1 N4 A P1 G0 T2 N0 G1 F2 P2 G3 Xa1 Xa3 T1 M0 D0b M1 K0 Z0 G2 G5 S1 Xa4 T0 F3 Z1 Xa2 V0b V1b Z2 V0a W0123 Xa0 W4 F1 S2 "
+         "P0 Z3 Xv5 B1a D0a V1a G4 Xv7 R1 S3 K1 D1b EQ P3 N3 D1a S0 B0a GO R0 Xa6 F0 E0a E0v E1v E1a B0b WA P H PT RR PY RQ BO1 Y CW0 "
+         "QF VS KK BO4 WIM7 QC XN4 QK XN0 XC7 OM PS QT WO WO0 SK1 XH2 NI7 OC yw PRD XA3 XC5 NI6 RI AVM3 LS WU KB XN6 OFF K KA LO I7 "
+         "ZL6 XL6 WG WH U FW WF end")
+
+
+def _sb(n, d):
+    return ("sbuf", [128, n], d)
+
+
+SCRATCH = {
+    "PK": _sb(H, "int32"), "HI": _sb(H, "int32"), "FW": _sb(V + 32, "float32"), "REC": _sb(2 * V, "bfloat16"), "YO": _sb(H, "float32"),
+    "WI": _sb(K, "int32"), "WU": _sb(K, "uint16"), "EU": _sb(K, "uint16"), "EH": _sb(K, "float16"), "ET": _sb(K, "bfloat16"),
+    "G1": _sb(V, "float16"), "GF": _sb(1024, "float32"), "X": _sb(V, "bfloat16"), "AD": _sb(V, "bfloat16"), "MB": _sb(K, "bfloat16"),
+    "KF": _sb(1024, "float32"), "RQ": _sb(64, "float32"), "P16": _sb(64, "float16"), "PT": _sb(64, "float16"),
+    "PY": _sb(72, "float32"), "VS": _sb(48, "float32"), "RI": _sb(64, "int32"), "KK": _sb(64, "int32"),
+    "Q16": _sb(192, "float16"), "QT": _sb(192, "float16"), "SQ": _sb(16, "float32"), "ZI": _sb(16, "int32"), "ZA": _sb(16, "int32"),
+    "EQ": _sb(K, "bfloat16"), "GO": _sb(K, "bfloat16"), "WA": _sb(K, "bfloat16"), "PRD": _sb(K, "float32"),
+    "ACC": _sb(4, "float32"), "PI": _sb(4, "int32"), "PJ": _sb(4, "int32"), "THR": _sb(4, "float32"),
+    "Y2": _sb(128, "float16"), "RR": _sb(K, "float16"), "OC": _sb(16, "uint16"), "U": _sb(K, "bfloat16"),
+    "OM": _sb(K, "float32"), "LS": _sb(K, "float32"), "PS": _sb(2 * K, "float32"), "LO": _sb(32, "float32"), "K2": _sb(16, "float32"),
+    "K3": _sb(16, "float32"), "K4": _sb(16, "float32"), "OFF": _sb(16, "uint16"), "WF": _sb(K, "float32"), "WG": _sb(K, "float32"),
+    "RM": _sb(240, "float32"), "RG": _sb(128, "float32"), "RK": _sb(384, "float32"), "CP": _sb(4, "int32"), "CI": _sb(8, "int32"),
+    "CF": _sb(8, "float32"), "CC": _sb(32, "float32"), "MK": _sb(16, "float32"), "QM": _sb(4, "float32"),
+    "ISH": _sb(256, "bfloat16"), "NSH": _sb(128, "bfloat16"), "I16": _sb(128, "bfloat16"), "NI": _sb(128, "bfloat16"),
+    "NI2": _sb(128, "bfloat16"), "WIM": _sb(128, "bfloat16"), "DO": _sb(128, "bfloat16"), "SK": _sb(2048, "bfloat16"), "SKF": _sb(2048, "float32"),
+    "ZL": _sb(128, "bfloat16"), "O32": _sb(128, "bfloat16"), "O32F": _sb(128, "float32"), "MVH": _sb(128, "bfloat16"), "TBH": _sb(128, "bfloat16"),
+    "HDM": _sb(128, "bfloat16"), "AVM": _sb(128, "bfloat16"), "BO": _sb(128, "bfloat16"), "B8": _sb(8, "float32"),
+    "BP1": _sb(24, "bfloat16"), "BP2": _sb(24, "bfloat16"), "BN": _sb(24, "bfloat16"), "WT8": _sb(8, "bfloat16"),
+    "XN": _sb(640, "bfloat16"), "XL": _sb(640, "bfloat16"), "XC": _sb(640, "bfloat16"), "XH": _sb(640, "bfloat16"), "XA": _sb(640, "bfloat16"),
+    "BM": _sb(4, "float32"),
+    "CW": _sb(240, "bfloat16"), "MS0": _sb(256, "bfloat16"), "MSK": _sb(512, "bfloat16"), "HM": _sb(384, "bfloat16"),
+    "SC": _sb(384, "bfloat16"), "PM": _sb(512, "bfloat16"), "KC": _sb(384, "bfloat16"), "YF0": _sb(8, "float32"), "YOF": _sb(8, "uint16"),
+}
+for _t in range(NV):
+    SCRATCH["WH%d" % _t] = _sb(K, "float16")
+for _t in range(NV - 1):
+    SCRATCH["WO%d" % _t] = _sb(K, "float16")
+for _b in range(8):
+    SCRATCH["B%d" % _b] = ("psum", [128, 512], "float32")
+SEMAPHORES = ["sv", "sa", "sp", "sg", "sent"] + ["arr%d" % _t for _t in range(1, NV)] + ["d%d" % _i for _i in range(16)]
+
+
+TIME = {"G": 880, "GF": 1720, "X": 880, "AD": 170, "KF": 440, "EQ": 300, "GO": 300, "WA": 300, "U": 300, "LS": 300, "PRD": 300, "WO": 300,
+        "WF": 300, "WG": 300, "RR": 300, "PS": 570, "PN": 300, "MSM": 300, "OM": 460, "Y": 250, "MB": 170, "WU": 170, "QT": 140, "RQ": 100, "RI": 100, "P": 160,
+        "VS": 130, "QF": 110, "FW": 120, "HI": 570, "HJ": 570, "YO": 570, "SKF": 1100, "SK": 170, "HM": 400, "MS": 300, "SC": 440, "PM": 300,
+        "MSK": 300, "CW": 280, "HDM": 300, "AVM": 300, "WH": 300, "Z": 200, "PK": 1300, "REC": 5200, "WI": 600}
+TMM = {"SKF": 133, "KCa0": 200, "HDM": 133, "AVM": 133, "ZL": 133, "BO": 133, "NI2": 133, "WIM": 133, "O32F": 133, "I": 67, "NI": 67,
+       "MSK": 266, "SH": 133, "U": 133}
+HOP, SAME, LINK, SLACK = 110, 60, 2600, 60
+
+
+def arrange(ops):
+    n = len(ops)
+    pred = [set() for _ in range(n)]
+    writer, readers, bank = {}, {}, {}
+    for i, o in enumerate(ops):
+        for r in o["r"]:
+            if r in writer:
+                pred[i].add(writer[r])
+        for w in o["w"]:
+            pred[i].update(readers.get(w, []))
+            if w in writer:
+                pred[i].add(writer[w])
+        for b in o["b"]:
+            kind, run, before = bank.get(b, ("w", [], []))
+            if kind == o["k"] != "w":
+                pred[i].update(before)
+                run.append(i)
+            else:
+                pred[i].update(run)
+                bank[b] = (o["k"], [i], run)
+        for r in o["r"]:
+            readers.setdefault(r, []).append(i)
+        for w in o["w"]:
+            writer[w] = i
+            readers[w] = []
+        if "line" in o:
+            if o["line"] in writer:
+                pred[i].add(writer[o["line"]])
+            writer[o["line"]] = i
+        pred[i].discard(i)
+    succ = [[] for _ in range(n)]
+    for i in range(n):
+        for j in pred[i]:
+            succ[j].append(i)
+
+    def lag(j, i):
+        if ops[j].get("line", 0) == ops[i].get("line", 1):
+            return LINK if ops[i]["fn"] is None else 0
+        if ops[j]["src"] != ops[i]["src"]:
+            return HOP + ops[j]["lat"]
+        return SAME if ops[i]["q"] != "p" and (ops[j]["k"] != "r" or ops[i]["k"] != "r" or not ops[j]["b"] or set(ops[j]["w"]) & set(ops[i]["r"])) else 0
+
+    rank = {s: j for j, s in enumerate(FIRST.split())}
+    path, prio = [0.0] * n, [None] * n
+    for i in range(n - 1, -1, -1):
+        o = ops[i]
+        path[i] = o["t"] + max([path[j] + lag(i, j) for j in succ[i]] + [0.0])
+        if o["visit"] >= 0:
+            prio[i] = (-1000 * o["visit"] - rank.get(o["tag"], 999), 0)
+        else:
+            prio[i] = (max(prio[j][0] for j in succ[i]) + EARLY, path[i])
+    left = [len(p) for p in pred]
+    ready = [i for i in range(n) if not left[i]]
+    est, end, free, used, order = [0.0] * n, [0.0] * n, {}, {}, []
+
+    def start(i):
+        o = ops[i]
+        s = max(est[i], free.get(o["q"], 0.0)) if o["fn"] is not None else est[i]
+        for b in o["b"]:
+            for q, e in used.get(b, {}).items():
+                if q != o["q"]:
+                    s = max(s, e + HOP)
+        return s
+
+    while ready:
+        st = {i: start(i) for i in ready}
+        first = min(ready, key=lambda i: (st[i], i))
+        q = ops[first]["q"]
+        i = max((j for j in ready if ops[j]["q"] == q and st[j] <= st[first] + SLACK), key=lambda j: (prio[j], -j))
+        o = ops[i]
+        end[i] = st[i] + o["t"]
+        if o["fn"] is not None:
+            free[q] = end[i]
+        for b in o["b"]:
+            used.setdefault(b, {})[q] = end[i]
+        ready.remove(i)
+        order.append(i)
+        for j in succ[i]:
+            est[j] = max(est[j], end[i] + lag(i, j))
+            left[j] -= 1
+            if not left[j]:
+                ready.append(j)
+    ops[0]["span"] = max(end)
+    return [ops[i] for i in order]
+
+
+def emit(g, T, ops):
+    queues = {"v": g.vector, "a": g.scalar, "p": g.tensor, "g": g, "s": g.sync}
+    writer, readers, bank, clock, seen = {}, {}, {}, {}, {}
+    for i, o in enumerate(ops):
+        q, src = o["q"], o["src"]
+        deps = set()
+        for r in o["r"]:
+            if r in writer:
+                deps.add(writer[r])
+        for w in o["w"]:
+            deps.update(readers.get(w, []) + ([writer[w]] if w in writer else []))
+        for b in o["b"]:
+            for s, j in bank.get(b, {}).items():
+                if s != src or (s != "p" and "w" in (o["k"], ops[j]["k"])):
+                    deps.add(j)
+        know = seen.setdefault(q, {})
+        waits = []
+        for j in sorted(deps, reverse=True):
+            if know.get(ops[j]["src"], -1) < j:
+                waits.append(j)
+                ops[j]["sig"] = True
+                for s, n in clock[j].items():
+                    know[s] = max(know.get(s, -1), n)
+        o["waits"] = waits
+        clock[i] = dict(know) if o["fn"] is not None else {}
+        clock[i][src] = i
+        for r in o["r"]:
+            readers.setdefault(r, []).append(i)
+        for w in o["w"]:
+            writer[w] = i
+            readers[w] = []
+        for b in o["b"]:
+            bank.setdefault(b, {})[src] = i
+    count = {}
+    for o in ops:
+        if o["sem"] is None and o["sig"]:
+            count[o["q"]] = count.get(o["q"], 0) + 1
+            o["sem"], o["val"], o["inc"] = "s" + o["q"], count[o["q"]], 1
+    for o in ops:
+        q = queues[o["q"]]
+        for j in o["waits"]:
+            q.wait_ge(T.sem[ops[j]["sem"]], ops[j]["val"])
+        if o["fn"] is not None:
+            ins = o["fn"](q)
+            if o["inc"]:
+                ins.then_inc(T.sem[o["sem"]], o["inc"])
+
+
+def rank_program(g, core, T, topo):
+    rank = T.rank_of(core)
+    if rank is None:
+        return
+    n = len(T.cores)
+    nxt, prv = T.cores[(rank + 1) % n], T.cores[(rank - 1) % n]
+    rid, pid, _ = topo.addr(nxt)
+    mask_out, n_out, n_in = topo.mask(core, nxt), len(topo.engines(core, nxt)), len(topo.engines(prv, core))
+    ops, nd, lat, now = [], [0], [0], [-1, None]
+    B = [T["B%d" % b] for b in range(8)]
+
+    def op(q, fn, r=(), w=(), b=()):
+        tm = TIME.get(w[0].rstrip("0123456789_"), 90) if w else 90
+        ops.append({"q": q, "src": q, "fn": fn, "r": list(r), "w": list(w), "b": list(b), "sig": False, "sem": None, "val": 0, "inc": 0,
+                    "k": "r", "t": tm, "lat": 0, "visit": now[0],
+                    "tag": now[1] or (w[0].rstrip("0123456789") if w else "%s%d" % (r[0].rstrip("0123456789"), b[0] if b else 0))})
+
+    def note(**kw):
+        ops[-1].update(kw)
+
+    def dma(q, out, in_, r=(), w=()):
+        s = "d%d" % nd[0]
+        nd[0] += 1
+        op(q, lambda e: e.dma_start(out, in_), r, w)
+        lat[0] += ops[-1]["t"]
+        note(src=s, sem=s, val=16, inc=16, t=50, lat=2000 + lat[0], line="dma" + q)
+
+    def ts(out, in0, s1, op0, s2=None, op1=None, r=(), w=(), b=()):
+        if op1 is None:
+            op("v", lambda e: e.tensor_scalar(out, in0, s1, None, op0), r, w, b)
+        else:
+            op("v", lambda e: e.tensor_scalar(out, in0, s1, s2, op0, op1), r, w, b)
+
+    def tt(out, in0, in1, o, r=(), w=(), b=()):
+        op("v", lambda e: e.tensor_tensor(out, in0, in1, o), r, w, b)
+
+    def cp(out, in_, r=(), w=(), b=()):
+        op("v", lambda e: e.tensor_copy(out, in_), r, w, b)
+
+    def fill(out, c, w=(), b=()):
+        op("v", lambda e: e.memset(out, c), (), w, b)
+
+    def act(out, in_, f, bias=0.0, scale=1.0, acc=None, r=(), w=(), b=()):
+        op("a", lambda e: e.activation(out, in_, f, bias=bias, scale=scale, accum_out=acc), r, w, b)
+
+    def mm(bk, out, lhsT, rhs, start, stop, r=()):
+        op("p", lambda e: e.matmul(out, lhsT, rhs, start, stop), r, (), [bk])
+        note(k="w" if start or stop else "add", t=max(TMM.get(x, 34) for x in r), lat=60)
+
+    def scan(out, d0, d1, init, o0, o1, r=(), w=(), b=()):
+        op("v", lambda e: e.tensor_tensor_scan(out, d0, d1, init, o0, o1), r, w, b)
+
+    def iota(out, pat, base, mult, w, flag=True):
+        if flag:
+            op("g", lambda e: e.iota(out, pat, base, mult, allow_small_or_imprecise_dtypes=True), ["pool"], w + ["pool"])
+        else:
+            op("g", lambda e: e.iota(out, pat, base, mult), ["pool"], w + ["pool"])
+
+    lw = H // LCH
+    for c in range(LCH):
+        dma("s", T.PK[:, c * lw:(c + 1) * lw], T.fld[:, c * lw:(c + 1) * lw], w=["PK%d" % c])
+        if c == 0:
+            dma("a", T.WI[:], T.wnd[:], w=["WI"])
+    dma("s", T.REC[:, 0:V], T.rec[:], w=["REC"])
+    dma("s", T.REC[:, V:2 * V], T.rec[:], w=["REC2"])
+
+    lat[0] = 0
+
+    iota(T.CP[:, 0:1], [[1, 1]], 0, 1, ["CP"], False)
+    iota(T.RM[:], [[1, 240]], 0, 0, ["RM"])
+    iota(T.RK[:], [[0, 24], [1, 16]], 0, 0, ["RK"])
+    iota(T.RG[:], [[1, 8], [0, 16]], 0, 0, ["RG"])
+    iota(T.FW[:, V:V + 32], [[0, 32]], 0, 0, ["FWd"])
+    iota(T.SKF[:], [[0, 2048]], 1, 0, ["SKF"])
+    note(t=4300)
+    op("g", lambda e: e.affine_select(T.SKF[:], T.SKF[:], [[-256, 16], [-16, 8], [255, 16]], A.is_equal, 0.0, 0, 1),
+       ["SKF", "pool"], ["SKF", "pool"])
+    note(t=4300)
+    iota(T.KC[32:64, :], [[0, 24], [8192, 16]], 0, 0, ["KCb"])
+    iota(T.KC[64:96, 256:384], [[0, 64], [2048, 2]], -2048, 0, ["KCc"])
+    iota(T.KC[0:32, 0:128], [[0, 128]], -120 * 131072, 0, ["KCa0"])
+    iota(T.KC[0:32, 128:384], [[0, 256]], 120 * 131072, 0, ["KCa1"])
+    iota(T.KC[64:96, 0:256], [[0, 256]], 0, 0, ["KCd"])
+    iota(T.ZL[:], [[0, 128]], 0, 0, ["ZL"])
+    iota(T.PY[:, 64:72], [[0, 8]], 0, 0, ["PY0"])
+    p = T.CP[:, 0:1]
+    fill(T.O32[:], 1.0 / 32, ["O32"])
+    bits = [(0, 127), (0, 15), (4, 7), (0, 7), (3, 3), (0, 1), (3, 1), (5, 3)]
+    for j, (sh, m) in enumerate(bits):
+        ts(T.CI[:, j:j + 1], p, sh, A.logical_shift_right, m, A.bitwise_and, r=["CP"], w=["CI%d" % j])
+    cp(T.CF[:], T.CI[:], r=["CI%d" % j for j in range(8)], w=["CF"])
+    cP, c16, cG, c8, cQ, cO, cH, cB = [T.CF[:, j:j + 1] for j in range(8)]
+    ident = T.ISH[:, 0:128]
+    ts(ident, T.RM[:, 0:128], cP, A.is_equal, r=["RM", "CF"], w=["I"])
+    ts(T.MK[:], T.RM[:, 0:16], c16, A.is_equal, r=["RM", "CF"], w=["MK"])
+    ts(T.QM[:], T.RM[:, 0:4], cQ, A.is_equal, r=["RM", "CF"], w=["QM"])
+    nc = [0]
+
+    def col(in0, s1, s2, r=("CF",)):
+        j = nc[0]
+        nc[0] += 1
+        act(T.CC[:, j:j + 1], in0, F.Identity, scale=s1, bias=s2, r=r, w=["CC%d" % j])
+        return T.CC[:, j:j + 1], "CC%d" % j
+
+    def col2(a, b_, o, r):
+        j = nc[0]
+        nc[0] += 1
+        tt(T.CC[:, j:j + 1], a, b_, o, r=r, w=["CC%d" % j])
+        return T.CC[:, j:j + 1], "CC%d" % j
+
+    def eqm(name, out, row, rrow, c, wt):
+        ts(out, row, c[0], A.is_equal, wt[0] if isinstance(wt, tuple) else wt, A.mult,
+           r=[rrow, c[1]] + ([wt[1]] if isinstance(wt, tuple) else []), w=[name])
+
+    p1 = col(cP, 1.0, 1.0)
+    even = col(cO, -1.0, 1.0)
+    odd16 = col(cO, 65536.0, 0.0)
+    not15 = col(T.MK[:, 15:16], -0.5, 0.5, r=["MK"])
+    eqm("SH", T.ISH[:, 128:256], T.RM[:, 0:128], "RM", p1, even)
+    eqm("DO", T.DO[:], T.RM[:, 0:128], "RM", (cP, "CF"), odd16)
+    for k in range(16):
+        act(T.SK[:, 128 * k:128 * k + 128], ident, F.Identity, scale=T.MK[:, k:k + 1], r=["I", "MK"], w=["SK%d" % k])
+    act(T.NSH[:], T.ISH[:, 128:256], F.Identity, scale=-1.0, r=["SH"], w=["NSH"])
+    act(T.I16[:], ident, F.Identity, scale=1.0 / 16, r=["I"], w=["I16"])
+    a15 = col(c16, -2.0, 15.0)
+    odd_w = col(c16, 2.0, 1.0)
+    c8x = col(c8, 16.0, 0.0)
+    c112 = col(c16, 1.0, 112.0)
+    dummy = [col(c16, 1.0, float(V)), col(c16, 1.0, float(V + 16))]
+    kbias = col(c16, -8192.0, 0.0)
+    ybase = col(cH, 32.0, -56.0)
+    q0n = col(T.QM[:, 0:1], -1.0, 0.0, r=["QM"])
+    q1s = col(T.QM[:, 1:2], 2.0 ** -14, 0.0, r=["QM"])
+    q0h = col(T.QM[:, 0:1], 0.5, 0.0, r=["QM"])
+    q3h = col(T.QM[:, 3:4], 0.5, 0.0, r=["QM"])
+    rev = col2(a15[0], cP, A.add, [a15[1], "CF"])
+    ymask = col2(c8, cG, A.is_equal, ["CF"])
+    q02 = col2(T.QM[:, 0:1], T.QM[:, 2:3], A.add, ["QM"])
+    qh = col2(q0h[0], q3h[0], A.subtract, [q0h[1], q3h[1]])
+    qa = col2(q0h[0], q3h[0], A.add, [q0h[1], q3h[1]])
+    ts(T.B8[:], T.RM[:, 0:8], cG, A.is_equal, r=["RM", "CF"], w=["B8"])
+    ts(T.WH0[:], T.WI[:], -2048.0, A.add, r=["WI"], w=["WH0"])
+    cp(T.WU[:], T.WI[:], r=["WI"], w=["WU"])
+    ts(T.HM[:], T.RK[:], 0.0, A.not_equal, r=["RK"], w=["HM"])
+    ts(T.MS0[:], T.RK[:, 0:256], c16, A.is_ge, 0.375, A.mult, r=["RK", "CF"], w=["MS0"])
+    eqm("MVH", T.MVH[:], T.RM[:, 0:128], "RM", p1, not15)
+    eqm("TBH", T.TBH[:], T.RM[:, 0:128], "RM", rev, not15)
+    eqm("BO", T.BO[:], T.RG[:], "RG", (cG, "CF"), 1.0 / 32)
+    eqm("XN", T.XN[:, 0:128], T.RG[:], "RG", (c8, "CF"), q0n)
+    eqm("XL", T.XL[:, 0:128], T.RG[:], "RG", (c8, "CF"), q02)
+    eqm("XC", T.XC[:, 0:128], T.RG[:], "RG", (c8, "CF"), q1s)
+    eqm("XH", T.XH[:, 0:128], T.RM[:, 0:128], "RM", c8x, qh)
+    eqm("XA", T.XA[:, 0:128], T.RM[:, 0:128], "RM", c8x, qa)
+    ts(T.BM[:], T.RM[:, 0:4], cB, A.is_equal, r=["RM", "CF"], w=["BM"])
+    for name in ("XN", "XH", "XA", "XC", "XL"):
+        for a in range(4):
+            act(T[name][:, 128 * a + 128:128 * a + 256], T[name][:, 0:128], F.Identity, scale=T.BM[:, a:a + 1], r=[name, "BM"], w=[name + str(a)])
+            note(t=170)
+    eqm("CW", T.CW[:], T.RM[:], "RM", c112, 2.0 ** -13)
+    ts(T.YF0[:], T.RM[:, 0:8], ybase[0], A.add, ymask[0], A.mult, r=["RM", ybase[1], ymask[1]], w=["YF0"])
+    tt(T.HDM[:], T.MVH[:], T.TBH[:], A.subtract, r=["MVH", "TBH"], w=["HDM"])
+    tt(T.AVM[:], T.MVH[:], T.TBH[:], A.add, r=["MVH", "TBH"], w=["AVM"])
+    ts(T.YOF[:], T.YF0[:], 64.0, A.add, r=["YF0"], w=["YOF"])
+    act(T.O32F[:], T.O32[:], F.Identity, r=["O32"], w=["O32F"])
+    fill(T.Q16[:, 64:192], 0.0, ["Q0"])
+    fill(T.THR[:], -4.5, ["THR"])
+    fill(B[0][:, 256:512], 0.0, ["Z0"], [0])
+    note(k="w")
+
+    for c in range(LCH):
+        sl = slice(c * lw, (c + 1) * lw)
+        if c in UNP:
+            ts(T.YO[:, sl], T.PK[:, sl], -2.0 ** 23, A.add, -2047.5, A.add, r=["PK%d" % c], w=["YO%d" % c])
+            act(T.YO[:, sl], T.YO[:, sl], F.Identity, bias=MAG / 2, r=["YO%d" % c], w=["YO%d" % c])
+            act(B[2 + c][:, 0:lw], T.YO[:, sl], F.Identity, bias=2.0 ** 23 - MAG / 2, r=["YO%d" % c], w=["HJ%d" % c], b=[2 + c])
+        else:
+            ts(T.HI[:, sl], T.PK[:, sl], 12, A.logical_shift_right, r=["PK%d" % c], w=["HI%d" % c])
+            ts(B[2 + c][:, 0:lw], T.HI[:, sl], float(V), A.mult, r=["HI%d" % c], w=["HJ%d" % c], b=[2 + c])
+        note(k="w")
+        tt(T.FW[:, sl], T.PK[:, sl], B[2 + c][:, 0:lw], A.subtract, r=["HJ%d" % c], w=["FW%d" % c], b=[2 + c])
+        note(t=570)
+        act(T.FW[:, H + c * lw:H + (c + 1) * lw], B[2 + c][:, 0:lw], F.Identity, scale=1.0 / V, r=["HJ%d" % c], w=["FW%d" % (LCH + c)], b=[2 + c])
+        note(t=570)
+
+    def late_constants():
+        act(T.NI[:], ident, F.Identity, scale=-1.0, r=["I"], w=["NI"])
+        act(T.NI2[:], ident, F.Identity, scale=-0.5, r=["I"], w=["NI2"])
+        act(T.WIM[:], ident, F.Identity, scale=-0.1875, r=["I"], w=["WIM"])
+        for name, wt in (("BP1", 131072.0), ("BP2", 262144.0), ("BN", -131072.0)):
+            for j in range(3):
+                act(T[name][:, 8 * j:8 * j + 8], T.B8[:], F.Identity, scale=(wt if j == 0 else -wt), r=["B8"], w=[name + str(j)])
+        act(T.WT8[:], T.B8[:], F.Identity, scale=odd_w[0], r=["B8", odd_w[1]], w=["WT8"])
+        act(T.SC[:], T.HM[:], F.Identity, scale=-1.0e8, bias=1.0e8, r=["HM"], w=["SC"])
+        act(T.PM[:, 0:256], T.HM[:, 0:256], F.Identity, scale=-2.0 ** 99, bias=2.0 ** 98, r=["HM"], w=["PM"])
+        act(T.PM[:, 256:512], T.HM[:, 0:256], F.Identity, scale=-2.0 ** 99, bias=2.0 ** 98, r=["HM"], w=["PN"])
+        act(T.MSK[:, 0:256], T.MS0[:], F.Identity, bias=0.1875, r=["MS0"], w=["MSK"])
+        act(T.MSK[:, 256:272], T.HM[:, 0:16], F.Identity, scale=0.0, bias=0.5625, r=["HM"], w=["MSL"])
+        act(T.MSK[:, 272:512], T.HM[:, 0:240], F.Identity, scale=0.0, bias=0.1875, r=["HM"], w=["MSM"])
+
+    late_constants()
+    FWR = ["FW%d" % c for c in range(2 * LCH)] + ["FWd"]
+    KCR = ["KCa0", "KCa1", "KCb", "KCc", "KCd", "O32"]
+
+    def expand(bk, out0, mat, name, src, sname, c0, start, stop):
+        for h in range(2):
+            for a in range(4):
+                o = out0 + 128 * h + 32 * a
+                m = min(32, 512 - o)
+                mm(bk, B[bk][:, o:o + m], mat[:, 128 * a + 128:128 * a + 256], src[:, c0 + 32 * h:c0 + 32 * h + m],
+                   start, stop and (start or (h == 1 and a == 3)), r=[name + str(a), sname])
+
+    def chunk_of(w):
+        return [c for c in range(len(PC)) if PC[c][0] <= w < PC[c][0] + PC[c][1]][0]
+
+    def arrive(t):
+        op("v", None, w=["WH%d" % t])
+        note(src="arr%d" % t, sem="arr%d" % t, val=n_in, t=0, line="ring")
+        ts(T.WU[:], T["WH%d" % t][:], 2048.0, A.add, r=["WH%d" % t], w=["WU"])
+
+    for t in range(NV):
+        last = t == NV - 1
+        WH, wh = T["WH%d" % t], "WH%d" % t
+
+        def gather_f(j):
+            ts(T.G1[:, 512 * j:512 * j + 512], T.FW[:, 0:V].indirect(T.WU[:, 32 * j:32 * j + 32]), -2048.0, A.add, r=FWR + ["WU"], w=["G%d" % j])
+
+        def gather_fa():
+            w0, m, _ = PC[AF]
+            act(T.GF[:, 0:16 * m], T.FW[:, 0:V].indirect(T.WU[:, w0:w0 + m]), F.Identity, bias=-2048.0, r=FWR + ["WU"], w=["GF"])
+
+        def before(c):
+            w0, m, bk = PC[c]
+            mm(bk, B[bk][:, w0:w0 + m], T.NSH[:], WH[:, w0:w0 + m], True, False, r=["NSH", wh])
+            mm(bk, B[bk][:, w0:w0 + m], T.DO[:], T.O32[:, 0:m], False, False, r=["DO", "O32"])
+
+        def pick(c):
+            w0, m, bk = PC[c]
+            before(c)
+            for k in range(16):
+                mm(bk, B[bk][:, w0:w0 + m], T.SK[:, 128 * k:128 * k + 128], T.G1[:, 16 * w0 + k:16 * (w0 + m):16], False, k == 15,
+                   r=["SK%d" % k] + ["G%d" % j for j in range(w0 // 32, (w0 + m) // 32)])
+
+        def pick_a(part):
+            w0, m, bk = PC[AF]
+            if part == 0:
+                before(AF)
+            for k in range(4 * part, 4 * part + 4):
+                mm(bk, B[bk][:, w0:w0 + m], T.SKF[:, 128 * k:128 * k + 128], T.GF[:, k:16 * m:16], False, k == 15, r=["SKF", "GF"])
+
+        def names(c):
+            w0, m, bk = PC[c]
+            sl = slice(w0, w0 + m)
+            if t:
+                ts(T.EU[:, sl], B[bk][:, sl], 2048.0, A.add, w=["EU%d" % c], b=[bk])
+                return
+            ts(T.ET[:, sl], B[bk][:, sl], 2048.0, A.is_ge, -4096.0, A.mult, w=["ET%d" % c], b=[bk])
+            tt(T.EH[:, sl], T.ET[:, sl], B[bk][:, sl], A.add, r=["ET%d" % c], w=["EH%d" % c], b=[bk])
+            ts(T.EU[:, sl], T.EH[:, sl], 2048.0, A.add, r=["EH%d" % c], w=["EU%d" % c])
+
+        def wrap(cs):
+            if t:
+                bk, sl = PC[cs[0]][2], slice(PC[cs[0]][0], PC[cs[-1]][0] + PC[cs[-1]][1])
+                m = sl.stop - sl.start
+                ts(T.ET[:, sl], T.EU[:, sl], float(V), A.is_ge, -4096.0, A.mult, r=["EU%d" % c for c in cs], w=["ET%d" % c for c in cs])
+                note(t=50 + m // 2)
+                tt(T.EH[:, sl], T.ET[:, sl], B[bk][:, sl], A.add, r=["ET%d" % c for c in cs], w=["EH%d" % c for c in cs], b=[bk])
+                note(t=50 + m)
+
+        def gather_x(q, js):
+            w0, w1 = 32 * js[0], 32 * js[-1] + 32
+            win = T.REC[:] if t else T.REC[:, 0:V]
+            src, w = win.indirect(T.EU[:, w0:w1]), ["X%d" % j for j in js]
+            r = ["REC"] + (["REC2"] if t else []) + ["EU%d" % chunk_of(32 * j) for j in js]
+            if q == "a":
+                act(T.X[:, 16 * w0:16 * w1], src, F.Identity, bias=192.0, r=r, w=w)
+            else:
+                ts(T.X[:, 16 * w0:16 * w1], src, 192.0, A.add, r=r, w=w)
+            note(t=60 + 830 * len(js))
+
+        def sums(s):
+            bk, o = 2 + s // 2, 64 * (s % 2)
+            for k in range(16):
+                mm(bk, B[bk][:, o:o + 64], T.I16[:], T.X[:, 1024 * s + k:1024 * (s + 1):16], k == 0, k == 15, r=["I16", "X%d" % (2 * s), "X%d" % (2 * s + 1)])
+
+        def xs(h):
+            return ["X%d" % j for j in range(4 * h, 4 * h + 4)]
+
+        def xk(h, k):
+            return T.X[:, H * h + k:H * (h + 1):16]
+
+        def mb(h):
+            return T.MB[:, 128 * h:128 * h + 128]
+
+        def key_start(h):
+            mm(4 + h, B[4 + h][:, 0:384], T.O32[0:96, :], T.KC[0:96, :], True, False, r=KCR)
+            for k in KD[h]:
+                mm(4 + h, B[4 + h][:, k:384:16], xk(h, k), T.BN[:], False, False, r=xs(h) + ["BN0", "BN1", "BN2"])
+
+        def mean(h):
+            if MV[h]:
+                ts(mb(h), B[2 + h][:, 0:128], -0.46875, A.add, w=["MB%d" % h], b=[2 + h])
+            else:
+                act(mb(h), B[2 + h][:, 0:128], F.Identity, bias=-0.46875, w=["MB%d" % h], b=[2 + h])
+            mm(2 + h, B[2 + h][:, 128:256], ident, mb(h), True, True, r=["I", "MB%d" % h])
+
+        def ad(h, k):
+            return T.AD[:, H * h + 128 * k:H * h + 128 * k + 128]
+
+        def dist_v(h, part):
+            m = len(KD[h]) // 2
+            for k in (KD[h][m:] if part else KD[h][:m]):
+                tt(ad(h, k), xk(h, k), B[2 + h][:, 128:256], A.max, r=xs(h), w=["AD%d_%d" % (h, k)], b=[2 + h])
+
+        def group(h, i):
+            ka = [k for k in range(16) if k not in KD[h]]
+            return ka[4 * i:4 * i + 4]
+
+        def key_v(h):
+            for k in KD[h]:
+                mm(4 + h, B[4 + h][:, k:384:16], mb(h), T.BN[:], False, False, r=["MB%d" % h, "BN0", "BN1", "BN2"])
+            for k in KD[h]:
+                mm(4 + h, B[4 + h][:, k:384:16], ad(h, k), T.BP2[:], False, False, r=["AD%d_%d" % (h, k), "BP20", "BP21", "BP22"])
+
+        def key_a(h):
+            for k in range(16):
+                if k not in KD[h]:
+                    mm(4 + h, B[4 + h][:, k:384:16], ad(h, k), T.BP1[:], False, False, r=["AD%d_%d" % (h, k), "BP10", "BP11", "BP12"])
+
+        def diff(h, i):
+            bk, ks = 7 - (i & 1), group(h, i)
+            for j, k in enumerate(ks):
+                mm(bk, B[bk][:, 128 * j:128 * j + 128], ident, xk(h, k), j == 0, False, r=xs(h) + ["I"])
+                note(k="w" if j == 0 else "new")
+            for j, k in enumerate(ks):
+                mm(bk, B[bk][:, 128 * j:128 * j + 128], T.NI[:], mb(h), False, j == len(ks) - 1, r=["NI", "MB%d" % h])
+
+        def dist_a(h, i):
+            ks, bk = group(h, i), 7 - (i & 1)
+            if ks:
+                c0 = H * h + 128 * ks[0]
+                act(T.AD[:, c0:c0 + 128 * len(ks)], B[bk][:, 0:128 * len(ks)], F.Abs, w=["AD%d_%d" % (h, k) for k in ks], b=[bk])
+                note(t=60 + 133 * len(ks))
+
+        def key_end(h):
+            eh = ["EH%d" % c for c in range(len(PC)) if PC[c][0] // 128 == h]
+            mm(4 + h, B[4 + h][:, 0:128], T.EH[:, 128 * h:128 * h + 128], ident, False, False, r=eh + ["I"])
+            note(k="w")
+            mm(4 + h, B[4 + h][:, 128:384], WH[:, 128 * h:128 * h + 128], T.ISH[:], False, True, r=[wh, "I", "SH"])
+            scan(T.KF[:, 512 * h:512 * h + 384], T.SC[:], B[4 + h][:, 0:384], 0.0, A.add, A.min, r=["SC"], w=["KF%d" % h], b=[4 + h])
+
+        def jump(step):
+            if step == 0:
+                for h in range(2):
+                    mm(1, B[1][:, 288 + 8 * h:296 + 8 * h], mb(h), T.WT8[:], True, True, r=["WT8", "MB%d" % h])
+                act(T.SQ[:], B[1][:, 288:304], F.Square, bias=-48560.0, w=["SQ"], b=[1])
+            elif step == 1:
+                ts(T.ZI[:], T.SQ[:], 1.0 / 32, A.mult, -10952.375, A.add, r=["SQ"], w=["ZI"])
+            elif step == 2:
+                ts(T.ZA[:], T.ZI[:], V - 1, A.bitwise_and, r=["ZI"], w=["ZA"])
+            else:
+                for h in range(2):
+                    ts(T.KF[:, 512 * h + 399:512 * h + 512:16], T.ZA[:, 8 * h:8 * h + 8], -2048.0, A.add, r=["ZA"], w=["KZ%d" % h])
+
+        def threshold(step):
+            if t == 0:
+                return
+            if step == 0:
+                mm(3, B[3][:, 280:281], T.O32F[:], T.ACC[:, 0:1], True, True, r=["O32F", "ACC"])
+                cp(T.PI[:, 0:1], B[3][:, 280:281], w=["PI"], b=[3])
+            elif step == 1:
+                ts(T.PJ[:, 0:1], T.PI[:, 0:1], 1, A.bitwise_and, r=["PI"], w=["PJ"])
+            else:
+                ts(T.THR[:, 0:1], T.PJ[:, 0:1], -1.0, A.mult, -4.5, A.add, r=["PJ"], w=["THR"])
+
+        for s in ORDER.split():
+            c, a = s[0], s[1:]
+            now[0], now[1] = t, s
+            if c == "A":
+                gather_fa()
+            elif c == "G":
+                gather_f(int(a))
+            elif c == "P":
+                pick(int(a))
+            elif c == "F":
+                pick_a(int(a))
+            elif c == "N":
+                names(int(a))
+            elif c == "W":
+                wrap([int(j) for j in a])
+            elif c == "X":
+                gather_x(a[0], [int(j) for j in a[1:]])
+            elif c == "S":
+                sums(int(a))
+            elif c == "K":
+                key_start(int(a))
+            elif c == "M":
+                mean(int(a))
+            elif c == "D":
+                diff(int(a[0]), "abcd".index(a[1]))
+            elif c == "B":
+                dist_a(int(a[0]), "abcd".index(a[1]))
+            elif c == "V":
+                dist_v(int(a[0]), "ab".index(a[1]))
+            elif c == "E":
+                (key_v if a[1] == "v" else key_a)(int(a[0]))
+            elif c == "R":
+                key_end(int(a))
+            elif c == "Z":
+                jump(int(a))
+            elif c == "T":
+                threshold(int(a))
+            elif c == "H":
+                mm(2, B[2][:, 0:256], T.HDM[:], WH[:], True, False, r=["HDM", wh])
+                mm(0, B[0][:, 0:256], ident, T.EH[:], True, False, r=["I"] + ["EH%d" % q for q in range(len(PC))])
+        now[1] = None
+        mm(3, B[3][:, 0:256], T.AVM[:], WH[:], True, False, r=["AVM", wh])
+        mm(7, B[7][:], ident, T.MSK[:], True, False, r=["I", "MSK", "MSL", "MSM"])
+        mm(6, B[6][:, 0:256], T.ZL[:], WH[:], True, False, r=["ZL", wh])
+        keys, kr = T.KF[:, 15:1024:16], ["KF0", "KF1", "KZ0", "KZ1"]
+        ts(T.RQ[:], keys, MAG, A.add, -MAG, A.add, r=kr, w=["RQ"])
+        ts(T.RI[:], keys, 4096.0, A.add, r=kr, w=["RI"])
+        tt(T.P16[:], keys, T.RQ[:], A.subtract, r=kr + ["RQ"], w=["P16"])
+        ts(T.KK[:], T.RI[:], 13, A.arith_shift_right, 15, A.bitwise_and, r=["RI"], w=["KK"])
+        op("v", lambda e: e.transpose(T.PT[:], T.P16[:]), ["P16"], ["PT"])
+        expand(0, 0, T.XN, "XN", T.PT, "PT", 0, False, True)
+        expand(2, 0, T.XH, "XH", T.PT, "PT", 0, False, True)
+        cp(T.Q16[:, 0:64], T.KK[:], r=["KK"], w=["QK"])
+        cp(T.PY[:, 0:64], T.P16[:], r=["P16"], w=["PY"])
+        tt(T.VS[:], T.P16[:, 0:48], T.P16[:, 16:64], A.add, r=["P16"], w=["VS"])
+        ts(T.EQ[:], B[0][:, 0:256], 0.0, A.is_equal, w=["EQ"], b=[0])
+        mm(1, B[1][:, 0:256], T.BO[:], T.EQ[:], True, True, r=["BO", "EQ"])
+        act(T.GO[:], B[1][:, 0:256], F.Sign, bias=T.THR[:, 0:1], scale=32.0, acc=(None if last else T.ACC[:, 0:1]),
+            r=["THR"], w=["GO", "ACC"], b=[1])
+        cp(T.Y2[:], T.PY[:].indirect(T.YOF[:]), r=["PY", "PY0", "YOF"], w=["Y2"])
+        tt(T.Q16[:, 128:168], T.Q16[:, 0:40], T.Q16[:, 8:48], A.is_equal, r=["QK", "Q0"], w=["QF"])
+        ts(T.Q16[:, 64:112], T.VS[:], 0.0, A.is_lt, -4096.0, A.mult, r=["VS", "Q0"], w=["QC"])
+        for gg in range(8):
+            mm(0, B[0][:, 256:512:16], T.CW[:, 112 - 16 * gg:240 - 16 * gg], T.Y2[:, 16 * gg:16 * gg + 16], gg == 0, gg == 7, r=["CW", "Y2", "Z0"])
+        expand(3, 0, T.XA, "XA", T.PT, "PT", 0, False, True)
+        op("v", lambda e: e.transpose(T.QT[:], T.Q16[:]), ["QK", "QF", "QC"], ["QT"])
+        mm(4, B[4][:, 0:256], T.BO[:], T.EQ[:], True, False, r=["BO", "EQ"])
+        expand(4, 0, T.XN, "XN", T.QT, "QT", 128, False, True)
+        expand(5, 0, T.XC, "XC", T.QT, "QT", 0, True, True)
+        expand(7, 0, T.XC, "XC", T.PT, "PT", 0, False, False)
+        expand(7, 272, T.XC, "XC", T.PT, "PT", 0, False, False)
+        scan(T.RR[:], T.HM[:, 0:256], B[0][:, 256:512], 0.0, A.mult, A.add, r=["HM"], w=["RR"], b=[0])
+        tt(T.PRD[:], T.GO[:], B[2][:, 0:256], A.mult, r=["GO"], w=["PRD"], b=[2])
+        ts(T.OC[:], B[0][:, 256:512:16], 8192.0, A.mult, 2048.0, A.add, w=["OC"], b=[0])
+        if last:
+            tt(T.WF[:], T.PRD[:], B[3][:, 0:256], A.add, r=["PRD"], w=["WF"], b=[3])
+        else:
+            WO, nx = T["WO%d" % t], T["WH%d" % (t + 1)]
+            tt(WO[:], T.PRD[:], B[3][:, 0:256], A.add, r=["PRD"], w=["WO%d" % t], b=[3])
+            op("g", lambda e, WO=WO, nx=nx, t=t: e.remote_dma(nx[:], WO[:], T.sem["arr%d" % (t + 1)], T.sem.sent, pid, rid, mask_out), ["WO%d" % t])
+            note(line="ring")
+        act(T.WA[:], B[4][:, 0:256], F.Sign, bias=T.THR[:, 0:1], scale=32.0, r=["THR"], w=["WA"], b=[4])
+        act(T.U[:], B[5][:, 0:256], F.Abs, bias=kbias[0], scale=2.0 ** 27, r=[kbias[1]], w=["U"], b=[5])
+        mm(7, B[7][:, 0:256], T.NI2[:], T.RR[:], False, False, r=["NI2", "RR"])
+        mm(7, B[7][:, 256:512], T.NI2[:], T.RR[:], False, False, r=["NI2", "RR"])
+        expand(6, 0, T.XL, "XL", T.PT, "PT", 0, False, False)
+        mm(7, B[7][:, 272:512], T.WIM[:], T.WA[:, 0:240], False, False, r=["WIM", "WA"])
+        mm(7, B[7][:, 0:256], T.WIM[:], T.WA[:], False, True, r=["WIM", "WA"])
+        expand(6, 0, T.XN, "XN", T.QT, "QT", 64, False, False)
+        for a in range(16):
+            mm(1, B[1][:, 256:272], T.SK[:, 128 * a:128 * a + 128], T.WA[:, a:256:16], a == 0, a == 15, r=["SK%d" % a, "WA"])
+        mm(6, B[6][:, 0:256], T.NI[:], T.U[:], False, True, r=["NI", "U"])
+        act(T.LS[:], B[6][:, 0:256], F.Identity, w=["LS"], b=[6])
+        if last:
+            act(T.WG[:], T.WF[:], F.Identity, bias=2048.0, r=["WF"], w=["WG"])
+            dma("a", T.yw[:], T.WG[:], r=["WG"], w=["yw"])
+        scan(T.PS[:], T.PM[:], B[7][:], 1.0, A.max, A.mult, r=["PM", "PN"], w=["PS"], b=[7])
+        tt(T.OM[:], T.FW[:, 0:V].indirect(T.OC[:]), T.U[:], A.min, r=FWR + ["OC", "U"], w=["OM"])
+        ts(T.LO[:], T.PS[:, 15:512:16], 0.0, A.is_equal, 0.625, A.add, r=["PS"], w=["LO"])
+        tt(T.K2[:], T.RR[:, 0:256:16], B[1][:, 256:272], A.subtract, r=["RR"], w=["K2"], b=[1])
+        tt(T.K3[:], T.LO[:, 0:16], T.LO[:, 16:32], A.add, r=["LO"], w=["KA"])
+        tt(T.K4[:], T.K3[:], T.K2[:], A.add, r=["KA", "K2"], w=["KB"])
+        for j in range(2):
+            ts(T.OFF[:, j:16:2], T.K4[:, j:16:2], 8192.0, A.mult, dummy[j][0], A.min, r=["KB", dummy[j][1]], w=["OFF%d" % j])
+        for b in range(7, -1, -1):
+            if b == 3 and not last:
+                arrive(t + 1)
+            tt(T.FW[:].indirect(T.OFF[:, 2 * b:2 * b + 2]), T.OM[:, 32 * b:32 * b + 32], T.LS[:, 32 * b:32 * b + 32], A.max,
+               r=["OFF0", "OFF1", "OM", "LS"], w=FWR)
+            note(t=180)
+
+    now[0], now[1] = NV, "end"
+    for c in range(LCH):
+        act(B[2 + c][:, 0:lw], T.FW[:, H + c * lw:H + (c + 1) * lw], F.Identity, scale=float(V), r=FWR, b=[2 + c])
+        note(k="w", t=570)
+        tt(T.YO[:, c * lw:(c + 1) * lw], T.FW[:, c * lw:(c + 1) * lw], B[2 + c][:, 0:lw], A.add, r=FWR, w=["YO%d" % c], b=[2 + c])
+        dma("s", T.yf[:, c * lw:(c + 1) * lw], T.YO[:, c * lw:(c + 1) * lw], r=["YO%d" % c], w=["yf%d" % c])
+    op("s", None, r=["yw"] + ["yf%d" % c for c in range(LCH)])
+    note(src="end")
+    emit(g, T, arrange(ops))
+    g.wait_ge(T.sem.sent, n_out * (NV - 1))

@@ -2,19 +2,21 @@ from concourse.mybir import AluOpType as A, ActivationFunctionType as F
 
 V, H, K, NV = 4096, 2048, 256, 5
 MAG = 1.5 * 2.0 ** 36
-LCH = 4
+IN = [0, 512, 1024, 1536, 1792, 2048]
+OUT = [0, 256, 768, 1280, 1792, 2048]
 PC = [(0, 32, 0), (32, 32, 0), (64, 64, 0), (128, 64, 0), (192, 64, 6)]
 AF = 4
 MV = [1, 1]
-UNP = ()
-EARLY = 200
+UNP = (1, 2, 4)
+EARLY = 0
+XACT = 4
 KD = [list(range(0, 8)), list(range(0, 8))]
-ORDER = ("A G0 T0 P0 G1 T1 N0 P1 Xa0 F0 G2 T2 N1 Xa1 F1 G3 F2 P2 F3 G4 N2 N4 Xa2 Xa3 G5 P3 S0 Xa6 S1 Xv7 N3 Xa4 Xv5 W4 W0123 K0 M0 S3 S2 "
+ORDER = ("A G0 T0 P0 G1 N0 P1 Xa0 F0 G2 N1 Xa1 F1 G3 F2 P2 F3 G4 N2 N4 Xa2 Xa3 G5 P3 S0 Xa6 S1 Xv7 N3 Xa4 Xv5 W4 W0123 K0 M0 S3 S2 "
          "M1 K1 Z0 Z1 Z2 Z3 V0a V0b D0a B0a D0b B0b E0v E0a R0 V1a V1b D1a B1a D1b B1b H E1v E1a R1")
-FIRST = ("B1b N2 N1 N4 A P1 G0 T2 N0 G1 F2 P2 G3 Xa1 Xa3 T1 M0 D0b M1 K0 Z0 G2 G5 S1 Xa4 T0 F3 Z1 Xa2 V0b V1b Z2 V0a W0123 Xa0 W4 F1 S2 "
-         "P0 Z3 Xv5 B1a D0a V1a G4 Xv7 R1 S3 K1 D1b EQ P3 N3 D1a S0 B0a GO R0 Xa6 F0 E0a E0v E1v E1a B0b WA P H PT RR PY RQ BO1 Y CW0 "
-         "QF VS KK BO4 WIM7 QC XN4 QK XN0 XC7 OM PS QT WO WO0 SK1 XH2 NI7 OC yw PRD XA3 XC5 NI6 RI AVM3 LS WU KB XN6 OFF K KA LO I7 "
-         "ZL6 XL6 WG WH U FW WF end")
+FIRST = ("F2 QT V1b W4 W0123 N3 A V0a Xa4 P1 F3 P2 Xa2 G0 B0a EQ S1 Xa3 N1 Z0 M0 G3 M1 B1b N0 P3 G1 Xa1 N2 V1a G2 G4 K0 Xv5 G5 R1 D0a RQ "
+         "S3 S2 D0b F1 F0 D1a E0v Z3 RR Z1 D1b QF P0 WO XN4 R0 N4 E0a Xv7 S0 E1v KK yw B0b LO E1a SG PT P WO0 XN0 WF T0 RI PY OC CW0 Z2 "
+         "XC5 V0b Xa0 KB WA K1 end QK XH2 K AVM3 BO1 NI6 DC6 XA3 I6 BO4 PRD Y LS WU WIM7 XL5 WG B1a GO U NI7 XC7 KA H FW OFF PS I7 SK1 "
+         "OM XL6 Xa6 WH")
 
 
 def _sb(n, d):
@@ -26,18 +28,18 @@ SCRATCH = {
     "WI": _sb(K, "int32"), "WU": _sb(K, "uint16"), "EU": _sb(K, "uint16"), "EH": _sb(K, "float16"), "ET": _sb(K, "bfloat16"),
     "G1": _sb(V, "float16"), "GF": _sb(1024, "float32"), "X": _sb(V, "bfloat16"), "AD": _sb(V, "bfloat16"), "MB": _sb(K, "bfloat16"),
     "KF": _sb(1024, "float32"), "RQ": _sb(64, "float32"), "P16": _sb(64, "float16"), "PT": _sb(64, "float16"),
-    "PY": _sb(72, "float32"), "VS": _sb(48, "float32"), "RI": _sb(64, "int32"), "KK": _sb(64, "int32"),
-    "Q16": _sb(192, "float16"), "QT": _sb(192, "float16"), "SQ": _sb(16, "float32"), "ZI": _sb(16, "int32"), "ZA": _sb(16, "int32"),
-    "EQ": _sb(K, "bfloat16"), "GO": _sb(K, "bfloat16"), "WA": _sb(K, "bfloat16"), "PRD": _sb(K, "float32"),
-    "ACC": _sb(4, "float32"), "PI": _sb(4, "int32"), "PJ": _sb(4, "int32"), "THR": _sb(4, "float32"),
+    "PY": _sb(72, "float32"), "RI": _sb(64, "int32"), "KK": _sb(64, "int32"),
+    "Q16": _sb(128, "float16"), "QT": _sb(128, "float16"), "SQ": _sb(16, "float32"), "ZI": _sb(16, "int32"), "ZA": _sb(16, "int32"),
+    "EQ": _sb(K, "bfloat16"), "GO": _sb(K, "bfloat16"), "WA": _sb(K, "bfloat16"), "PRD": _sb(K, "float32"), "SG": _sb(K, "bfloat16"),
+    "ACC": _sb(4, "float32"), "TA": _sb(4, "float32"), "THR": _sb(4, "float32"),
     "Y2": _sb(128, "float16"), "RR": _sb(K, "float16"), "OC": _sb(16, "uint16"), "U": _sb(K, "bfloat16"),
     "OM": _sb(K, "float32"), "LS": _sb(K, "float32"), "PS": _sb(2 * K, "float32"), "LO": _sb(32, "float32"), "K2": _sb(16, "float32"),
     "K3": _sb(16, "float32"), "K4": _sb(16, "float32"), "OFF": _sb(16, "uint16"), "WF": _sb(K, "float32"), "WG": _sb(K, "float32"),
-    "RM": _sb(240, "float32"), "RG": _sb(128, "float32"), "RK": _sb(384, "float32"), "CP": _sb(4, "int32"), "CI": _sb(8, "int32"),
-    "CF": _sb(8, "float32"), "CC": _sb(32, "float32"), "MK": _sb(16, "float32"), "QM": _sb(4, "float32"),
-    "ISH": _sb(256, "bfloat16"), "NSH": _sb(128, "bfloat16"), "I16": _sb(128, "bfloat16"), "NI": _sb(128, "bfloat16"),
+    "RM": _sb(240, "bfloat16"), "RD": _sb(128, "bfloat16"), "RG": _sb(128, "bfloat16"), "RK": _sb(384, "bfloat16"), "CP": _sb(4, "int32"),
+    "CI": _sb(8, "int32"), "CF": _sb(8, "float32"), "CC": _sb(32, "float32"), "MK": _sb(16, "float32"), "QM": _sb(4, "float32"),
+    "ISH": _sb(256, "bfloat16"), "NSH": _sb(128, "bfloat16"), "I16": _sb(128, "bfloat16"), "NI": _sb(128, "bfloat16"), "I2K": _sb(128, "bfloat16"),
     "NI2": _sb(128, "bfloat16"), "WIM": _sb(128, "bfloat16"), "DO": _sb(128, "bfloat16"), "SK": _sb(2048, "bfloat16"), "SKF": _sb(2048, "float32"),
-    "ZL": _sb(128, "bfloat16"), "O32": _sb(128, "bfloat16"), "O32F": _sb(128, "float32"), "MVH": _sb(128, "bfloat16"), "TBH": _sb(128, "bfloat16"),
+    "DC": _sb(256, "bfloat16"), "O32": _sb(128, "bfloat16"), "O32F": _sb(128, "float32"), "MVH": _sb(128, "bfloat16"), "TBH": _sb(128, "bfloat16"),
     "HDM": _sb(128, "bfloat16"), "AVM": _sb(128, "bfloat16"), "BO": _sb(128, "bfloat16"), "B8": _sb(8, "float32"),
     "BP1": _sb(24, "bfloat16"), "BP2": _sb(24, "bfloat16"), "BN": _sb(24, "bfloat16"), "WT8": _sb(8, "bfloat16"),
     "XN": _sb(640, "bfloat16"), "XL": _sb(640, "bfloat16"), "XC": _sb(640, "bfloat16"), "XH": _sb(640, "bfloat16"), "XA": _sb(640, "bfloat16"),
@@ -55,12 +57,14 @@ SEMAPHORES = ["sv", "sa", "sp", "sg", "sent"] + ["arr%d" % _t for _t in range(1,
 
 
 TIME = {"G": 880, "GF": 1720, "X": 880, "AD": 170, "KF": 440, "EQ": 300, "GO": 300, "WA": 300, "U": 300, "LS": 300, "PRD": 300, "WO": 300,
-        "WF": 300, "WG": 300, "RR": 300, "PS": 570, "PN": 300, "MSM": 300, "OM": 460, "Y": 250, "MB": 170, "WU": 170, "QT": 140, "RQ": 100, "RI": 100, "P": 160,
-        "VS": 130, "QF": 110, "FW": 120, "HI": 570, "HJ": 570, "YO": 570, "SKF": 1100, "SK": 170, "HM": 400, "MS": 300, "SC": 440, "PM": 300,
-        "MSK": 300, "CW": 280, "HDM": 300, "AVM": 300, "WH": 300, "Z": 200, "PK": 1300, "REC": 5200, "WI": 600}
-TMM = {"SKF": 133, "KCa0": 200, "HDM": 133, "AVM": 133, "ZL": 133, "BO": 133, "NI2": 133, "WIM": 133, "O32F": 133, "I": 67, "NI": 67,
-       "MSK": 266, "SH": 133, "U": 133}
+        "WF": 300, "WG": 300, "RR": 300, "PS": 570, "PN": 300, "MSM": 300, "OM": 460, "Y": 250, "MB": 170, "WU": 170, "QT": 120, "RQ": 100,
+        "RI": 100, "P": 160, "SG": 300, "QF": 110, "HI": 570, "HJ": 570, "YO": 570, "SK": 170, "HM": 250, "MS": 190, "SC": 440, "PM": 300,
+        "MSK": 300, "CW": 180, "HDM": 300, "AVM": 300, "WH": 300, "Z": 200, "PK": 500, "REC": 5200, "WI": 600, "RM": 630, "RD": 400,
+        "RG": 460, "RK": 990, "DC": 720, "KCb": 990, "KCc": 460, "KCa": 600, "KCd": 720, "FWd": 260, "PY": 130, "CP": 190}
+TMM = {"SKF": 133, "KCa0": 200, "HDM": 133, "AVM": 133, "DC": 133, "BO": 133, "NI2": 133, "WIM": 133, "O32F": 133, "I": 67, "NI": 67,
+       "MSK": 266, "SH": 133, "U": 133, "SG": 133}
 HOP, SAME, LINK, SLACK = 110, 60, 2600, 60
+TURNS = [200, 120, 60, 60, 30, 30]
 
 
 def arrange(ops):
@@ -103,49 +107,61 @@ def arrange(ops):
             return LINK if ops[i]["fn"] is None else 0
         if ops[j]["src"] != ops[i]["src"]:
             return HOP + ops[j]["lat"]
-        return SAME if ops[i]["q"] != "p" and (ops[j]["k"] != "r" or ops[i]["k"] != "r" or not ops[j]["b"] or set(ops[j]["w"]) & set(ops[i]["r"])) else 0
+        return SAME if ops[i]["q"] != "p" else 0
 
     rank = {s: j for j, s in enumerate(FIRST.split())}
     path, prio = [0.0] * n, [None] * n
     for i in range(n - 1, -1, -1):
         o = ops[i]
-        path[i] = o["t"] + max([path[j] + lag(i, j) for j in succ[i]] + [0.0])
+        path[i] = o["path"] = o["t"] + max([path[j] + lag(i, j) for j in succ[i]] + [0.0])
         if o["visit"] >= 0:
             prio[i] = (-1000 * o["visit"] - rank.get(o["tag"], 999), 0)
         else:
             prio[i] = (max(prio[j][0] for j in succ[i]) + EARLY, path[i])
-    left = [len(p) for p in pred]
-    ready = [i for i in range(n) if not left[i]]
-    est, end, free, used, order = [0.0] * n, [0.0] * n, {}, {}, []
+    fore = [[(j, lag(i, j)) for j in succ[i]] for i in range(n)]
+    back = [[(j, lag(j, i)) for j in pred[i]] for i in range(n)]
 
-    def start(i):
-        o = ops[i]
-        s = max(est[i], free.get(o["q"], 0.0)) if o["fn"] is not None else est[i]
-        for b in o["b"]:
-            for q, e in used.get(b, {}).items():
-                if q != o["q"]:
-                    s = max(s, e + HOP)
-        return s
+    def schedule(after, before, prio, slack):
+        left = [len(p) for p in before]
+        ready = [i for i in range(n) if not left[i]]
+        est, end, free, used, order = [0.0] * n, [0.0] * n, {}, {}, []
 
-    while ready:
-        st = {i: start(i) for i in ready}
-        first = min(ready, key=lambda i: (st[i], i))
-        q = ops[first]["q"]
-        i = max((j for j in ready if ops[j]["q"] == q and st[j] <= st[first] + SLACK), key=lambda j: (prio[j], -j))
-        o = ops[i]
-        end[i] = st[i] + o["t"]
-        if o["fn"] is not None:
-            free[q] = end[i]
-        for b in o["b"]:
-            used.setdefault(b, {})[q] = end[i]
-        ready.remove(i)
-        order.append(i)
-        for j in succ[i]:
-            est[j] = max(est[j], end[i] + lag(i, j))
-            left[j] -= 1
-            if not left[j]:
-                ready.append(j)
-    ops[0]["span"] = max(end)
+        def start(i):
+            o = ops[i]
+            s = max(est[i], free.get(o["q"], 0.0)) if o["fn"] is not None else est[i]
+            for b in o["b"]:
+                for q, e in used.get(b, {}).items():
+                    if q != o["q"]:
+                        s = max(s, e + HOP)
+            return s
+
+        while ready:
+            st = {i: start(i) for i in ready}
+            first = min(ready, key=lambda i: (st[i], i))
+            q = ops[first]["q"]
+            i = max((j for j in ready if ops[j]["q"] == q and st[j] <= st[first] + slack), key=lambda j: (prio[j], -j))
+            o = ops[i]
+            end[i] = st[i] + o["t"]
+            if o["fn"] is not None:
+                free[q] = end[i]
+            for b in o["b"]:
+                used.setdefault(b, {})[q] = end[i]
+            ready.remove(i)
+            order.append(i)
+            for j, d in after[i]:
+                est[j] = max(est[j], end[i] + d)
+                left[j] -= 1
+                if not left[j]:
+                    ready.append(j)
+        return max(end), end, order
+
+    span, end, order = schedule(fore, back, prio, SLACK)
+    for slack in TURNS:
+        late = schedule(back, fore, end, slack)[1]
+        s, end, o = schedule(fore, back, late, slack)
+        if s < span:
+            span, order = s, o
+    ops[0]["span"] = span
     return [ops[i] for i in order]
 
 
@@ -221,8 +237,9 @@ def rank_program(g, core, T, topo):
         s = "d%d" % nd[0]
         nd[0] += 1
         op(q, lambda e: e.dma_start(out, in_), r, w)
-        lat[0] += ops[-1]["t"]
-        note(src=s, sem=s, val=16, inc=16, t=50, lat=2000 + lat[0], line="dma" + q)
+        big = w[0][:2] != "PK"
+        lat[0] += ops[-1]["t"] * big
+        note(src=s, sem=s, val=16, inc=16, t=50, lat=2000 + lat[0] + (0 if big else 1000), line="dma" + q)
 
     def ts(out, in0, s1, op0, s2=None, op1=None, r=(), w=(), b=()):
         if op1 is None:
@@ -255,20 +272,21 @@ def rank_program(g, core, T, topo):
         else:
             op("g", lambda e: e.iota(out, pat, base, mult), ["pool"], w + ["pool"])
 
-    lw = H // LCH
+    LCH = len(IN) - 1
     for c in range(LCH):
-        dma("s", T.PK[:, c * lw:(c + 1) * lw], T.fld[:, c * lw:(c + 1) * lw], w=["PK%d" % c])
-        if c == 0:
+        dma("s", T.PK[:, IN[c]:IN[c + 1]], T.fld[:, IN[c]:IN[c + 1]], w=["PK%d" % c])
+        lat[0] += 2.55 * (IN[c + 1] - IN[c])
+        if c == 1:
             dma("a", T.WI[:], T.wnd[:], w=["WI"])
     dma("s", T.REC[:, 0:V], T.rec[:], w=["REC"])
     dma("s", T.REC[:, V:2 * V], T.rec[:], w=["REC2"])
-
     lat[0] = 0
 
     iota(T.CP[:, 0:1], [[1, 1]], 0, 1, ["CP"], False)
+    iota(T.RD[:], [[1, 128]], 0, -1, ["RD"])
     iota(T.RM[:], [[1, 240]], 0, 0, ["RM"])
-    iota(T.RK[:], [[0, 24], [1, 16]], 0, 0, ["RK"])
     iota(T.RG[:], [[1, 8], [0, 16]], 0, 0, ["RG"])
+    iota(T.RK[:], [[0, 24], [1, 16]], 0, 0, ["RK"])
     iota(T.FW[:, V:V + 32], [[0, 32]], 0, 0, ["FWd"])
     iota(T.SKF[:], [[0, 2048]], 1, 0, ["SKF"])
     note(t=4300)
@@ -280,17 +298,17 @@ def rank_program(g, core, T, topo):
     iota(T.KC[0:32, 0:128], [[0, 128]], -120 * 131072, 0, ["KCa0"])
     iota(T.KC[0:32, 128:384], [[0, 256]], 120 * 131072, 0, ["KCa1"])
     iota(T.KC[64:96, 0:256], [[0, 256]], 0, 0, ["KCd"])
-    iota(T.ZL[:], [[0, 128]], 0, 0, ["ZL"])
+    iota(T.DC[:], [[0, 256]], 512, 0, ["DC"])
     iota(T.PY[:, 64:72], [[0, 8]], 0, 0, ["PY0"])
     p = T.CP[:, 0:1]
     fill(T.O32[:], 1.0 / 32, ["O32"])
-    bits = [(0, 127), (0, 15), (4, 7), (0, 7), (3, 3), (0, 1), (3, 1), (5, 3)]
+    bits = [(0, 15), (4, 7), (0, 7), (3, 3), (0, 1), (3, 1), (5, 3)]
     for j, (sh, m) in enumerate(bits):
         ts(T.CI[:, j:j + 1], p, sh, A.logical_shift_right, m, A.bitwise_and, r=["CP"], w=["CI%d" % j])
-    cp(T.CF[:], T.CI[:], r=["CI%d" % j for j in range(8)], w=["CF"])
-    cP, c16, cG, c8, cQ, cO, cH, cB = [T.CF[:, j:j + 1] for j in range(8)]
+    cp(T.CF[:, 0:7], T.CI[:, 0:7], r=["CI%d" % j for j in range(7)], w=["CF"])
+    c16, cG, c8, cQ, cO, cH, cB = [T.CF[:, j:j + 1] for j in range(7)]
     ident = T.ISH[:, 0:128]
-    ts(ident, T.RM[:, 0:128], cP, A.is_equal, r=["RM", "CF"], w=["I"])
+    ts(ident, T.RD[:], 0.0, A.is_equal, r=["RD"], w=["I"])
     ts(T.MK[:], T.RM[:, 0:16], c16, A.is_equal, r=["RM", "CF"], w=["MK"])
     ts(T.QM[:], T.RM[:, 0:4], cQ, A.is_equal, r=["RM", "CF"], w=["QM"])
     nc = [0]
@@ -298,7 +316,7 @@ def rank_program(g, core, T, topo):
     def col(in0, s1, s2, r=("CF",)):
         j = nc[0]
         nc[0] += 1
-        act(T.CC[:, j:j + 1], in0, F.Identity, scale=s1, bias=s2, r=r, w=["CC%d" % j])
+        ts(T.CC[:, j:j + 1], in0, s1, A.mult, s2, A.add, r=r, w=["CC%d" % j])
         return T.CC[:, j:j + 1], "CC%d" % j
 
     def col2(a, b_, o, r):
@@ -308,19 +326,17 @@ def rank_program(g, core, T, topo):
         return T.CC[:, j:j + 1], "CC%d" % j
 
     def eqm(name, out, row, rrow, c, wt):
-        ts(out, row, c[0], A.is_equal, wt[0] if isinstance(wt, tuple) else wt, A.mult,
-           r=[rrow, c[1]] + ([wt[1]] if isinstance(wt, tuple) else []), w=[name])
+        ts(out, row, c[0] if isinstance(c, tuple) else c, A.is_equal, wt[0] if isinstance(wt, tuple) else wt, A.mult,
+           r=[rrow] + [x[1] for x in (c, wt) if isinstance(x, tuple)], w=[name])
 
-    p1 = col(cP, 1.0, 1.0)
     even = col(cO, -1.0, 1.0)
-    odd16 = col(cO, 65536.0, 0.0)
     not15 = col(T.MK[:, 15:16], -0.5, 0.5, r=["MK"])
-    eqm("SH", T.ISH[:, 128:256], T.RM[:, 0:128], "RM", p1, even)
-    eqm("DO", T.DO[:], T.RM[:, 0:128], "RM", (cP, "CF"), odd16)
+    eqm("SH", T.ISH[:, 128:256], T.RD[:], "RD", 1.0, even)
     for k in range(16):
         act(T.SK[:, 128 * k:128 * k + 128], ident, F.Identity, scale=T.MK[:, k:k + 1], r=["I", "MK"], w=["SK%d" % k])
-    act(T.NSH[:], T.ISH[:, 128:256], F.Identity, scale=-1.0, r=["SH"], w=["NSH"])
-    act(T.I16[:], ident, F.Identity, scale=1.0 / 16, r=["I"], w=["I16"])
+    ts(T.DO[:], ident, cO, A.mult, 65536.0, A.mult, r=["I", "CF"], w=["DO"])
+    ts(T.NSH[:], T.ISH[:, 128:256], -1.0, A.mult, r=["SH"], w=["NSH"])
+    ts(T.I16[:], ident, 1.0 / 16, A.mult, r=["I"], w=["I16"])
     a15 = col(c16, -2.0, 15.0)
     odd_w = col(c16, 2.0, 1.0)
     c8x = col(c8, 16.0, 0.0)
@@ -330,20 +346,17 @@ def rank_program(g, core, T, topo):
     ybase = col(cH, 32.0, -56.0)
     q0n = col(T.QM[:, 0:1], -1.0, 0.0, r=["QM"])
     q1s = col(T.QM[:, 1:2], 2.0 ** -14, 0.0, r=["QM"])
-    q0h = col(T.QM[:, 0:1], 0.5, 0.0, r=["QM"])
-    q3h = col(T.QM[:, 3:4], 0.5, 0.0, r=["QM"])
-    rev = col2(a15[0], cP, A.add, [a15[1], "CF"])
     ymask = col2(c8, cG, A.is_equal, ["CF"])
     q02 = col2(T.QM[:, 0:1], T.QM[:, 2:3], A.add, ["QM"])
-    qh = col2(q0h[0], q3h[0], A.subtract, [q0h[1], q3h[1]])
-    qa = col2(q0h[0], q3h[0], A.add, [q0h[1], q3h[1]])
+    qh = col2(T.QM[:, 0:1], T.QM[:, 3:4], A.subtract, ["QM"])
+    qa = col2(T.QM[:, 0:1], T.QM[:, 3:4], A.add, ["QM"])
     ts(T.B8[:], T.RM[:, 0:8], cG, A.is_equal, r=["RM", "CF"], w=["B8"])
     ts(T.WH0[:], T.WI[:], -2048.0, A.add, r=["WI"], w=["WH0"])
     cp(T.WU[:], T.WI[:], r=["WI"], w=["WU"])
     ts(T.HM[:], T.RK[:], 0.0, A.not_equal, r=["RK"], w=["HM"])
     ts(T.MS0[:], T.RK[:, 0:256], c16, A.is_ge, 0.375, A.mult, r=["RK", "CF"], w=["MS0"])
-    eqm("MVH", T.MVH[:], T.RM[:, 0:128], "RM", p1, not15)
-    eqm("TBH", T.TBH[:], T.RM[:, 0:128], "RM", rev, not15)
+    eqm("MVH", T.MVH[:], T.RD[:], "RD", 1.0, not15)
+    eqm("TBH", T.TBH[:], T.RD[:], "RD", a15, not15)
     eqm("BO", T.BO[:], T.RG[:], "RG", (cG, "CF"), 1.0 / 32)
     eqm("XN", T.XN[:, 0:128], T.RG[:], "RG", (c8, "CF"), q0n)
     eqm("XL", T.XL[:, 0:128], T.RG[:], "RG", (c8, "CF"), q02)
@@ -351,23 +364,27 @@ def rank_program(g, core, T, topo):
     eqm("XH", T.XH[:, 0:128], T.RM[:, 0:128], "RM", c8x, qh)
     eqm("XA", T.XA[:, 0:128], T.RM[:, 0:128], "RM", c8x, qa)
     ts(T.BM[:], T.RM[:, 0:4], cB, A.is_equal, r=["RM", "CF"], w=["BM"])
+    ts(T.CC[:, 28:32], T.BM[:], 0.5, A.mult, r=["BM"], w=["BH"])
     for name in ("XN", "XH", "XA", "XC", "XL"):
+        half = name in ("XH", "XA")
         for a in range(4):
-            act(T[name][:, 128 * a + 128:128 * a + 256], T[name][:, 0:128], F.Identity, scale=T.BM[:, a:a + 1], r=[name, "BM"], w=[name + str(a)])
-            note(t=170)
+            ts(T[name][:, 128 * a + 128:128 * a + 256], T[name][:, 0:128], (T.CC[:, 28 + a:29 + a] if half else T.BM[:, a:a + 1]), A.mult,
+               r=[name, "BH" if half else "BM"], w=[name + str(a)])
+            if a < XACT:
+                src, sc, out = T[name][:, 0:128], (T.CC[:, 28 + a:29 + a] if half else T.BM[:, a:a + 1]), T[name][:, 128 * a + 128:128 * a + 256]
+                note(q="a", src="a", t=170, fn=lambda e, out=out, src=src, sc=sc: e.activation(out, src, F.Identity, scale=sc))
     eqm("CW", T.CW[:], T.RM[:], "RM", c112, 2.0 ** -13)
     ts(T.YF0[:], T.RM[:, 0:8], ybase[0], A.add, ymask[0], A.mult, r=["RM", ybase[1], ymask[1]], w=["YF0"])
     tt(T.HDM[:], T.MVH[:], T.TBH[:], A.subtract, r=["MVH", "TBH"], w=["HDM"])
     tt(T.AVM[:], T.MVH[:], T.TBH[:], A.add, r=["MVH", "TBH"], w=["AVM"])
     ts(T.YOF[:], T.YF0[:], 64.0, A.add, r=["YF0"], w=["YOF"])
-    act(T.O32F[:], T.O32[:], F.Identity, r=["O32"], w=["O32F"])
-    fill(T.Q16[:, 64:192], 0.0, ["Q0"])
+    fill(T.Q16[:, 64:128], 0.0, ["Q0"])
     fill(T.THR[:], -4.5, ["THR"])
     fill(B[0][:, 256:512], 0.0, ["Z0"], [0])
     note(k="w")
 
     for c in range(LCH):
-        sl = slice(c * lw, (c + 1) * lw)
+        sl, lw, first = slice(IN[c], IN[c + 1]), IN[c + 1] - IN[c], len(ops)
         if c in UNP:
             ts(T.YO[:, sl], T.PK[:, sl], -2.0 ** 23, A.add, -2047.5, A.add, r=["PK%d" % c], w=["YO%d" % c])
             act(T.YO[:, sl], T.YO[:, sl], F.Identity, bias=MAG / 2, r=["YO%d" % c], w=["YO%d" % c])
@@ -377,44 +394,38 @@ def rank_program(g, core, T, topo):
             ts(B[2 + c][:, 0:lw], T.HI[:, sl], float(V), A.mult, r=["HI%d" % c], w=["HJ%d" % c], b=[2 + c])
         note(k="w")
         tt(T.FW[:, sl], T.PK[:, sl], B[2 + c][:, 0:lw], A.subtract, r=["HJ%d" % c], w=["FW%d" % c], b=[2 + c])
-        note(t=570)
-        act(T.FW[:, H + c * lw:H + (c + 1) * lw], B[2 + c][:, 0:lw], F.Identity, scale=1.0 / V, r=["HJ%d" % c], w=["FW%d" % (LCH + c)], b=[2 + c])
-        note(t=570)
+        act(T.FW[:, H + IN[c]:H + IN[c + 1]], B[2 + c][:, 0:lw], F.Identity, scale=1.0 / V, r=["HJ%d" % c], w=["FW%d" % (LCH + c)], b=[2 + c])
+        for o in ops[first:]:
+            o["t"] = 60 + lw
 
-    def late_constants():
-        act(T.NI[:], ident, F.Identity, scale=-1.0, r=["I"], w=["NI"])
-        act(T.NI2[:], ident, F.Identity, scale=-0.5, r=["I"], w=["NI2"])
-        act(T.WIM[:], ident, F.Identity, scale=-0.1875, r=["I"], w=["WIM"])
-        for name, wt in (("BP1", 131072.0), ("BP2", 262144.0), ("BN", -131072.0)):
-            for j in range(3):
-                act(T[name][:, 8 * j:8 * j + 8], T.B8[:], F.Identity, scale=(wt if j == 0 else -wt), r=["B8"], w=[name + str(j)])
-        act(T.WT8[:], T.B8[:], F.Identity, scale=odd_w[0], r=["B8", odd_w[1]], w=["WT8"])
-        act(T.SC[:], T.HM[:], F.Identity, scale=-1.0e8, bias=1.0e8, r=["HM"], w=["SC"])
-        act(T.PM[:, 0:256], T.HM[:, 0:256], F.Identity, scale=-2.0 ** 99, bias=2.0 ** 98, r=["HM"], w=["PM"])
-        act(T.PM[:, 256:512], T.HM[:, 0:256], F.Identity, scale=-2.0 ** 99, bias=2.0 ** 98, r=["HM"], w=["PN"])
-        act(T.MSK[:, 0:256], T.MS0[:], F.Identity, bias=0.1875, r=["MS0"], w=["MSK"])
-        act(T.MSK[:, 256:272], T.HM[:, 0:16], F.Identity, scale=0.0, bias=0.5625, r=["HM"], w=["MSL"])
-        act(T.MSK[:, 272:512], T.HM[:, 0:240], F.Identity, scale=0.0, bias=0.1875, r=["HM"], w=["MSM"])
+    act(T.O32F[:], T.O32[:], F.Identity, scale=0.5, r=["O32"], w=["O32F"])
+    for name, wt in (("NI", -1.0), ("NI2", -0.5), ("WIM", -0.1875), ("I2K", -2048.0)):
+        act(T[name][:], ident, F.Identity, scale=wt, r=["I"], w=[name])
+        note(t=170)
+    for name, wt in (("BP1", 131072.0), ("BP2", 262144.0), ("BN", -131072.0)):
+        for j in range(3):
+            act(T[name][:, 8 * j:8 * j + 8], T.B8[:], F.Identity, scale=(wt if j == 0 else -wt), r=["B8"], w=[name + str(j)])
+    act(T.WT8[:], T.B8[:], F.Identity, scale=odd_w[0], r=["B8", odd_w[1]], w=["WT8"])
+    act(T.SC[:], T.HM[:], F.Identity, scale=-1.0e8, bias=1.0e8, r=["HM"], w=["SC"])
+    act(T.PM[:, 0:256], T.HM[:, 0:256], F.Identity, scale=-2.0 ** 99, bias=2.0 ** 98, r=["HM"], w=["PM"])
+    act(T.PM[:, 256:512], T.HM[:, 0:256], F.Identity, scale=-2.0 ** 99, bias=2.0 ** 98, r=["HM"], w=["PN"])
+    act(T.MSK[:, 0:256], T.MS0[:], F.Identity, bias=0.1875, r=["MS0"], w=["MSK"])
+    act(T.MSK[:, 256:272], T.HM[:, 0:16], F.Identity, scale=0.0, bias=0.5625, r=["HM"], w=["MSL"])
+    act(T.MSK[:, 272:512], T.HM[:, 0:240], F.Identity, scale=0.0, bias=0.1875, r=["HM"], w=["MSM"])
 
-    late_constants()
     FWR = ["FW%d" % c for c in range(2 * LCH)] + ["FWd"]
     KCR = ["KCa0", "KCa1", "KCb", "KCc", "KCd", "O32"]
 
-    def expand(bk, out0, mat, name, src, sname, c0, start, stop):
+    def expand(bk, out0, name, src, sname, c0, start, stop):
         for h in range(2):
             for a in range(4):
                 o = out0 + 128 * h + 32 * a
                 m = min(32, 512 - o)
-                mm(bk, B[bk][:, o:o + m], mat[:, 128 * a + 128:128 * a + 256], src[:, c0 + 32 * h:c0 + 32 * h + m],
+                mm(bk, B[bk][:, o:o + m], T[name][:, 128 * a + 128:128 * a + 256], src[:, c0 + 32 * h:c0 + 32 * h + m],
                    start, stop and (start or (h == 1 and a == 3)), r=[name + str(a), sname])
 
     def chunk_of(w):
         return [c for c in range(len(PC)) if PC[c][0] <= w < PC[c][0] + PC[c][1]][0]
-
-    def arrive(t):
-        op("v", None, w=["WH%d" % t])
-        note(src="arr%d" % t, sem="arr%d" % t, val=n_in, t=0, line="ring")
-        ts(T.WU[:], T["WH%d" % t][:], 2048.0, A.add, r=["WH%d" % t], w=["WU"])
 
     for t in range(NV):
         last = t == NV - 1
@@ -560,16 +571,14 @@ def rank_program(g, core, T, topo):
                 for h in range(2):
                     ts(T.KF[:, 512 * h + 399:512 * h + 512:16], T.ZA[:, 8 * h:8 * h + 8], -2048.0, A.add, r=["ZA"], w=["KZ%d" % h])
 
-        def threshold(step):
-            if t == 0:
-                return
-            if step == 0:
-                mm(3, B[3][:, 280:281], T.O32F[:], T.ACC[:, 0:1], True, True, r=["O32F", "ACC"])
-                cp(T.PI[:, 0:1], B[3][:, 280:281], w=["PI"], b=[3])
-            elif step == 1:
-                ts(T.PJ[:, 0:1], T.PI[:, 0:1], 1, A.bitwise_and, r=["PI"], w=["PJ"])
-            else:
-                ts(T.THR[:, 0:1], T.PJ[:, 0:1], -1.0, A.mult, -4.5, A.add, r=["PJ"], w=["THR"])
+        def threshold():
+            if t:
+                x = B[3][:, 280:281]
+                mm(3, x, T.O32F[:], T.ACC[:, 0:1], True, True, r=["O32F", "ACC"])
+                act(T.TA[:, 0:1], x, F.Identity, bias=1.5 * 2.0 ** 23, w=["TA"], b=[3])
+                act(T.TA[:, 1:2], T.TA[:, 0:1], F.Identity, scale=-1.0, bias=1.5 * 2.0 ** 23, r=["TA"], w=["TB"])
+                act(T.TA[:, 2:3], x, F.Abs, bias=T.TA[:, 1:2], r=["TB"], w=["TC"], b=[3])
+                act(T.THR[:, 0:1], T.TA[:, 2:3], F.Identity, scale=-2.0, bias=-4.5, r=["TC"], w=["THR"])
 
         for s in ORDER.split():
             c, a = s[0], s[1:]
@@ -607,41 +616,42 @@ def rank_program(g, core, T, topo):
             elif c == "Z":
                 jump(int(a))
             elif c == "T":
-                threshold(int(a))
+                threshold()
             elif c == "H":
                 mm(2, B[2][:, 0:256], T.HDM[:], WH[:], True, False, r=["HDM", wh])
                 mm(0, B[0][:, 0:256], ident, T.EH[:], True, False, r=["I"] + ["EH%d" % q for q in range(len(PC))])
         now[1] = None
         mm(3, B[3][:, 0:256], T.AVM[:], WH[:], True, False, r=["AVM", wh])
         mm(7, B[7][:], ident, T.MSK[:], True, False, r=["I", "MSK", "MSL", "MSM"])
-        mm(6, B[6][:, 0:256], T.ZL[:], WH[:], True, False, r=["ZL", wh])
+        mm(6, B[6][:, 0:256], T.O32[:], T.DC[:], True, False, r=["DC", "O32"])
         keys, kr = T.KF[:, 15:1024:16], ["KF0", "KF1", "KZ0", "KZ1"]
         ts(T.RQ[:], keys, MAG, A.add, -MAG, A.add, r=kr, w=["RQ"])
         ts(T.RI[:], keys, 4096.0, A.add, r=kr, w=["RI"])
         tt(T.P16[:], keys, T.RQ[:], A.subtract, r=kr + ["RQ"], w=["P16"])
         ts(T.KK[:], T.RI[:], 13, A.arith_shift_right, 15, A.bitwise_and, r=["RI"], w=["KK"])
         op("v", lambda e: e.transpose(T.PT[:], T.P16[:]), ["P16"], ["PT"])
-        expand(0, 0, T.XN, "XN", T.PT, "PT", 0, False, True)
-        expand(2, 0, T.XH, "XH", T.PT, "PT", 0, False, True)
+        expand(0, 0, "XN", T.PT, "PT", 0, False, True)
+        expand(2, 0, "XH", T.PT, "PT", 0, False, True)
         cp(T.Q16[:, 0:64], T.KK[:], r=["KK"], w=["QK"])
         cp(T.PY[:, 0:64], T.P16[:], r=["P16"], w=["PY"])
-        tt(T.VS[:], T.P16[:, 0:48], T.P16[:, 16:64], A.add, r=["P16"], w=["VS"])
         ts(T.EQ[:], B[0][:, 0:256], 0.0, A.is_equal, w=["EQ"], b=[0])
         mm(1, B[1][:, 0:256], T.BO[:], T.EQ[:], True, True, r=["BO", "EQ"])
         act(T.GO[:], B[1][:, 0:256], F.Sign, bias=T.THR[:, 0:1], scale=32.0, acc=(None if last else T.ACC[:, 0:1]),
             r=["THR"], w=["GO", "ACC"], b=[1])
         cp(T.Y2[:], T.PY[:].indirect(T.YOF[:]), r=["PY", "PY0", "YOF"], w=["Y2"])
-        tt(T.Q16[:, 128:168], T.Q16[:, 0:40], T.Q16[:, 8:48], A.is_equal, r=["QK", "Q0"], w=["QF"])
-        ts(T.Q16[:, 64:112], T.VS[:], 0.0, A.is_lt, -4096.0, A.mult, r=["VS", "Q0"], w=["QC"])
+        tt(T.Q16[:, 64:104], T.Q16[:, 0:40], T.Q16[:, 8:48], A.is_equal, r=["QK", "Q0"], w=["QF"])
         for gg in range(8):
             mm(0, B[0][:, 256:512:16], T.CW[:, 112 - 16 * gg:240 - 16 * gg], T.Y2[:, 16 * gg:16 * gg + 16], gg == 0, gg == 7, r=["CW", "Y2", "Z0"])
-        expand(3, 0, T.XA, "XA", T.PT, "PT", 0, False, True)
-        op("v", lambda e: e.transpose(T.QT[:], T.Q16[:]), ["QK", "QF", "QC"], ["QT"])
+        expand(3, 0, "XA", T.PT, "PT", 0, False, True)
+        expand(6, 0, "XL", T.PT, "PT", 0, False, False)
+        expand(5, 256, "XL", T.PT, "PT", 0, True, True)
+        act(T.SG[:], B[5][:, 256:512], F.Sign, bias=0.5, w=["SG"], b=[5])
+        op("v", lambda e: e.transpose(T.QT[:], T.Q16[:]), ["QK", "QF"], ["QT"])
         mm(4, B[4][:, 0:256], T.BO[:], T.EQ[:], True, False, r=["BO", "EQ"])
-        expand(4, 0, T.XN, "XN", T.QT, "QT", 128, False, True)
-        expand(5, 0, T.XC, "XC", T.QT, "QT", 0, True, True)
-        expand(7, 0, T.XC, "XC", T.PT, "PT", 0, False, False)
-        expand(7, 272, T.XC, "XC", T.PT, "PT", 0, False, False)
+        expand(4, 0, "XN", T.QT, "QT", 64, False, True)
+        expand(5, 0, "XC", T.QT, "QT", 0, True, True)
+        expand(7, 0, "XC", T.PT, "PT", 0, False, False)
+        expand(7, 272, "XC", T.PT, "PT", 0, False, False)
         scan(T.RR[:], T.HM[:, 0:256], B[0][:, 256:512], 0.0, A.mult, A.add, r=["HM"], w=["RR"], b=[0])
         tt(T.PRD[:], T.GO[:], B[2][:, 0:256], A.mult, r=["GO"], w=["PRD"], b=[2])
         ts(T.OC[:], B[0][:, 256:512:16], 8192.0, A.mult, 2048.0, A.add, w=["OC"], b=[0])
@@ -656,12 +666,12 @@ def rank_program(g, core, T, topo):
         act(T.U[:], B[5][:, 0:256], F.Abs, bias=kbias[0], scale=2.0 ** 27, r=[kbias[1]], w=["U"], b=[5])
         mm(7, B[7][:, 0:256], T.NI2[:], T.RR[:], False, False, r=["NI2", "RR"])
         mm(7, B[7][:, 256:512], T.NI2[:], T.RR[:], False, False, r=["NI2", "RR"])
-        expand(6, 0, T.XL, "XL", T.PT, "PT", 0, False, False)
         mm(7, B[7][:, 272:512], T.WIM[:], T.WA[:, 0:240], False, False, r=["WIM", "WA"])
         mm(7, B[7][:, 0:256], T.WIM[:], T.WA[:], False, True, r=["WIM", "WA"])
-        expand(6, 0, T.XN, "XN", T.QT, "QT", 64, False, False)
         for a in range(16):
             mm(1, B[1][:, 256:272], T.SK[:, 128 * a:128 * a + 128], T.WA[:, a:256:16], a == 0, a == 15, r=["SK%d" % a, "WA"])
+        mm(6, B[6][:, 0:256], T.I2K[:], T.SG[:], False, False, r=["I2K", "SG"])
+        note(tag="I6")
         mm(6, B[6][:, 0:256], T.NI[:], T.U[:], False, True, r=["NI", "U"])
         act(T.LS[:], B[6][:, 0:256], F.Identity, w=["LS"], b=[6])
         if last:
@@ -675,20 +685,24 @@ def rank_program(g, core, T, topo):
         tt(T.K4[:], T.K3[:], T.K2[:], A.add, r=["KA", "K2"], w=["KB"])
         for j in range(2):
             ts(T.OFF[:, j:16:2], T.K4[:, j:16:2], 8192.0, A.mult, dummy[j][0], A.min, r=["KB", dummy[j][1]], w=["OFF%d" % j])
+        if not last:
+            op("v", None, w=["WH%d" % (t + 1)])
+            note(src="arr%d" % (t + 1), sem="arr%d" % (t + 1), val=n_in, t=0, line="ring")
+            ts(T.WU[:], T["WH%d" % (t + 1)][:], 2048.0, A.add, r=["WH%d" % (t + 1)], w=["WU"])
         for b in range(7, -1, -1):
-            if b == 3 and not last:
-                arrive(t + 1)
             tt(T.FW[:].indirect(T.OFF[:, 2 * b:2 * b + 2]), T.OM[:, 32 * b:32 * b + 32], T.LS[:, 32 * b:32 * b + 32], A.max,
                r=["OFF0", "OFF1", "OM", "LS"], w=FWR)
             note(t=180)
 
     now[0], now[1] = NV, "end"
-    for c in range(LCH):
-        act(B[2 + c][:, 0:lw], T.FW[:, H + c * lw:H + (c + 1) * lw], F.Identity, scale=float(V), r=FWR, b=[2 + c])
-        note(k="w", t=570)
-        tt(T.YO[:, c * lw:(c + 1) * lw], T.FW[:, c * lw:(c + 1) * lw], B[2 + c][:, 0:lw], A.add, r=FWR, w=["YO%d" % c], b=[2 + c])
-        dma("s", T.yf[:, c * lw:(c + 1) * lw], T.YO[:, c * lw:(c + 1) * lw], r=["YO%d" % c], w=["yf%d" % c])
-    op("s", None, r=["yw"] + ["yf%d" % c for c in range(LCH)])
+    for c in range(len(OUT) - 1):
+        a, b, bk = OUT[c], OUT[c + 1], 2 + c
+        act(B[bk][:, 0:b - a], T.FW[:, H + a:H + b], F.Identity, scale=float(V), r=FWR, b=[bk])
+        note(k="w", t=60 + b - a)
+        tt(T.YO[:, a:b], T.FW[:, a:b], B[bk][:, 0:b - a], A.add, r=FWR, w=["YP%d" % c] + ["YO%d" % j for j in UNP], b=[bk])
+        note(t=60 + b - a)
+        dma("s", T.yf[:, a:b], T.YO[:, a:b], r=["YP%d" % c], w=["yf%d" % c])
+    op("s", None, r=["yw"] + ["yf%d" % c for c in range(len(OUT) - 1)])
     note(src="end")
     emit(g, T, arrange(ops))
     g.wait_ge(T.sem.sent, n_out * (NV - 1))

@@ -2,21 +2,37 @@ from concourse.mybir import AluOpType as A, ActivationFunctionType as F
 
 V, H, K, NV = 4096, 2048, 256, 5
 MAG = 1.5 * 2.0 ** 36
-IN = [0, 512, 1024, 1536, 1792, 2048]
-OUT = [0, 256, 768, 1280, 1792, 2048]
-PC = [(0, 32, 0), (32, 32, 0), (64, 64, 0), (128, 64, 0), (192, 64, 6)]
-AF = 4
-MV = [1, 1]
-UNP = (1, 2, 4)
-EARLY = 0
-XACT = 4
-KD = [list(range(0, 8)), list(range(0, 8))]
-ORDER = ("A G0 T0 P0 G1 N0 P1 Xa0 F0 G2 N1 Xa1 F1 G3 F2 P2 F3 G4 N2 N4 Xa2 Xa3 G5 P3 S0 Xa6 S1 Xv7 N3 Xa4 Xv5 W4 W0123 K0 M0 S3 S2 "
-         "M1 K1 Z0 Z1 Z2 Z3 V0a V0b D0a B0a D0b B0b E0v E0a R0 V1a V1b D1a B1a D1b B1b H E1v E1a R1")
-FIRST = ("F2 QT V1b W4 W0123 N3 A V0a Xa4 P1 F3 P2 Xa2 G0 B0a EQ S1 Xa3 N1 Z0 M0 G3 M1 B1b N0 P3 G1 Xa1 N2 V1a G2 G4 K0 Xv5 G5 R1 D0a RQ "
-         "S3 S2 D0b F1 F0 D1a E0v Z3 RR Z1 D1b QF P0 WO XN4 R0 N4 E0a Xv7 S0 E1v KK yw B0b LO E1a SG PT P WO0 XN0 WF T0 RI PY OC CW0 Z2 "
-         "XC5 V0b Xa0 KB WA K1 end QK XH2 K AVM3 BO1 NI6 DC6 XA3 I6 BO4 PRD Y LS WU WIM7 XL5 WG B1a GO U NI7 XC7 KA H FW OFF PS I7 SK1 "
-         "OM XL6 Xa6 WH")
+AL = 0.1875
+CFG = {
+    "IN": [0, 256, 768, 1280, 1792, 2048],
+    "OUT": [0, 256, 768, 1280, 1792, 2048],
+    "UNP": (1, 3),
+    "PC": [(224, 32, 0, "v"), (192, 32, 0, "v"), (128, 64, 0, "v"), (64, 64, 1, "v"), (0, 64, 1, "v")],
+    "WR": [(0, 128, 1), (128, 128, 0)],
+    "XV": (0,),
+    "KD": [0, 12],
+    "GW": 32,
+    "VG": 2,
+    "MEAN": "aa",
+    "TB": [dict(eq=(0, 0), vo=(2, 256), df=(3, 0), av=(5, 384), va=(6, 0), ls=(1, 256), kk=(4, 384), pr=(7, 0), cc=(2, 384), zz=(2, 420)),
+           dict(eq=(0, 256), vo=(3, 384), df=(0, 384), av=(5, 128), va=(5, 0), ls=(5, 256), kk=(3, 256), pr=(1, 0), cc=(3, 128), zz=(0, 0))],
+    "TH": (2, 500),
+    "WR0": [(192, 64, 0), (128, 64, 0), (64, 64, 1), (0, 64, 1)],
+    "HEAD": {"v": "G0a G1a G2a IH0 IN0 G2b G3a IH1 IN1 G3b G4a IH2 IN2 G4b IX2 IH3 IN3 IX0",
+             "a": "IT0 X7 X6 IT1 X5 X4 IT2 X3 M1 IT3 X1", "p": "P0 P1 P2 K1 P3 S3 S2 P4 K0"},
+    "LOAD": {"v": "Ua0 Ub0 Uc0 Ua1 Ua2 Ub2 Uc1 Ua3 Uc2 Ua4 Ub4 UW Uc4 Uc3 UH", "a": "Uc0 Ua1 Ub1 Uc1 Uc2 Ua3 Ub3 Uc3 Uc4"},
+    "XV0": (2, 0),
+    "WAT": 4,
+    "ORDER": {
+        "v": "G0a G1a N0 G2a N1 G2b WU0< G3a N2 G3b G4a N3 G4b N4 V1a X0 V1f V1c V1b V1d V1e EH1 EH0 ZI1 SC1 RQ1 ZA1 PP1 QS1 ZP1 MX1 PT1 "
+             "CS1 EQ1 RR1 ZI0 OC1 SC0 ZA0 RQ0 ZP0 PP0 QS0 PD1 MX0 PS1 PT0 LO1 WO1 KA1 EQ0 CS0 OM1 RR0 OC0 KB1 OM0 OF1 PS0 F7 LO0 F6 KA0 "
+             "F5 KB0 F4 OF0 PD0 F3 WO0 F2 F1 WU1 F0",
+        "a": "TA TB X7 X6 TC X4 X5 X3 M1 X2 X1 ET1 B1a M0 SQ1 ET0 B0b TD B0a B0d B0c SQ0 GO1 SG1 U1 U0 GO0 LS1 SG0 LS0",
+        "p": "P0 K1 TM P1 K0 P2 S3 P3 S2 DX1a P4 MP1 KX1 DM1a EM1 ZM1 S1 EV1a S0 DX0b EB1a EV1c DM0b DX0a DM0a EV1b EV1f EV1e EV1d R1 "
+             "DX0d DM0d DX0c DM0c EB0a EB0b ZM0 CM1 QB1 EB0d PA1 EB0c R0 SA1 BO1 SB1 DA1 PB1 DB1 PC1 AA1 PW1 AB1 KM1 PA0 SA0 LA0 QB0 CM0 "
+             "KM0 PB0 BO0 LA1 LB1 LC1 LD1 PC0 PW0 AA0 LB0 DA0 DB0 SB0 LC0 LD0 AB0",
+        "g": "TO1 TO0"},
+}
 
 
 def _sb(n, d):
@@ -24,28 +40,28 @@ def _sb(n, d):
 
 
 SCRATCH = {
-    "PK": _sb(H, "int32"), "HI": _sb(H, "int32"), "FW": _sb(V + 32, "float32"), "REC": _sb(2 * V, "bfloat16"), "YO": _sb(H, "float32"),
+    "PK": _sb(H, "int32"), "HI": _sb(H, "int32"), "FW": _sb(V + 96, "float32"), "REC": _sb(2 * V, "bfloat16"), "YO": _sb(H, "float32"),
     "WI": _sb(K, "int32"), "WU": _sb(K, "uint16"), "EU": _sb(K, "uint16"), "EH": _sb(K, "float16"), "ET": _sb(K, "bfloat16"),
-    "G1": _sb(V, "float16"), "GF": _sb(1024, "float32"), "X": _sb(V, "bfloat16"), "AD": _sb(V, "bfloat16"), "MB": _sb(K, "bfloat16"),
-    "KF": _sb(1024, "float32"), "RQ": _sb(64, "float32"), "P16": _sb(64, "float16"), "PT": _sb(64, "float16"),
-    "PY": _sb(72, "float32"), "RI": _sb(64, "int32"), "KK": _sb(64, "int32"),
-    "Q16": _sb(128, "float16"), "QT": _sb(128, "float16"), "SQ": _sb(16, "float32"), "ZI": _sb(16, "int32"), "ZA": _sb(16, "int32"),
-    "EQ": _sb(K, "bfloat16"), "GO": _sb(K, "bfloat16"), "WA": _sb(K, "bfloat16"), "PRD": _sb(K, "float32"), "SG": _sb(K, "bfloat16"),
+    "G1": _sb(V, "float16"), "GF": _sb(2048, "float32"), "X": _sb(V, "bfloat16"), "AD": _sb(V, "bfloat16"), "MB": _sb(K, "bfloat16"),
+    "KF": _sb(1024, "float32"), "RQ": _sb(64, "float32"), "P16": _sb(64, "float16"), "PT": _sb(64, "float16"), "QS": _sb(16, "float32"),
+    "SQ": _sb(16, "float32"), "ZI": _sb(16, "int32"), "ZA": _sb(16, "int32"),
+    "EQ": _sb(K, "bfloat16"), "GO": _sb(K, "bfloat16"), "PRD": _sb(K, "float32"), "SG": _sb(K, "bfloat16"),
     "ACC": _sb(4, "float32"), "TA": _sb(4, "float32"), "THR": _sb(4, "float32"),
-    "Y2": _sb(128, "float16"), "RR": _sb(K, "float16"), "OC": _sb(16, "uint16"), "U": _sb(K, "bfloat16"),
-    "OM": _sb(K, "float32"), "LS": _sb(K, "float32"), "PS": _sb(2 * K, "float32"), "LO": _sb(32, "float32"), "K2": _sb(16, "float32"),
+    "CS0": _sb(512, "float32"), "CS1": _sb(512, "float32"), "RR": _sb(K, "float16"), "OC": _sb(16, "uint16"), "U": _sb(K, "bfloat16"),
+    "OM": _sb(K, "float32"), "LS": _sb(K, "float32"), "PS": _sb(2 * K, "float32"), "LO": _sb(32, "float32"),
     "K3": _sb(16, "float32"), "K4": _sb(16, "float32"), "OFF": _sb(16, "uint16"), "WF": _sb(K, "float32"), "WG": _sb(K, "float32"),
-    "RM": _sb(240, "bfloat16"), "RD": _sb(128, "bfloat16"), "RG": _sb(128, "bfloat16"), "RK": _sb(384, "bfloat16"), "CP": _sb(4, "int32"),
-    "CI": _sb(8, "int32"), "CF": _sb(8, "float32"), "CC": _sb(32, "float32"), "MK": _sb(16, "float32"), "QM": _sb(4, "float32"),
-    "ISH": _sb(256, "bfloat16"), "NSH": _sb(128, "bfloat16"), "I16": _sb(128, "bfloat16"), "NI": _sb(128, "bfloat16"), "I2K": _sb(128, "bfloat16"),
-    "NI2": _sb(128, "bfloat16"), "WIM": _sb(128, "bfloat16"), "DO": _sb(128, "bfloat16"), "SK": _sb(2048, "bfloat16"), "SKF": _sb(2048, "float32"),
-    "DC": _sb(256, "bfloat16"), "O32": _sb(128, "bfloat16"), "O32F": _sb(128, "float32"), "MVH": _sb(128, "bfloat16"), "TBH": _sb(128, "bfloat16"),
+    "RD": _sb(128, "bfloat16"), "RG": _sb(128, "bfloat16"), "RK": _sb(128, "bfloat16"), "CP": _sb(4, "int32"),
+    "CI": _sb(4, "int32"), "CF": _sb(4, "float32"), "CC": _sb(16, "float32"), "MK": _sb(16, "float32"),
+    "I": _sb(128, "bfloat16"), "SH": _sb(128, "bfloat16"), "NSH": _sb(128, "bfloat16"), "I16": _sb(128, "bfloat16"), "NI": _sb(128, "bfloat16"),
+    "I2K": _sb(128, "bfloat16"), "PSH": _sb(128, "bfloat16"), "NIU": _sb(128, "bfloat16"), "BNW": _sb(768, "bfloat16"),
+    "NI2": _sb(128, "bfloat16"), "WIM": _sb(128, "bfloat16"), "SK": _sb(2048, "bfloat16"), "SKF": _sb(2048, "float32"),
+    "O32": _sb(128, "bfloat16"), "O32F": _sb(128, "float32"), "MVH": _sb(128, "bfloat16"), "TBH": _sb(128, "bfloat16"),
     "HDM": _sb(128, "bfloat16"), "AVM": _sb(128, "bfloat16"), "BO": _sb(128, "bfloat16"), "B8": _sb(8, "float32"),
     "BP1": _sb(24, "bfloat16"), "BP2": _sb(24, "bfloat16"), "BN": _sb(24, "bfloat16"), "WT8": _sb(8, "bfloat16"),
-    "XN": _sb(640, "bfloat16"), "XL": _sb(640, "bfloat16"), "XC": _sb(640, "bfloat16"), "XH": _sb(640, "bfloat16"), "XA": _sb(640, "bfloat16"),
-    "BM": _sb(4, "float32"),
-    "CW": _sb(240, "bfloat16"), "MS0": _sb(256, "bfloat16"), "MSK": _sb(512, "bfloat16"), "HM": _sb(384, "bfloat16"),
-    "SC": _sb(384, "bfloat16"), "PM": _sb(512, "bfloat16"), "KC": _sb(384, "bfloat16"), "YF0": _sb(8, "float32"), "YOF": _sb(8, "uint16"),
+    "XN": _sb(512, "bfloat16"), "XC": _sb(512, "bfloat16"), "XK": _sb(512, "bfloat16"), "XH": _sb(512, "bfloat16"), "XA": _sb(512, "bfloat16"),
+    "ZR": _sb(512, "bfloat16"), "CM0": _sb(160, "bfloat16"), "CM1": _sb(160, "bfloat16"),
+    "MS0": _sb(128, "bfloat16"), "MSK": _sb(256, "bfloat16"), "HM": _sb(128, "bfloat16"),
+    "SC": _sb(384, "bfloat16"), "PM": _sb(256, "bfloat16"), "KC": _sb(384, "bfloat16"),
 }
 for _t in range(NV):
     SCRATCH["WH%d" % _t] = _sb(K, "float16")
@@ -53,164 +69,685 @@ for _t in range(NV - 1):
     SCRATCH["WO%d" % _t] = _sb(K, "float16")
 for _b in range(8):
     SCRATCH["B%d" % _b] = ("psum", [128, 512], "float32")
-SEMAPHORES = ["sv", "sa", "sp", "sg", "sent"] + ["arr%d" % _t for _t in range(1, NV)] + ["d%d" % _i for _i in range(16)]
+SEMAPHORES = (["sv", "sa", "sp", "sg", "sent"] + ["arr%d_%d" % (_t, _h) for _t in range(1, NV) for _h in range(2)]
+              + ["d%d" % _i for _i in range(16)])
+
+CYC, PCYC, GATHER, SCATTER, VCALL, ACALL = 0.95, 0.48, 1.5, 3.5, 50, 65
+HOP, SAME, LINK, SLACK, DMA0, DMARATE = 70, 60, 2600, 60, 2000, 200.0
+POOL = ("pool", (0, 128, 0, 0, 1))
+_KEPT = {}
 
 
-TIME = {"G": 880, "GF": 1720, "X": 880, "AD": 170, "KF": 440, "EQ": 300, "GO": 300, "WA": 300, "U": 300, "LS": 300, "PRD": 300, "WO": 300,
-        "WF": 300, "WG": 300, "RR": 300, "PS": 570, "PN": 300, "MSM": 300, "OM": 460, "Y": 250, "MB": 170, "WU": 170, "QT": 120, "RQ": 100,
-        "RI": 100, "P": 160, "SG": 300, "QF": 110, "HI": 570, "HJ": 570, "YO": 570, "SK": 170, "HM": 250, "MS": 190, "SC": 440, "PM": 300,
-        "MSK": 300, "CW": 180, "HDM": 300, "AVM": 300, "WH": 300, "Z": 200, "PK": 500, "REC": 5200, "WI": 600, "RM": 630, "RD": 400,
-        "RG": 460, "RK": 990, "DC": 720, "KCb": 990, "KCc": 460, "KCa": 600, "KCd": 720, "FWd": 260, "PY": 130, "CP": 190}
-TMM = {"SKF": 133, "KCa0": 200, "HDM": 133, "AVM": 133, "DC": 133, "BO": 133, "NI2": 133, "WIM": 133, "O32F": 133, "I": 67, "NI": 67,
-       "MSK": 266, "SH": 133, "U": 133, "SG": 133}
-HOP, SAME, LINK, SLACK = 110, 60, 2600, 60
-TURNS = [200, 120, 60, 60, 30, 30]
+def meet(a, b):
+    if a[1] <= b[0] or b[1] <= a[0] or a[3] < b[2] or b[3] < a[2]:
+        return False
+    return a[4] != b[4] or (a[2] - b[2]) % a[4] == 0
+
+
+def depend(ops):
+    seen = {}
+    for i, o in enumerate(ops):
+        dep = set(o["dep"])
+        for name, reg in o["r"]:
+            dep.update(j for j, w, q in seen.get(name, []) if w and meet(reg, q))
+        for name, reg in o["w"]:
+            old = seen.get(name, [])
+            dep.update(j for j, w, q in old if meet(reg, q))
+            seen[name] = [e for e in old if not (reg[0] <= e[2][0] and e[2][1] <= reg[1] and reg[2] <= e[2][2] and e[2][3] <= reg[3]
+                                                 and (reg[4] == 1 or (reg[4] == e[2][4] and meet(reg, e[2]))))]
+        for name, reg in o["r"]:
+            seen.setdefault(name, []).append((i, False, reg))
+        for name, reg in o["w"]:
+            seen.setdefault(name, []).append((i, True, reg))
+        if o["q"] != "p":
+            dep.update([ops[j]["group"][-1] for j in dep if "group" in ops[j]])
+        dep.discard(i)
+        o["dep"] = dep
+
+
+def lag(a, b):
+    if a.get("line", 0) == b.get("line", 1):
+        return LINK if b["fn"] is None else 0
+    if a["src"] != b["src"]:
+        return HOP + a["lat"]
+    return SAME if b["q"] != "p" else 0
 
 
 def arrange(ops):
     n = len(ops)
-    pred = [set() for _ in range(n)]
-    writer, readers, bank = {}, {}, {}
+    back = [dict((j, lag(ops[j], o)) for j in o["dep"]) for o in ops]
+    line, steps = {}, {}
     for i, o in enumerate(ops):
-        for r in o["r"]:
-            if r in writer:
-                pred[i].add(writer[r])
-        for w in o["w"]:
-            pred[i].update(readers.get(w, []))
-            if w in writer:
-                pred[i].add(writer[w])
-        for b in o["b"]:
-            kind, run, before = bank.get(b, ("w", [], []))
-            if kind == o["k"] != "w":
-                pred[i].update(before)
-                run.append(i)
-            else:
-                pred[i].update(run)
-                bank[b] = (o["k"], [i], run)
-        for r in o["r"]:
-            readers.setdefault(r, []).append(i)
-        for w in o["w"]:
-            writer[w] = i
-            readers[w] = []
         if "line" in o:
-            if o["line"] in writer:
-                pred[i].add(writer[o["line"]])
-            writer[o["line"]] = i
-        pred[i].discard(i)
-    succ = [[] for _ in range(n)]
+            if o["line"] in line:
+                back[i].setdefault(line[o["line"]], lag(ops[line[o["line"]]], o))
+            line[o["line"]] = i
+        steps.setdefault((o["q"], o["visit"], o["tag"]), []).append(i)
+    for (q, t, s), members in steps.items():
+        for i in (members[1:] if q == "p" else []):
+            for j in set(ops[i]["dep"]).difference(members):
+                back[members[0]].setdefault(j, -1e9)
+    for q, names in CFG["ORDER"].items():
+        chain = []
+        for t in range(-1, NV + 1):
+            head = CFG[("LOAD", "HEAD")[t + 1]].get(q, "").split() if t < 1 else []
+            for s in head + [s for s in names.split() if s not in head]:
+                chain += steps.get((q, t + s.count(">") - s.count("<"), s.strip("<>")), [])
+        for a, b in zip(chain, chain[1:]):
+            back[b].setdefault(a, 0)
+    fore = [[] for _ in range(n)]
     for i in range(n):
-        for j in pred[i]:
-            succ[j].append(i)
+        for j, d in back[i].items():
+            fore[j].append((i, d))
+    left = [len(f) for f in fore]
+    todo, path = [i for i in range(n) if not left[i]], [0.0] * n
+    while todo:
+        i = todo.pop()
+        path[i] = ops[i]["t"] + max([path[j] + d for j, d in fore[i]] + [0.0])
+        for j in back[i]:
+            left[j] -= 1
+            if not left[j]:
+                todo.append(j)
+    left = [len(b) for b in back]
+    ready = [i for i in range(n) if not left[i]]
+    est, end, free, used, opened, order = [0.0] * n, [0.0] * n, {}, {}, set(), []
 
-    def lag(j, i):
-        if ops[j].get("line", 0) == ops[i].get("line", 1):
-            return LINK if ops[i]["fn"] is None else 0
-        if ops[j]["src"] != ops[i]["src"]:
-            return HOP + ops[j]["lat"]
-        return SAME if ops[i]["q"] != "p" else 0
-
-    rank = {s: j for j, s in enumerate(FIRST.split())}
-    path, prio = [0.0] * n, [None] * n
-    for i in range(n - 1, -1, -1):
+    def start(i):
         o = ops[i]
-        path[i] = o["path"] = o["t"] + max([path[j] + lag(i, j) for j in succ[i]] + [0.0])
-        if o["visit"] >= 0:
-            prio[i] = (-1000 * o["visit"] - rank.get(o["tag"], 999), 0)
-        else:
-            prio[i] = (max(prio[j][0] for j in succ[i]) + EARLY, path[i])
-    fore = [[(j, lag(i, j)) for j in succ[i]] for i in range(n)]
-    back = [[(j, lag(j, i)) for j in pred[i]] for i in range(n)]
-
-    def schedule(after, before, prio, slack):
-        left = [len(p) for p in before]
-        ready = [i for i in range(n) if not left[i]]
-        est, end, free, used, order = [0.0] * n, [0.0] * n, {}, {}, []
-
-        def start(i):
-            o = ops[i]
-            s = max(est[i], free.get(o["q"], 0.0)) if o["fn"] is not None else est[i]
-            for b in o["b"]:
-                for q, e in used.get(b, {}).items():
-                    if q != o["q"]:
-                        s = max(s, e + HOP)
-            return s
-
-        while ready:
-            st = {i: start(i) for i in ready}
-            first = min(ready, key=lambda i: (st[i], i))
-            q = ops[first]["q"]
-            i = max((j for j in ready if ops[j]["q"] == q and st[j] <= st[first] + slack), key=lambda j: (prio[j], -j))
-            o = ops[i]
-            end[i] = st[i] + o["t"]
-            if o["fn"] is not None:
-                free[q] = end[i]
-            for b in o["b"]:
-                used.setdefault(b, {})[q] = end[i]
-            ready.remove(i)
-            order.append(i)
-            for j, d in after[i]:
-                est[j] = max(est[j], end[i] + d)
-                left[j] -= 1
-                if not left[j]:
-                    ready.append(j)
-        return max(end), end, order
-
-    span, end, order = schedule(fore, back, prio, SLACK)
-    for slack in TURNS:
-        late = schedule(back, fore, end, slack)[1]
-        s, end, o = schedule(fore, back, late, slack)
-        if s < span:
-            span, order = s, o
-    ops[0]["span"] = span
-    return [ops[i] for i in order]
-
-
-def emit(g, T, ops):
-    queues = {"v": g.vector, "a": g.scalar, "p": g.tensor, "g": g, "s": g.sync}
-    writer, readers, bank, clock, seen = {}, {}, {}, {}, {}
-    for i, o in enumerate(ops):
-        q, src = o["q"], o["src"]
-        deps = set()
-        for r in o["r"]:
-            if r in writer:
-                deps.add(writer[r])
-        for w in o["w"]:
-            deps.update(readers.get(w, []) + ([writer[w]] if w in writer else []))
+        s = max(est[i], free.get(o["q"], 0.0)) if o["fn"] is not None else est[i]
         for b in o["b"]:
-            for s, j in bank.get(b, {}).items():
-                if s != src or (s != "p" and "w" in (o["k"], ops[j]["k"])):
-                    deps.add(j)
+            for q, e in used.get(b, {}).items():
+                if q != o["q"]:
+                    s = max(s, e + HOP)
+        return s
+
+    unread, owed = [0] * 8, [[] for _ in range(n)]
+    for i, o in enumerate(ops):
+        for b in (o["b"] if o["q"] != "p" and o["visit"] < NV else []):
+            for j in sorted(j for j in o["dep"] if ops[j]["q"] == "p" and ops[j]["b"] == [b])[-1:]:
+                owed[ops[j]["group"][-1]].append((b, 1))
+                owed[i].append((b, -1))
+
+    def may(i):
+        o = ops[i]
+        if o["q"] == "p" and o["group"][0] != i:
+            return True
+        return not opened.intersection(o["b"]) and not (o["q"] == "p" and o["long"][0] and unread[o["b"][0]])
+
+    while ready:
+        st = {i: start(i) for i in ready if may(i)}
+        first = min(st, key=lambda i: (st[i], i))
+        q = ops[first]["q"]
+        i = max((j for j in st if ops[j]["q"] == q and st[j] <= st[first] + SLACK), key=lambda j: (path[j], -j))
+        o = ops[i]
+        end[i] = st[i] + o["t"]
+        if o["fn"] is not None:
+            free[q] = end[i]
+        for b in o["b"]:
+            used.setdefault(b, {})[q] = end[i] + o["lat"]
+            if q == "p" and o["group"][0] == i:
+                opened.add(b)
+            if q == "p" and o["group"][-1] == i:
+                opened.discard(b)
+        for b, d in owed[i]:
+            unread[b] += d
+        ready.remove(i)
+        order.append(i)
+        for j, d in fore[i]:
+            est[j] = max(est[j], end[i] + d)
+            left[j] -= 1
+            if not left[j]:
+                ready.append(j)
+    assert len(order) == n
+    _KEPT["span"] = max(end)
+    return order
+
+
+def emit(g, T, ops, order):
+    queues = {"v": g.vector, "a": g.scalar, "p": g.tensor, "g": g, "s": g.sync}
+    place = {i: n for n, i in enumerate(order)}
+    run = [ops[i] for i in order]
+    bank, clock, seen = {}, {}, {}
+    for i, o in enumerate(run):
+        q, src = o["q"], o["src"]
+        deps = set(place[j] for j in o["dep"] if q != "p" or ops[j]["q"] != "p")
+        for b in o["b"]:
+            deps.update(j for s, j in bank.get(b, {}).items() if s != src)
         know = seen.setdefault(q, {})
         waits = []
         for j in sorted(deps, reverse=True):
-            if know.get(ops[j]["src"], -1) < j:
+            if know.get(run[j]["src"], -1) < j:
                 waits.append(j)
-                ops[j]["sig"] = True
+                run[j]["sig"] = True
                 for s, n in clock[j].items():
                     know[s] = max(know.get(s, -1), n)
         o["waits"] = waits
         clock[i] = dict(know) if o["fn"] is not None else {}
         clock[i][src] = i
-        for r in o["r"]:
-            readers.setdefault(r, []).append(i)
-        for w in o["w"]:
-            writer[w] = i
-            readers[w] = []
         for b in o["b"]:
             bank.setdefault(b, {})[src] = i
     count = {}
-    for o in ops:
+    for o in run:
         if o["sem"] is None and o["sig"]:
             count[o["q"]] = count.get(o["q"], 0) + 1
             o["sem"], o["val"], o["inc"] = "s" + o["q"], count[o["q"]], 1
-    for o in ops:
+    for o in run:
         q = queues[o["q"]]
         for j in o["waits"]:
-            q.wait_ge(T.sem[ops[j]["sem"]], ops[j]["val"])
+            q.wait_ge(T.sem[run[j]["sem"]], run[j]["val"])
         if o["fn"] is not None:
             ins = o["fn"](q)
             if o["inc"]:
                 ins.then_inc(T.sem[o["sem"]], o["inc"])
+
+
+def record(T, route):
+    pid, rid, mask_out, n_in = route
+    ops, nd, lat, now, group = [], [0], [0.0], [-1, None], {}
+    IN, OUT, UNP, PC, XV, KD, VG = [CFG[k] for k in ("IN", "OUT", "UNP", "PC", "XV", "KD", "VG")]
+    shapes = {"fld": H, "rec": V, "wnd": K, "yf": H, "yw": K}
+
+    def S(name, a=0, b=None, st=1, p=(0, 128)):
+        where, shape, dt = SCRATCH.get(name, ("hbm", [128, shapes.get(name)], "float32"))
+        b = shape[1] if b is None else b
+        m = (b - a + st - 1) // st
+        return {"ap": T[name][p[0]:p[1], a:b:st], "name": name, "reg": (p[0], p[1], a, a + st * (m - 1), st), "n": m, "ps": where == "psum",
+                "two": dt in ("bfloat16", "float16", "uint16"), "f32": dt == "float32"}
+
+    def B(bk, a=0, b=None, st=1):
+        return S("B%d" % bk, a, b, st)
+
+    def IND(win, off):
+        return dict(win, ap=win["ap"].indirect(off["ap"]), n=16 * off["n"], off=off)
+
+    def ap(x):
+        return x["ap"] if isinstance(x, dict) else x
+
+    def op(q, fn, r, w, t):
+        r = [x for x in r if isinstance(x, dict)]
+        r += [x["off"] for x in r + w if "off" in x]
+        banks = sorted(set(int(x["name"][1]) for x in r + w if x["ps"]))
+        ops.append({"q": q, "src": q, "fn": fn, "r": [(x["name"], x["reg"]) for x in r], "w": [(x["name"], x["reg"]) for x in w],
+                    "b": banks, "sig": False, "sem": None, "val": 0, "inc": 0, "dep": [], "t": t, "lat": 0, "visit": now[0], "tag": now[1]})
+
+    def note(**kw):
+        ops[-1].update(kw)
+
+    def step(tag):
+        now[1] = tag
+
+    def vt(out, *ins):
+        x = ins[0]
+        if "off" in x:
+            return VCALL + CYC * GATHER * x["n"]
+        if "off" in out:
+            return VCALL + CYC * SCATTER * x["n"]
+        return VCALL + CYC * x["n"] * (0.5 if all(y["two"] for y in (out,) + ins) else 1)
+
+    def dma(q, out, in_, size):
+        s = "d%d" % nd[0]
+        nd[0] += 1
+        op(q, lambda e: e.dma_start(out["ap"], in_["ap"]), [in_], [out], 50)
+        lat[0] += 128 * size * out["n"] / DMARATE
+        note(src=s, sem=s, val=16, inc=16, lat=DMA0 + lat[0], line="dma" + q)
+
+    def ts(out, in0, s1, op0, s2=None, op1=None):
+        if op1 is None:
+            op("v", lambda e: e.tensor_scalar(out["ap"], in0["ap"], ap(s1), None, op0), [in0, s1], [out], vt(out, in0))
+        else:
+            op("v", lambda e: e.tensor_scalar(out["ap"], in0["ap"], ap(s1), ap(s2), op0, op1), [in0, s1, s2], [out], vt(out, in0))
+
+    def tt(out, in0, in1, o):
+        plain = "off" not in in0 and "off" not in out
+        t = VCALL + CYC * in0["n"] * (1 if in0["ps"] or in1["ps"] else 2) if plain else vt(out, in0)
+        op("v", lambda e: e.tensor_tensor(out["ap"], in0["ap"], in1["ap"], o), [in0, in1], [out], t)
+
+    def cp(out, in_):
+        op("v", lambda e: e.tensor_copy(out["ap"], in_["ap"]), [in_], [out], vt(out, in_))
+
+    def turn(out, in_):
+        op("v", lambda e: e.transpose(out["ap"], in_["ap"]), [in_], [out], vt(out, in_))
+
+    def fill(out, c):
+        op("v", lambda e: e.memset(out["ap"], c), [], [out], vt(out, out))
+
+    def scan(out, d0, d1, init, o0, o1):
+        op("v", lambda e: e.tensor_tensor_scan(out["ap"], d0["ap"], d1["ap"], init, o0, o1), [d0, d1], [out], vt(out, d0, d1))
+
+    def act(out, in_, f, bias=0.0, scale=1.0, acc=None):
+        op("a", lambda e: e.activation(out["ap"], in_["ap"], f, bias=ap(bias), scale=ap(scale), accum_out=ap(acc)),
+           [in_, bias, scale], [out] + ([acc] if acc else []), ACALL + CYC * in_["n"] * (GATHER if "off" in in_ else 1))
+
+    def mm(out, lhsT, rhs, start, stop):
+        op("p", lambda e: e.matmul(out["ap"], lhsT["ap"], rhs["ap"], start, stop), [lhsT, rhs], [out],
+           PCYC * max(min(64, lhsT["n"]), rhs["n"]) * (4 if lhsT["f32"] else 1))
+        if start:
+            group[out["name"]] = ([], [False])
+        members, long = group[out["name"]]
+        long[0] = long[0] or bool(members) and ops[members[0]]["tag"] != now[1]
+        note(lat=60, group=members, long=long, dep=(list(members) if stop else members[:1]))
+        members.append(len(ops) - 1)
+
+    def iota(out, pat, base, mult, flag=True):
+        if flag:
+            op("g", lambda e: e.iota(out["ap"], pat, base, mult, allow_small_or_imprecise_dtypes=True), [], [out], 200 + 2 * CYC * out["n"])
+        else:
+            op("g", lambda e: e.iota(out["ap"], pat, base, mult), [], [out], 200 + 2 * CYC * out["n"])
+        ops[-1]["w"].append(POOL)
+
+    def mark(out, pat, base, mult, value, src=None, keep=A.not_equal):
+        src = src or out
+        op("g", lambda e: e.affine_select(out["ap"], src["ap"], pat, keep, value, base, mult), [src], [out], 200 + 2 * CYC * out["n"])
+        ops[-1]["w"].append(POOL)
+
+    LCH = len(IN) - 1
+    for c in range(LCH):
+        dma("s", S("PK", IN[c], IN[c + 1]), S("fld", IN[c], IN[c + 1]), 4)
+        if c == CFG["WAT"]:
+            dma("s", S("WI"), S("wnd"), 4)
+    dma("s", S("REC", 0, V), S("rec"), 2)
+    dma("s", S("REC", V, 2 * V), S("rec"), 2)
+    lat[0] = 0
+
+    iota(S("CP", 0, 1), [[1, 1]], 0, 1, False)
+    iota(S("RD"), [[1, 128]], 0, -1)
+    iota(S("RK"), [[0, 8], [1, 16]], 0, 0)
+    iota(S("RG"), [[1, 8], [0, 16]], 0, 0)
+    if any(c[3] == "a" for c in PC):
+        iota(S("SKF"), [[0, 2048]], 1, 0)
+        mark(S("SKF"), [[-256, 16], [-16, 8], [255, 16]], 0, 1, 0.0, keep=A.is_equal)
+    iota(S("KC", 0, 256, p=(32, 64)), [[0, 16], [8192, 16]], 0, 0)
+    iota(S("KC", 256, 384, p=(32, 64)), [[0, 8], [64, 16]], 2112, 0)
+    iota(S("KC", 0, 128, p=(0, 32)), [[0, 128]], -120 * 131072, 0)
+    iota(S("KC", 128, 384, p=(0, 32)), [[0, 256]], 120 * 131072, 0)
+    fill(S("ZR"), 0.0)
+    mark(S("SC"), [[0, 24], [1, 16]], 0, 0, 1.0e8, S("ZR", 0, 384))
+    every, top = [[-32, 4], [-1, 8], [0, 16]], [[-32, 4], [-1, 8], [-256, 16]]
+    mark(S("XN"), every, 0, 1, 2.0 ** -11, S("ZR"))
+    for j in range(2):
+        mark(S("CM%d" % j), [[-2, 5], [-32, 16], [300, 2]], -6 - j, 1, 2.0 ** -13, S("ZR", 0, 160))
+        iota(S("CS%d" % j, 0, 128), [[0, 128]], 0, 0)
+    mark(S("HM"), [[0, 8], [1, 16]], 0, 0, 1.0, S("ZR", 0, 128), A.is_equal)
+    mark(S("XK"), every, -16, 1, 2.0 ** -6, S("ZR"))
+    mark(S("XC"), every, -8, 1, 2.0 ** -14, S("ZR"))
+    for name, wt in (("XH", -0.5), ("XA", 0.5)):
+        mark(S(name), top, 0, 1, 0.5, S("ZR"))
+        mark(S(name), top, -24, 1, wt)
+    iota(S("FW", V), [[0, 96]], 0, 0)
+    mark(S("PM"), [[0, 16], [1, 16]], 0, 0, -2.0 ** 98, S("ZR", 0, 256), A.is_equal)
+    mark(S("PM"), [[0, 16], [1, 16]], 0, 0, 2.0 ** 98)
+    fill(S("O32"), 1.0 / 32)
+    bits = [(0, 15), (4, 7), (0, 1)]
+    for j, (sh, m) in enumerate(bits):
+        ts(S("CI", j, j + 1), S("CP", 0, 1), sh, A.logical_shift_right, m, A.bitwise_and)
+    cp(S("CF", 0, 3), S("CI", 0, 3))
+    c16, cG, cO = [S("CF", j, j + 1) for j in range(3)]
+    ident = S("I")
+    ts(ident, S("RD"), 0.0, A.is_equal)
+    ts(S("MK"), S("RK", 0, 16), c16, A.is_equal)
+    nc = [0]
+
+    def col(in0, s1, s2, o0=A.mult, o1=A.add):
+        nc[0] += 1
+        ts(S("CC", nc[0] - 1, nc[0]), in0, s1, o0, s2, o1)
+        return S("CC", nc[0] - 1, nc[0])
+
+    def eqm(name, row, c, wt):
+        ts(S(name), row, c, A.is_equal, wt, A.mult)
+
+    even = col(cO, -1.0, 1.0)
+    eqm("SH", S("RD"), 1.0, even)
+    for k in range(16):
+        act(S("SK", 128 * k, 128 * k + 128), ident, F.Identity, scale=S("MK", k, k + 1))
+    ts(S("NSH"), S("SH"), -2.0 ** -11, A.mult)
+    ts(S("I16"), ident, 1.0 / 16, A.mult)
+    not15 = col(S("MK", 15, 16), -0.5, 0.5)
+    a15 = col(c16, -2.0, 15.0)
+    odd_w = col(c16, 2.0, 1.0)
+    dummy = [col(c16, 1.0, float(V)), col(c16, 1.0, float(V + 16))]
+    kbias = col(c16, -8192.0, -33 * 8192.0)
+    eu_add = col(cO, 2048.0, 2048.0)
+    odd_tiny = col(cO, 2.0 ** -12, 0.0)
+    ms_add = col(c16, 2 * AL, -AL)
+    ts(S("B8"), S("RK", 0, 8), cG, A.is_equal)
+    ts(S("MS0"), S("RK", 0, 128), -2 * AL, A.mult, ms_add, A.add)
+    ts(S("MSK", 0, 128), S("MS0"), AL, A.min, -3 * AL, A.max)
+    fill(S("MSK", 128, 144), 3 * AL)
+    fill(S("MSK", 144, 256), AL)
+    eqm("MVH", S("RD"), 1.0, not15)
+    eqm("TBH", S("RD"), a15, not15)
+    eqm("BO", S("RG", 0, 128), cG, 1.0 / 32)
+    tt(S("HDM"), S("MVH"), S("TBH"), A.subtract)
+    tt(S("AVM"), S("MVH"), S("TBH"), A.add)
+    fill(S("THR"), -4.5)
+
+    for c in range(LCH):
+        a, b = IN[c], IN[c + 1]
+        hj = B(2 + c, 0, b - a)
+        if c in UNP:
+            step("Ua%d" % c)
+            ts(S("YO", a, b), S("PK", a, b), -2.0 ** 23, A.add, -2047.5, A.add)
+            act(S("YO", a, b), S("YO", a, b), F.Identity, bias=MAG / 2)
+            step("Ub%d" % c)
+            act(hj, S("YO", a, b), F.Identity, bias=2.0 ** 23 - MAG / 2)
+        else:
+            step("Ua%d" % c)
+            ts(S("HI", a, b), S("PK", a, b), 12, A.logical_shift_right)
+            step("Ub%d" % c)
+            ts(hj, S("HI", a, b), float(V), A.mult)
+        step("Uc%d" % c)
+        tt(S("FW", a, b), S("PK", a, b), hj, A.subtract)
+        if c in UNP:
+            act(S("FW", H + a, H + b), S("YO", a, b), F.Identity, scale=1.0 / V, bias=(2.0 ** 23 - MAG / 2) / V)
+        else:
+            act(S("FW", H + a, H + b), hj, F.Identity, scale=1.0 / V)
+    step("UW")
+    cp(S("WU"), S("WI"))
+    step("UH")
+    ts(S("WH0"), S("WU"), -2048.0, A.add)
+    step(None)
+
+    act(S("O32F"), S("O32"), F.Identity, scale=0.5)
+    for name, wt in (("NI", -1.0), ("NI2", -0.5), ("WIM", -AL), ("I2K", 2048.0), ("NIU", -2.0 ** -11)):
+        act(S(name), ident, F.Identity, scale=wt)
+    act(S("PSH"), S("SH"), F.Identity, scale=2.0 ** -11)
+    for h in range(2):
+        if KD[h] > 6:
+            for j in range(3):
+                act(S("BNW", 384 * h + 128 * j, 384 * h + 128 * j + 128), S("BO"), F.Identity, scale=(-1 if j == 0 else 1) * 32 * 131072.0)
+            if KD[h] < 16:
+                mark(S("BNW", 384 * h, 384 * h + 384), [[0, 24], [-1, 16]], KD[h] - 1, 0, 0.0, keep=A.is_ge)
+    for name, wt in (("BP1", 131072.0), ("BP2", 262144.0), ("BN", -131072.0)):
+        for j in range(3):
+            act(S(name, 8 * j, 8 * j + 8), S("B8"), F.Identity, scale=(wt if j == 0 else -wt))
+    act(S("WT8"), S("B8"), F.Identity, scale=odd_w)
+
+    for t in range(NV):
+        last = t == NV - 1
+        wh, WR = "WH%d" % t, CFG["WR" if t else "WR0"]
+        now[0] = t
+
+        def proposals(c):
+            w0, m, bk, q = PC[c]
+            e = B(bk, w0, w0 + m)
+            if q == "a":
+                step("GA%d" % c)
+                gf = 1024 * ([j for j in range(len(PC)) if PC[j][3] == "a"].index(c) % 2)
+                act(S("GF", gf, gf + 16 * m), IND(S("FW", 0, V), S("WU", w0, w0 + m)), F.Identity, bias=-1.0, scale=2.0 ** -11)
+            else:
+                for w in range(w0, w0 + m, CFG["GW"]):
+                    w1 = min(w + CFG["GW"], w0 + m)
+                    step("G%d%s" % (c, "abcd"[(w - w0) // CFG["GW"]]))
+                    ts(S("G1", 16 * w, 16 * w1), IND(S("FW", 0, V), S("WU", w, w1)), -2048.0, A.add, 2.0 ** -11, A.mult)
+            step("P%d" % c)
+            mm(e, S("NSH"), S(wh, w0, w0 + m), True, False)
+            for k in range(16):
+                if q == "a":
+                    step("P%d%s" % (c, "abcd"[k // 4]))
+                    mm(e, S("SKF", 128 * k, 128 * k + 128), S("GF", gf + k, gf + 16 * m, 16), False, k == 15)
+                else:
+                    mm(e, S("SK", 128 * k, 128 * k + 128), S("G1", 16 * w0 + k, 16 * (w0 + m), 16), False, k == 15)
+            step("N%d" % c)
+            if t:
+                ts(S("EU", w0, w0 + m), e, 2048.0, A.mult, eu_add, A.add)
+
+        def wrap(c):
+            w0, m, bk = WR[c]
+            step(("ET%d" if t else "IT%d") % c)
+            act(S("ET", w0, w0 + m), B(bk, w0, w0 + m), F.Sign, bias=odd_tiny, scale=cO)
+            step(("EH%d" if t else "IH%d") % c)
+            tt(S("EH", w0, w0 + m), B(bk, w0, w0 + m), S("ET", w0, w0 + m), A.subtract)
+            if not t:
+                step("IN%d" % c)
+                ts(S("EU", w0, w0 + m), S("EH", w0, w0 + m), 2048.0, A.mult, 2048.0, A.add)
+
+        def gather_x(j):
+            step(("X%d" if t or j not in CFG["XV0"] else "IX%d") % j)
+            src = IND(S("REC", 0, 2 * V if t else V), S("EU", 32 * j, 32 * j + 32))
+            if j in (XV if t else CFG["XV0"]):
+                ts(S("X", 512 * j, 512 * j + 512), src, 192.0, A.add)
+            else:
+                act(S("X", 512 * j, 512 * j + 512), src, F.Identity, bias=192.0)
+
+        def sums(s):
+            step("S%d" % s)
+            bk, o = 2 + s // 2, 64 * (s % 2)
+            for k in range(16):
+                mm(B(bk, o, o + 64), S("I16"), S("X", 1024 * s + k, 1024 * (s + 1), 16), k == 0, k == 15)
+
+        def xk(h, k):
+            return S("X", H * h + k, H * (h + 1), 16)
+
+        def mb(h):
+            return S("MB", 128 * h, 128 * h + 128)
+
+        def ad(h, k):
+            return S("AD", H * h + 128 * k, H * h + 128 * k + 128)
+
+        def distances(h):
+            kb, kv = 4 + h, KD[h]
+            step("K%d" % h)
+            mm(B(kb, 0, 384), S("O32", p=(0, 64)), S("KC", p=(0, 64)), True, False)
+            step("KX%d" % h)
+            for k in range(kv):
+                mm(B(kb, k, 384, 16), xk(h, k), S("BN"), False, False)
+            step("M%d" % h)
+            if CFG["MEAN"][h] == "v":
+                ts(mb(h), B(2 + h, 0, 128), -0.46875, A.add)
+            else:
+                act(mb(h), B(2 + h, 0, 128), F.Identity, bias=-0.46875)
+            step("MP%d" % h)
+            if kv:
+                mm(B(2 + h, 128, 256), ident, mb(h), True, True)
+            step("EM%d" % h)
+            if kv > 6:
+                mm(B(kb, 0, 384), mb(h), S("BNW", 384 * h, 384 * h + 384), False, False)
+            for k in range(kv if kv <= 6 else 0):
+                mm(B(kb, k, 384, 16), mb(h), S("BN"), False, False)
+            for k in range(kv):
+                step("V%d%s" % (h, "abcdefghijklmnop"[k // VG]))
+                tt(ad(h, k), xk(h, k), B(2 + h, 128, 256), A.max)
+            for k in range(kv):
+                step("EV%d%s" % (h, "abcdefghijklmnop"[k // VG]))
+                mm(B(kb, k, 384, 16), ad(h, k), S("BP2"), False, False)
+            for i, k0 in enumerate(range(kv, 16, 4)):
+                ks, bk, c = list(range(k0, min(16, k0 + 4))), 7 - (i & 1), "abcd"[i]
+                step("DX%d%s" % (h, c))
+                for j, k in enumerate(ks):
+                    mm(B(bk, 128 * j, 128 * j + 128), ident, xk(h, k), j == 0, False)
+                step("DM%d%s" % (h, c))
+                for j, k in enumerate(ks):
+                    mm(B(bk, 128 * j, 128 * j + 128), S("NI"), mb(h), False, j == len(ks) - 1)
+                step("B%d%s" % (h, c))
+                act(S("AD", H * h + 128 * k0, H * h + 128 * (ks[-1] + 1)), B(bk, 0, 128 * len(ks)), F.Abs)
+                step("EB%d%s" % (h, c))
+                for k in ks:
+                    mm(B(kb, k, 384, 16), ad(h, k), S("BP1"), False, False)
+            step("R%d" % h)
+            mm(B(kb, 0, 128), S("EH", 128 * h, 128 * h + 128), S("I2K"), False, False)
+            mm(B(kb, 128, 256), S(wh, 128 * h, 128 * h + 128), ident, False, True)
+            step("SC%d" % h)
+            scan(S("KF", 512 * h, 512 * h + 384), S("SC"), B(kb, 0, 384), 0.0, A.add, A.min)
+
+        def threshold():
+            step("TM")
+            x = B(CFG["TH"][0], CFG["TH"][1], CFG["TH"][1] + 1)
+            for j in range(2):
+                mm(x, S("O32F"), S("ACC", j, j + 1), j == 0, j == 1)
+            step("TA")
+            act(S("TA", 0, 1), x, F.Identity, bias=1.5 * 2.0 ** 23)
+            step("TB")
+            act(S("TA", 1, 2), S("TA", 0, 1), F.Identity, scale=-1.0, bias=1.5 * 2.0 ** 23)
+            step("TC")
+            act(S("TA", 2, 3), x, F.Abs, bias=S("TA", 1, 2))
+            step("TD")
+            act(S("THR", 0, 1), S("TA", 2, 3), F.Identity, scale=-2.0, bias=-4.5)
+
+        def choose(h):
+            tb, w0, s0, b0, cs = CFG["TB"][h], 128 * h, 32 * h, 8 * h, "CS%d" % h
+
+            def row(name):
+                return S(name, w0, w0 + 128)
+
+            def bank(name, a=0, b=128):
+                return B(tb[name][0], tb[name][1] + a, tb[name][1] + b)
+
+            def tag(s):
+                step("%s%d" % (s, h))
+
+            def expand(to, name, start, stop, at=0, shift=0):
+                for a in range(4):
+                    o, m = at + 32 * a + shift, 32 - (shift if a == 3 else 0)
+                    mm(bank(to, o, o + m), S(name, 128 * a, 128 * a + 128), S("PT", s0, s0 + m), start and a == 0, stop and a == 3)
+
+            tag("ZM")
+            mm(bank("zz", 0, 8), mb(h), S("WT8"), True, True)
+            tag("SQ")
+            act(S("SQ", b0, b0 + 8), bank("zz", 0, 8), F.Square, bias=-48560.0)
+            tag("ZI")
+            ts(S("ZI", b0, b0 + 8), S("SQ", b0, b0 + 8), 1.0 / 32, A.mult, -10952.375, A.add)
+            tag("ZA")
+            ts(S("ZA", b0, b0 + 8), S("ZI", b0, b0 + 8), V - 1, A.bitwise_and)
+            tag("ZP")
+            ts(S("P16", s0 + 24, s0 + 32), S("ZA", b0, b0 + 8), -2048.0, A.add)
+            keys = S("KF", 512 * h + 15, 512 * h + 384, 16)
+            tag("RQ")
+            ts(S("RQ", s0, s0 + 24), keys, MAG, A.add, -MAG, A.add)
+            tag("PP")
+            tt(S("P16", s0, s0 + 24), keys, S("RQ", s0, s0 + 24), A.subtract)
+            tag("QS")
+            tt(S("QS", b0, b0 + 8), S("RQ", s0, s0 + 8), S("KF", 512 * h + 271, 512 * h + 384, 16), A.add)
+            tag("MX")
+            tt(S("P16", s0 + 8, s0 + 16), S("P16", s0 + 8, s0 + 16), S("QS", b0, b0 + 8), A.max)
+            tag("PT")
+            turn(S("PT", s0, s0 + 32), S("P16", s0, s0 + 32))
+            tag("QB")
+            expand("eq", "XN", True, True)
+            tag("EQ")
+            tt(row("EQ"), row("EH"), bank("eq"), A.is_equal)
+            tag("CM")
+            for j in range(4):
+                g2, b1 = j // 2, j % 2
+                mm(bank("cc", 16 * g2, 16 * g2 + 16), S("CM%d" % g2, 32 - b1, 160 - b1), S("PT", s0 + 16 * b1, s0 + 16 * b1 + 16), j == 0, j == 3)
+            tag("CS")
+            turn(S(cs, 0, 512, 16), bank("cc", 0, 32))
+            tag("BO")
+            mm(bank("vo"), S("BO"), row("EQ"), True, True)
+            tag("GO")
+            act(row("GO"), bank("vo"), F.Sign, bias=S("THR", 0, 1), scale=32.0, acc=(None if last else S("ACC", h, h + 1)))
+            tag("RR")
+            scan(row("RR"), S("HM", 0, 128), S(cs, 0, 128), 0.0, A.mult, A.add)
+            tag("OC")
+            ts(S("OC", b0, b0 + 8), S(cs, 0, 128, 16), 8192.0, A.mult, 2048.0, A.add)
+            tag("KM")
+            expand("kk", "XK", True, True)
+            tag("U")
+            act(row("U"), bank("kk"), F.Abs, bias=kbias, scale=8192.0)
+            tag("SA")
+            mm(bank("va"), S("PSH"), row(wh), True, False)
+            tag("SB")
+            expand("va", "XN", False, True)
+            tag("SG")
+            act(row("SG"), bank("va"), F.Sign, bias=odd_tiny, scale=cO)
+            tag("DA")
+            mm(bank("df"), S("HDM"), row(wh), True, False)
+            tag("DB")
+            expand("df", "XH", False, True)
+            tag("PD")
+            tt(row("PRD"), row("GO"), bank("df"), A.mult)
+            tag("AA")
+            mm(bank("av"), S("AVM"), row(wh), True, False)
+            tag("AB")
+            expand("av", "XA", False, True)
+            tag("WO")
+            if last:
+                tt(row("WF"), row("PRD"), bank("av"), A.add)
+                tag("WG")
+                act(row("WG"), row("WF"), F.Identity, bias=2048.0)
+                dma("a", row("yw"), row("WG"), 4)
+            else:
+                src, dst, sem = row("WO%d" % t), row("WH%d" % (t + 1)), "arr%d_%d" % (t + 1, h)
+                tt(src, row("PRD"), bank("av"), A.add)
+                tag("TO")
+                op("g", lambda e: e.remote_dma(dst["ap"], src["ap"], T.sem[sem], T.sem.sent, pid, rid, mask_out), [src], [], 100)
+                note(line="ring%d" % h)
+            tag("OM")
+            tt(row("OM"), IND(S("FW"), S("OC", b0, b0 + 8)), row("U"), A.min)
+            tag("LA")
+            mm(bank("ls"), S("PSH"), row(wh), True, False)
+            tag("LB")
+            expand("ls", "XN", False, False)
+            tag("LC")
+            mm(bank("ls"), S("NI"), row("SG"), False, False)
+            tag("LD")
+            mm(bank("ls"), S("NIU"), row("U"), False, True)
+            tag("LS")
+            act(row("LS"), bank("ls"), F.Identity, bias=2048.0, scale=2048.0)
+            tag("PA")
+            mm(bank("pr", 0, 256), ident, S("MSK"), True, False)
+            tag("PB")
+            expand("pr", "XC", False, False)
+            expand("pr", "XC", False, False, 128, 16)
+            tag("PC")
+            mm(bank("pr"), S("NI2"), row("RR"), False, False)
+            mm(bank("pr", 128, 256), S("NI2"), row("RR"), False, False)
+            tag("PW")
+            mm(bank("pr", 144, 256), S("WIM"), S("GO", w0, w0 + 112), False, False)
+            mm(bank("pr"), S("WIM"), row("GO"), False, True)
+            tag("PS")
+            scan(S("PS", 2 * w0, 2 * w0 + 256), S("PM"), bank("pr", 0, 256), 1.0, A.max, A.mult)
+            tag("LO")
+            ts(S("LO", 2 * b0, 2 * b0 + 16), S("PS", 2 * w0 + 15, 2 * w0 + 256, 16), 0.0, A.is_equal, 0.125, A.add)
+            tag("KA")
+            tt(S("K3", b0, b0 + 8), S("LO", 2 * b0, 2 * b0 + 8), S("LO", 2 * b0 + 8, 2 * b0 + 16), A.add)
+            tag("KB")
+            tt(S("K4", b0, b0 + 8), S("K3", b0, b0 + 8), S(cs, 0, 128, 16), A.add)
+            tag("OF")
+            for j in range(2):
+                ts(S("OFF", b0 + j, b0 + 8, 2), S("K4", b0 + j, b0 + 8, 2), 8192.0, A.mult, dummy[j], A.min)
+
+        def arrive(h):
+            sem, nx = "arr%d_%d" % (t + 1, h), S("WH%d" % (t + 1), 128 * h, 128 * h + 128)
+            step("WU%d" % h)
+            op("v", None, [], [nx], 0)
+            note(src=sem, sem=sem, val=n_in, line="ring%d" % h)
+            ts(S("WU", 128 * h, 128 * h + 128), nx, 2048.0, A.add)
+
+        if t:
+            threshold()
+        for h in (1, 0):
+            for c in range(len(PC)):
+                if PC[c][0] // 128 == h:
+                    proposals(c)
+            for c in range(len(WR)):
+                if WR[c][0] // 128 == h:
+                    wrap(c)
+            for j in range(4 * h + 3, 4 * h - 1, -1):
+                gather_x(j)
+            sums(2 * h + 1)
+            sums(2 * h)
+        for h in (1, 0):
+            distances(h)
+            choose(h)
+        if not last:
+            for h in (1, 0):
+                arrive(h)
+        for b in range(7, -1, -1):
+            step("F%d" % b)
+            tt(IND(S("FW"), S("OFF", 2 * b, 2 * b + 2)), S("OM", 32 * b, 32 * b + 32), S("LS", 32 * b, 32 * b + 32), A.max)
+
+    now[0], now[1] = NV, "end"
+    lat[0] = 0
+    for c in range(len(OUT) - 1):
+        a, b = OUT[c], OUT[c + 1]
+        act(B(2 + c, 0, b - a), S("FW", H + a, H + b), F.Identity, scale=float(V))
+        tt(S("YO", a, b), S("FW", a, b), B(2 + c, 0, b - a), A.add)
+        dma("s", S("yf", a, b), S("YO", a, b), 4)
+        note(t=60 + 128 * 4 * (b - a) / DMARATE, lat=DMA0)
+    op("s", None, [S("yw"), S("yf")], [], 0)
+    note(src="end")
+    depend(ops)
+    return ops
 
 
 def rank_program(g, core, T, topo):
@@ -220,489 +757,8 @@ def rank_program(g, core, T, topo):
     n = len(T.cores)
     nxt, prv = T.cores[(rank + 1) % n], T.cores[(rank - 1) % n]
     rid, pid, _ = topo.addr(nxt)
-    mask_out, n_out, n_in = topo.mask(core, nxt), len(topo.engines(core, nxt)), len(topo.engines(prv, core))
-    ops, nd, lat, now = [], [0], [0], [-1, None]
-    B = [T["B%d" % b] for b in range(8)]
-
-    def op(q, fn, r=(), w=(), b=()):
-        tm = TIME.get(w[0].rstrip("0123456789_"), 90) if w else 90
-        ops.append({"q": q, "src": q, "fn": fn, "r": list(r), "w": list(w), "b": list(b), "sig": False, "sem": None, "val": 0, "inc": 0,
-                    "k": "r", "t": tm, "lat": 0, "visit": now[0],
-                    "tag": now[1] or (w[0].rstrip("0123456789") if w else "%s%d" % (r[0].rstrip("0123456789"), b[0] if b else 0))})
-
-    def note(**kw):
-        ops[-1].update(kw)
-
-    def dma(q, out, in_, r=(), w=()):
-        s = "d%d" % nd[0]
-        nd[0] += 1
-        op(q, lambda e: e.dma_start(out, in_), r, w)
-        big = w[0][:2] != "PK"
-        lat[0] += ops[-1]["t"] * big
-        note(src=s, sem=s, val=16, inc=16, t=50, lat=2000 + lat[0] + (0 if big else 1000), line="dma" + q)
-
-    def ts(out, in0, s1, op0, s2=None, op1=None, r=(), w=(), b=()):
-        if op1 is None:
-            op("v", lambda e: e.tensor_scalar(out, in0, s1, None, op0), r, w, b)
-        else:
-            op("v", lambda e: e.tensor_scalar(out, in0, s1, s2, op0, op1), r, w, b)
-
-    def tt(out, in0, in1, o, r=(), w=(), b=()):
-        op("v", lambda e: e.tensor_tensor(out, in0, in1, o), r, w, b)
-
-    def cp(out, in_, r=(), w=(), b=()):
-        op("v", lambda e: e.tensor_copy(out, in_), r, w, b)
-
-    def fill(out, c, w=(), b=()):
-        op("v", lambda e: e.memset(out, c), (), w, b)
-
-    def act(out, in_, f, bias=0.0, scale=1.0, acc=None, r=(), w=(), b=()):
-        op("a", lambda e: e.activation(out, in_, f, bias=bias, scale=scale, accum_out=acc), r, w, b)
-
-    def mm(bk, out, lhsT, rhs, start, stop, r=()):
-        op("p", lambda e: e.matmul(out, lhsT, rhs, start, stop), r, (), [bk])
-        note(k="w" if start or stop else "add", t=max(TMM.get(x, 34) for x in r), lat=60)
-
-    def scan(out, d0, d1, init, o0, o1, r=(), w=(), b=()):
-        op("v", lambda e: e.tensor_tensor_scan(out, d0, d1, init, o0, o1), r, w, b)
-
-    def iota(out, pat, base, mult, w, flag=True):
-        if flag:
-            op("g", lambda e: e.iota(out, pat, base, mult, allow_small_or_imprecise_dtypes=True), ["pool"], w + ["pool"])
-        else:
-            op("g", lambda e: e.iota(out, pat, base, mult), ["pool"], w + ["pool"])
-
-    LCH = len(IN) - 1
-    for c in range(LCH):
-        dma("s", T.PK[:, IN[c]:IN[c + 1]], T.fld[:, IN[c]:IN[c + 1]], w=["PK%d" % c])
-        lat[0] += 2.55 * (IN[c + 1] - IN[c])
-        if c == 1:
-            dma("a", T.WI[:], T.wnd[:], w=["WI"])
-    dma("s", T.REC[:, 0:V], T.rec[:], w=["REC"])
-    dma("s", T.REC[:, V:2 * V], T.rec[:], w=["REC2"])
-    lat[0] = 0
-
-    iota(T.CP[:, 0:1], [[1, 1]], 0, 1, ["CP"], False)
-    iota(T.RD[:], [[1, 128]], 0, -1, ["RD"])
-    iota(T.RM[:], [[1, 240]], 0, 0, ["RM"])
-    iota(T.RG[:], [[1, 8], [0, 16]], 0, 0, ["RG"])
-    iota(T.RK[:], [[0, 24], [1, 16]], 0, 0, ["RK"])
-    iota(T.FW[:, V:V + 32], [[0, 32]], 0, 0, ["FWd"])
-    iota(T.SKF[:], [[0, 2048]], 1, 0, ["SKF"])
-    note(t=4300)
-    op("g", lambda e: e.affine_select(T.SKF[:], T.SKF[:], [[-256, 16], [-16, 8], [255, 16]], A.is_equal, 0.0, 0, 1),
-       ["SKF", "pool"], ["SKF", "pool"])
-    note(t=4300)
-    iota(T.KC[32:64, :], [[0, 24], [8192, 16]], 0, 0, ["KCb"])
-    iota(T.KC[64:96, 256:384], [[0, 64], [2048, 2]], -2048, 0, ["KCc"])
-    iota(T.KC[0:32, 0:128], [[0, 128]], -120 * 131072, 0, ["KCa0"])
-    iota(T.KC[0:32, 128:384], [[0, 256]], 120 * 131072, 0, ["KCa1"])
-    iota(T.KC[64:96, 0:256], [[0, 256]], 0, 0, ["KCd"])
-    iota(T.DC[:], [[0, 256]], 512, 0, ["DC"])
-    iota(T.PY[:, 64:72], [[0, 8]], 0, 0, ["PY0"])
-    p = T.CP[:, 0:1]
-    fill(T.O32[:], 1.0 / 32, ["O32"])
-    bits = [(0, 15), (4, 7), (0, 7), (3, 3), (0, 1), (3, 1), (5, 3)]
-    for j, (sh, m) in enumerate(bits):
-        ts(T.CI[:, j:j + 1], p, sh, A.logical_shift_right, m, A.bitwise_and, r=["CP"], w=["CI%d" % j])
-    cp(T.CF[:, 0:7], T.CI[:, 0:7], r=["CI%d" % j for j in range(7)], w=["CF"])
-    c16, cG, c8, cQ, cO, cH, cB = [T.CF[:, j:j + 1] for j in range(7)]
-    ident = T.ISH[:, 0:128]
-    ts(ident, T.RD[:], 0.0, A.is_equal, r=["RD"], w=["I"])
-    ts(T.MK[:], T.RM[:, 0:16], c16, A.is_equal, r=["RM", "CF"], w=["MK"])
-    ts(T.QM[:], T.RM[:, 0:4], cQ, A.is_equal, r=["RM", "CF"], w=["QM"])
-    nc = [0]
-
-    def col(in0, s1, s2, r=("CF",)):
-        j = nc[0]
-        nc[0] += 1
-        ts(T.CC[:, j:j + 1], in0, s1, A.mult, s2, A.add, r=r, w=["CC%d" % j])
-        return T.CC[:, j:j + 1], "CC%d" % j
-
-    def col2(a, b_, o, r):
-        j = nc[0]
-        nc[0] += 1
-        tt(T.CC[:, j:j + 1], a, b_, o, r=r, w=["CC%d" % j])
-        return T.CC[:, j:j + 1], "CC%d" % j
-
-    def eqm(name, out, row, rrow, c, wt):
-        ts(out, row, c[0] if isinstance(c, tuple) else c, A.is_equal, wt[0] if isinstance(wt, tuple) else wt, A.mult,
-           r=[rrow] + [x[1] for x in (c, wt) if isinstance(x, tuple)], w=[name])
-
-    even = col(cO, -1.0, 1.0)
-    not15 = col(T.MK[:, 15:16], -0.5, 0.5, r=["MK"])
-    eqm("SH", T.ISH[:, 128:256], T.RD[:], "RD", 1.0, even)
-    for k in range(16):
-        act(T.SK[:, 128 * k:128 * k + 128], ident, F.Identity, scale=T.MK[:, k:k + 1], r=["I", "MK"], w=["SK%d" % k])
-    ts(T.DO[:], ident, cO, A.mult, 65536.0, A.mult, r=["I", "CF"], w=["DO"])
-    ts(T.NSH[:], T.ISH[:, 128:256], -1.0, A.mult, r=["SH"], w=["NSH"])
-    ts(T.I16[:], ident, 1.0 / 16, A.mult, r=["I"], w=["I16"])
-    a15 = col(c16, -2.0, 15.0)
-    odd_w = col(c16, 2.0, 1.0)
-    c8x = col(c8, 16.0, 0.0)
-    c112 = col(c16, 1.0, 112.0)
-    dummy = [col(c16, 1.0, float(V)), col(c16, 1.0, float(V + 16))]
-    kbias = col(c16, -8192.0, 0.0)
-    ybase = col(cH, 32.0, -56.0)
-    q0n = col(T.QM[:, 0:1], -1.0, 0.0, r=["QM"])
-    q1s = col(T.QM[:, 1:2], 2.0 ** -14, 0.0, r=["QM"])
-    ymask = col2(c8, cG, A.is_equal, ["CF"])
-    q02 = col2(T.QM[:, 0:1], T.QM[:, 2:3], A.add, ["QM"])
-    qh = col2(T.QM[:, 0:1], T.QM[:, 3:4], A.subtract, ["QM"])
-    qa = col2(T.QM[:, 0:1], T.QM[:, 3:4], A.add, ["QM"])
-    ts(T.B8[:], T.RM[:, 0:8], cG, A.is_equal, r=["RM", "CF"], w=["B8"])
-    ts(T.WH0[:], T.WI[:], -2048.0, A.add, r=["WI"], w=["WH0"])
-    cp(T.WU[:], T.WI[:], r=["WI"], w=["WU"])
-    ts(T.HM[:], T.RK[:], 0.0, A.not_equal, r=["RK"], w=["HM"])
-    ts(T.MS0[:], T.RK[:, 0:256], c16, A.is_ge, 0.375, A.mult, r=["RK", "CF"], w=["MS0"])
-    eqm("MVH", T.MVH[:], T.RD[:], "RD", 1.0, not15)
-    eqm("TBH", T.TBH[:], T.RD[:], "RD", a15, not15)
-    eqm("BO", T.BO[:], T.RG[:], "RG", (cG, "CF"), 1.0 / 32)
-    eqm("XN", T.XN[:, 0:128], T.RG[:], "RG", (c8, "CF"), q0n)
-    eqm("XL", T.XL[:, 0:128], T.RG[:], "RG", (c8, "CF"), q02)
-    eqm("XC", T.XC[:, 0:128], T.RG[:], "RG", (c8, "CF"), q1s)
-    eqm("XH", T.XH[:, 0:128], T.RM[:, 0:128], "RM", c8x, qh)
-    eqm("XA", T.XA[:, 0:128], T.RM[:, 0:128], "RM", c8x, qa)
-    ts(T.BM[:], T.RM[:, 0:4], cB, A.is_equal, r=["RM", "CF"], w=["BM"])
-    ts(T.CC[:, 28:32], T.BM[:], 0.5, A.mult, r=["BM"], w=["BH"])
-    for name in ("XN", "XH", "XA", "XC", "XL"):
-        half = name in ("XH", "XA")
-        for a in range(4):
-            ts(T[name][:, 128 * a + 128:128 * a + 256], T[name][:, 0:128], (T.CC[:, 28 + a:29 + a] if half else T.BM[:, a:a + 1]), A.mult,
-               r=[name, "BH" if half else "BM"], w=[name + str(a)])
-            if a < XACT:
-                src, sc, out = T[name][:, 0:128], (T.CC[:, 28 + a:29 + a] if half else T.BM[:, a:a + 1]), T[name][:, 128 * a + 128:128 * a + 256]
-                note(q="a", src="a", t=170, fn=lambda e, out=out, src=src, sc=sc: e.activation(out, src, F.Identity, scale=sc))
-    eqm("CW", T.CW[:], T.RM[:], "RM", c112, 2.0 ** -13)
-    ts(T.YF0[:], T.RM[:, 0:8], ybase[0], A.add, ymask[0], A.mult, r=["RM", ybase[1], ymask[1]], w=["YF0"])
-    tt(T.HDM[:], T.MVH[:], T.TBH[:], A.subtract, r=["MVH", "TBH"], w=["HDM"])
-    tt(T.AVM[:], T.MVH[:], T.TBH[:], A.add, r=["MVH", "TBH"], w=["AVM"])
-    ts(T.YOF[:], T.YF0[:], 64.0, A.add, r=["YF0"], w=["YOF"])
-    fill(T.Q16[:, 64:128], 0.0, ["Q0"])
-    fill(T.THR[:], -4.5, ["THR"])
-    fill(B[0][:, 256:512], 0.0, ["Z0"], [0])
-    note(k="w")
-
-    for c in range(LCH):
-        sl, lw, first = slice(IN[c], IN[c + 1]), IN[c + 1] - IN[c], len(ops)
-        if c in UNP:
-            ts(T.YO[:, sl], T.PK[:, sl], -2.0 ** 23, A.add, -2047.5, A.add, r=["PK%d" % c], w=["YO%d" % c])
-            act(T.YO[:, sl], T.YO[:, sl], F.Identity, bias=MAG / 2, r=["YO%d" % c], w=["YO%d" % c])
-            act(B[2 + c][:, 0:lw], T.YO[:, sl], F.Identity, bias=2.0 ** 23 - MAG / 2, r=["YO%d" % c], w=["HJ%d" % c], b=[2 + c])
-        else:
-            ts(T.HI[:, sl], T.PK[:, sl], 12, A.logical_shift_right, r=["PK%d" % c], w=["HI%d" % c])
-            ts(B[2 + c][:, 0:lw], T.HI[:, sl], float(V), A.mult, r=["HI%d" % c], w=["HJ%d" % c], b=[2 + c])
-        note(k="w")
-        tt(T.FW[:, sl], T.PK[:, sl], B[2 + c][:, 0:lw], A.subtract, r=["HJ%d" % c], w=["FW%d" % c], b=[2 + c])
-        act(T.FW[:, H + IN[c]:H + IN[c + 1]], B[2 + c][:, 0:lw], F.Identity, scale=1.0 / V, r=["HJ%d" % c], w=["FW%d" % (LCH + c)], b=[2 + c])
-        for o in ops[first:]:
-            o["t"] = 60 + lw
-
-    act(T.O32F[:], T.O32[:], F.Identity, scale=0.5, r=["O32"], w=["O32F"])
-    for name, wt in (("NI", -1.0), ("NI2", -0.5), ("WIM", -0.1875), ("I2K", -2048.0)):
-        act(T[name][:], ident, F.Identity, scale=wt, r=["I"], w=[name])
-        note(t=170)
-    for name, wt in (("BP1", 131072.0), ("BP2", 262144.0), ("BN", -131072.0)):
-        for j in range(3):
-            act(T[name][:, 8 * j:8 * j + 8], T.B8[:], F.Identity, scale=(wt if j == 0 else -wt), r=["B8"], w=[name + str(j)])
-    act(T.WT8[:], T.B8[:], F.Identity, scale=odd_w[0], r=["B8", odd_w[1]], w=["WT8"])
-    act(T.SC[:], T.HM[:], F.Identity, scale=-1.0e8, bias=1.0e8, r=["HM"], w=["SC"])
-    act(T.PM[:, 0:256], T.HM[:, 0:256], F.Identity, scale=-2.0 ** 99, bias=2.0 ** 98, r=["HM"], w=["PM"])
-    act(T.PM[:, 256:512], T.HM[:, 0:256], F.Identity, scale=-2.0 ** 99, bias=2.0 ** 98, r=["HM"], w=["PN"])
-    act(T.MSK[:, 0:256], T.MS0[:], F.Identity, bias=0.1875, r=["MS0"], w=["MSK"])
-    act(T.MSK[:, 256:272], T.HM[:, 0:16], F.Identity, scale=0.0, bias=0.5625, r=["HM"], w=["MSL"])
-    act(T.MSK[:, 272:512], T.HM[:, 0:240], F.Identity, scale=0.0, bias=0.1875, r=["HM"], w=["MSM"])
-
-    FWR = ["FW%d" % c for c in range(2 * LCH)] + ["FWd"]
-    KCR = ["KCa0", "KCa1", "KCb", "KCc", "KCd", "O32"]
-
-    def expand(bk, out0, name, src, sname, c0, start, stop):
-        for h in range(2):
-            for a in range(4):
-                o = out0 + 128 * h + 32 * a
-                m = min(32, 512 - o)
-                mm(bk, B[bk][:, o:o + m], T[name][:, 128 * a + 128:128 * a + 256], src[:, c0 + 32 * h:c0 + 32 * h + m],
-                   start, stop and (start or (h == 1 and a == 3)), r=[name + str(a), sname])
-
-    def chunk_of(w):
-        return [c for c in range(len(PC)) if PC[c][0] <= w < PC[c][0] + PC[c][1]][0]
-
-    for t in range(NV):
-        last = t == NV - 1
-        WH, wh = T["WH%d" % t], "WH%d" % t
-
-        def gather_f(j):
-            ts(T.G1[:, 512 * j:512 * j + 512], T.FW[:, 0:V].indirect(T.WU[:, 32 * j:32 * j + 32]), -2048.0, A.add, r=FWR + ["WU"], w=["G%d" % j])
-
-        def gather_fa():
-            w0, m, _ = PC[AF]
-            act(T.GF[:, 0:16 * m], T.FW[:, 0:V].indirect(T.WU[:, w0:w0 + m]), F.Identity, bias=-2048.0, r=FWR + ["WU"], w=["GF"])
-
-        def before(c):
-            w0, m, bk = PC[c]
-            mm(bk, B[bk][:, w0:w0 + m], T.NSH[:], WH[:, w0:w0 + m], True, False, r=["NSH", wh])
-            mm(bk, B[bk][:, w0:w0 + m], T.DO[:], T.O32[:, 0:m], False, False, r=["DO", "O32"])
-
-        def pick(c):
-            w0, m, bk = PC[c]
-            before(c)
-            for k in range(16):
-                mm(bk, B[bk][:, w0:w0 + m], T.SK[:, 128 * k:128 * k + 128], T.G1[:, 16 * w0 + k:16 * (w0 + m):16], False, k == 15,
-                   r=["SK%d" % k] + ["G%d" % j for j in range(w0 // 32, (w0 + m) // 32)])
-
-        def pick_a(part):
-            w0, m, bk = PC[AF]
-            if part == 0:
-                before(AF)
-            for k in range(4 * part, 4 * part + 4):
-                mm(bk, B[bk][:, w0:w0 + m], T.SKF[:, 128 * k:128 * k + 128], T.GF[:, k:16 * m:16], False, k == 15, r=["SKF", "GF"])
-
-        def names(c):
-            w0, m, bk = PC[c]
-            sl = slice(w0, w0 + m)
-            if t:
-                ts(T.EU[:, sl], B[bk][:, sl], 2048.0, A.add, w=["EU%d" % c], b=[bk])
-                return
-            ts(T.ET[:, sl], B[bk][:, sl], 2048.0, A.is_ge, -4096.0, A.mult, w=["ET%d" % c], b=[bk])
-            tt(T.EH[:, sl], T.ET[:, sl], B[bk][:, sl], A.add, r=["ET%d" % c], w=["EH%d" % c], b=[bk])
-            ts(T.EU[:, sl], T.EH[:, sl], 2048.0, A.add, r=["EH%d" % c], w=["EU%d" % c])
-
-        def wrap(cs):
-            if t:
-                bk, sl = PC[cs[0]][2], slice(PC[cs[0]][0], PC[cs[-1]][0] + PC[cs[-1]][1])
-                m = sl.stop - sl.start
-                ts(T.ET[:, sl], T.EU[:, sl], float(V), A.is_ge, -4096.0, A.mult, r=["EU%d" % c for c in cs], w=["ET%d" % c for c in cs])
-                note(t=50 + m // 2)
-                tt(T.EH[:, sl], T.ET[:, sl], B[bk][:, sl], A.add, r=["ET%d" % c for c in cs], w=["EH%d" % c for c in cs], b=[bk])
-                note(t=50 + m)
-
-        def gather_x(q, js):
-            w0, w1 = 32 * js[0], 32 * js[-1] + 32
-            win = T.REC[:] if t else T.REC[:, 0:V]
-            src, w = win.indirect(T.EU[:, w0:w1]), ["X%d" % j for j in js]
-            r = ["REC"] + (["REC2"] if t else []) + ["EU%d" % chunk_of(32 * j) for j in js]
-            if q == "a":
-                act(T.X[:, 16 * w0:16 * w1], src, F.Identity, bias=192.0, r=r, w=w)
-            else:
-                ts(T.X[:, 16 * w0:16 * w1], src, 192.0, A.add, r=r, w=w)
-            note(t=60 + 830 * len(js))
-
-        def sums(s):
-            bk, o = 2 + s // 2, 64 * (s % 2)
-            for k in range(16):
-                mm(bk, B[bk][:, o:o + 64], T.I16[:], T.X[:, 1024 * s + k:1024 * (s + 1):16], k == 0, k == 15, r=["I16", "X%d" % (2 * s), "X%d" % (2 * s + 1)])
-
-        def xs(h):
-            return ["X%d" % j for j in range(4 * h, 4 * h + 4)]
-
-        def xk(h, k):
-            return T.X[:, H * h + k:H * (h + 1):16]
-
-        def mb(h):
-            return T.MB[:, 128 * h:128 * h + 128]
-
-        def key_start(h):
-            mm(4 + h, B[4 + h][:, 0:384], T.O32[0:96, :], T.KC[0:96, :], True, False, r=KCR)
-            for k in KD[h]:
-                mm(4 + h, B[4 + h][:, k:384:16], xk(h, k), T.BN[:], False, False, r=xs(h) + ["BN0", "BN1", "BN2"])
-
-        def mean(h):
-            if MV[h]:
-                ts(mb(h), B[2 + h][:, 0:128], -0.46875, A.add, w=["MB%d" % h], b=[2 + h])
-            else:
-                act(mb(h), B[2 + h][:, 0:128], F.Identity, bias=-0.46875, w=["MB%d" % h], b=[2 + h])
-            mm(2 + h, B[2 + h][:, 128:256], ident, mb(h), True, True, r=["I", "MB%d" % h])
-
-        def ad(h, k):
-            return T.AD[:, H * h + 128 * k:H * h + 128 * k + 128]
-
-        def dist_v(h, part):
-            m = len(KD[h]) // 2
-            for k in (KD[h][m:] if part else KD[h][:m]):
-                tt(ad(h, k), xk(h, k), B[2 + h][:, 128:256], A.max, r=xs(h), w=["AD%d_%d" % (h, k)], b=[2 + h])
-
-        def group(h, i):
-            ka = [k for k in range(16) if k not in KD[h]]
-            return ka[4 * i:4 * i + 4]
-
-        def key_v(h):
-            for k in KD[h]:
-                mm(4 + h, B[4 + h][:, k:384:16], mb(h), T.BN[:], False, False, r=["MB%d" % h, "BN0", "BN1", "BN2"])
-            for k in KD[h]:
-                mm(4 + h, B[4 + h][:, k:384:16], ad(h, k), T.BP2[:], False, False, r=["AD%d_%d" % (h, k), "BP20", "BP21", "BP22"])
-
-        def key_a(h):
-            for k in range(16):
-                if k not in KD[h]:
-                    mm(4 + h, B[4 + h][:, k:384:16], ad(h, k), T.BP1[:], False, False, r=["AD%d_%d" % (h, k), "BP10", "BP11", "BP12"])
-
-        def diff(h, i):
-            bk, ks = 7 - (i & 1), group(h, i)
-            for j, k in enumerate(ks):
-                mm(bk, B[bk][:, 128 * j:128 * j + 128], ident, xk(h, k), j == 0, False, r=xs(h) + ["I"])
-                note(k="w" if j == 0 else "new")
-            for j, k in enumerate(ks):
-                mm(bk, B[bk][:, 128 * j:128 * j + 128], T.NI[:], mb(h), False, j == len(ks) - 1, r=["NI", "MB%d" % h])
-
-        def dist_a(h, i):
-            ks, bk = group(h, i), 7 - (i & 1)
-            if ks:
-                c0 = H * h + 128 * ks[0]
-                act(T.AD[:, c0:c0 + 128 * len(ks)], B[bk][:, 0:128 * len(ks)], F.Abs, w=["AD%d_%d" % (h, k) for k in ks], b=[bk])
-                note(t=60 + 133 * len(ks))
-
-        def key_end(h):
-            eh = ["EH%d" % c for c in range(len(PC)) if PC[c][0] // 128 == h]
-            mm(4 + h, B[4 + h][:, 0:128], T.EH[:, 128 * h:128 * h + 128], ident, False, False, r=eh + ["I"])
-            note(k="w")
-            mm(4 + h, B[4 + h][:, 128:384], WH[:, 128 * h:128 * h + 128], T.ISH[:], False, True, r=[wh, "I", "SH"])
-            scan(T.KF[:, 512 * h:512 * h + 384], T.SC[:], B[4 + h][:, 0:384], 0.0, A.add, A.min, r=["SC"], w=["KF%d" % h], b=[4 + h])
-
-        def jump(step):
-            if step == 0:
-                for h in range(2):
-                    mm(1, B[1][:, 288 + 8 * h:296 + 8 * h], mb(h), T.WT8[:], True, True, r=["WT8", "MB%d" % h])
-                act(T.SQ[:], B[1][:, 288:304], F.Square, bias=-48560.0, w=["SQ"], b=[1])
-            elif step == 1:
-                ts(T.ZI[:], T.SQ[:], 1.0 / 32, A.mult, -10952.375, A.add, r=["SQ"], w=["ZI"])
-            elif step == 2:
-                ts(T.ZA[:], T.ZI[:], V - 1, A.bitwise_and, r=["ZI"], w=["ZA"])
-            else:
-                for h in range(2):
-                    ts(T.KF[:, 512 * h + 399:512 * h + 512:16], T.ZA[:, 8 * h:8 * h + 8], -2048.0, A.add, r=["ZA"], w=["KZ%d" % h])
-
-        def threshold():
-            if t:
-                x = B[3][:, 280:281]
-                mm(3, x, T.O32F[:], T.ACC[:, 0:1], True, True, r=["O32F", "ACC"])
-                act(T.TA[:, 0:1], x, F.Identity, bias=1.5 * 2.0 ** 23, w=["TA"], b=[3])
-                act(T.TA[:, 1:2], T.TA[:, 0:1], F.Identity, scale=-1.0, bias=1.5 * 2.0 ** 23, r=["TA"], w=["TB"])
-                act(T.TA[:, 2:3], x, F.Abs, bias=T.TA[:, 1:2], r=["TB"], w=["TC"], b=[3])
-                act(T.THR[:, 0:1], T.TA[:, 2:3], F.Identity, scale=-2.0, bias=-4.5, r=["TC"], w=["THR"])
-
-        for s in ORDER.split():
-            c, a = s[0], s[1:]
-            now[0], now[1] = t, s
-            if c == "A":
-                gather_fa()
-            elif c == "G":
-                gather_f(int(a))
-            elif c == "P":
-                pick(int(a))
-            elif c == "F":
-                pick_a(int(a))
-            elif c == "N":
-                names(int(a))
-            elif c == "W":
-                wrap([int(j) for j in a])
-            elif c == "X":
-                gather_x(a[0], [int(j) for j in a[1:]])
-            elif c == "S":
-                sums(int(a))
-            elif c == "K":
-                key_start(int(a))
-            elif c == "M":
-                mean(int(a))
-            elif c == "D":
-                diff(int(a[0]), "abcd".index(a[1]))
-            elif c == "B":
-                dist_a(int(a[0]), "abcd".index(a[1]))
-            elif c == "V":
-                dist_v(int(a[0]), "ab".index(a[1]))
-            elif c == "E":
-                (key_v if a[1] == "v" else key_a)(int(a[0]))
-            elif c == "R":
-                key_end(int(a))
-            elif c == "Z":
-                jump(int(a))
-            elif c == "T":
-                threshold()
-            elif c == "H":
-                mm(2, B[2][:, 0:256], T.HDM[:], WH[:], True, False, r=["HDM", wh])
-                mm(0, B[0][:, 0:256], ident, T.EH[:], True, False, r=["I"] + ["EH%d" % q for q in range(len(PC))])
-        now[1] = None
-        mm(3, B[3][:, 0:256], T.AVM[:], WH[:], True, False, r=["AVM", wh])
-        mm(7, B[7][:], ident, T.MSK[:], True, False, r=["I", "MSK", "MSL", "MSM"])
-        mm(6, B[6][:, 0:256], T.O32[:], T.DC[:], True, False, r=["DC", "O32"])
-        keys, kr = T.KF[:, 15:1024:16], ["KF0", "KF1", "KZ0", "KZ1"]
-        ts(T.RQ[:], keys, MAG, A.add, -MAG, A.add, r=kr, w=["RQ"])
-        ts(T.RI[:], keys, 4096.0, A.add, r=kr, w=["RI"])
-        tt(T.P16[:], keys, T.RQ[:], A.subtract, r=kr + ["RQ"], w=["P16"])
-        ts(T.KK[:], T.RI[:], 13, A.arith_shift_right, 15, A.bitwise_and, r=["RI"], w=["KK"])
-        op("v", lambda e: e.transpose(T.PT[:], T.P16[:]), ["P16"], ["PT"])
-        expand(0, 0, "XN", T.PT, "PT", 0, False, True)
-        expand(2, 0, "XH", T.PT, "PT", 0, False, True)
-        cp(T.Q16[:, 0:64], T.KK[:], r=["KK"], w=["QK"])
-        cp(T.PY[:, 0:64], T.P16[:], r=["P16"], w=["PY"])
-        ts(T.EQ[:], B[0][:, 0:256], 0.0, A.is_equal, w=["EQ"], b=[0])
-        mm(1, B[1][:, 0:256], T.BO[:], T.EQ[:], True, True, r=["BO", "EQ"])
-        act(T.GO[:], B[1][:, 0:256], F.Sign, bias=T.THR[:, 0:1], scale=32.0, acc=(None if last else T.ACC[:, 0:1]),
-            r=["THR"], w=["GO", "ACC"], b=[1])
-        cp(T.Y2[:], T.PY[:].indirect(T.YOF[:]), r=["PY", "PY0", "YOF"], w=["Y2"])
-        tt(T.Q16[:, 64:104], T.Q16[:, 0:40], T.Q16[:, 8:48], A.is_equal, r=["QK", "Q0"], w=["QF"])
-        for gg in range(8):
-            mm(0, B[0][:, 256:512:16], T.CW[:, 112 - 16 * gg:240 - 16 * gg], T.Y2[:, 16 * gg:16 * gg + 16], gg == 0, gg == 7, r=["CW", "Y2", "Z0"])
-        expand(3, 0, "XA", T.PT, "PT", 0, False, True)
-        expand(6, 0, "XL", T.PT, "PT", 0, False, False)
-        expand(5, 256, "XL", T.PT, "PT", 0, True, True)
-        act(T.SG[:], B[5][:, 256:512], F.Sign, bias=0.5, w=["SG"], b=[5])
-        op("v", lambda e: e.transpose(T.QT[:], T.Q16[:]), ["QK", "QF"], ["QT"])
-        mm(4, B[4][:, 0:256], T.BO[:], T.EQ[:], True, False, r=["BO", "EQ"])
-        expand(4, 0, "XN", T.QT, "QT", 64, False, True)
-        expand(5, 0, "XC", T.QT, "QT", 0, True, True)
-        expand(7, 0, "XC", T.PT, "PT", 0, False, False)
-        expand(7, 272, "XC", T.PT, "PT", 0, False, False)
-        scan(T.RR[:], T.HM[:, 0:256], B[0][:, 256:512], 0.0, A.mult, A.add, r=["HM"], w=["RR"], b=[0])
-        tt(T.PRD[:], T.GO[:], B[2][:, 0:256], A.mult, r=["GO"], w=["PRD"], b=[2])
-        ts(T.OC[:], B[0][:, 256:512:16], 8192.0, A.mult, 2048.0, A.add, w=["OC"], b=[0])
-        if last:
-            tt(T.WF[:], T.PRD[:], B[3][:, 0:256], A.add, r=["PRD"], w=["WF"], b=[3])
-        else:
-            WO, nx = T["WO%d" % t], T["WH%d" % (t + 1)]
-            tt(WO[:], T.PRD[:], B[3][:, 0:256], A.add, r=["PRD"], w=["WO%d" % t], b=[3])
-            op("g", lambda e, WO=WO, nx=nx, t=t: e.remote_dma(nx[:], WO[:], T.sem["arr%d" % (t + 1)], T.sem.sent, pid, rid, mask_out), ["WO%d" % t])
-            note(line="ring")
-        act(T.WA[:], B[4][:, 0:256], F.Sign, bias=T.THR[:, 0:1], scale=32.0, r=["THR"], w=["WA"], b=[4])
-        act(T.U[:], B[5][:, 0:256], F.Abs, bias=kbias[0], scale=2.0 ** 27, r=[kbias[1]], w=["U"], b=[5])
-        mm(7, B[7][:, 0:256], T.NI2[:], T.RR[:], False, False, r=["NI2", "RR"])
-        mm(7, B[7][:, 256:512], T.NI2[:], T.RR[:], False, False, r=["NI2", "RR"])
-        mm(7, B[7][:, 272:512], T.WIM[:], T.WA[:, 0:240], False, False, r=["WIM", "WA"])
-        mm(7, B[7][:, 0:256], T.WIM[:], T.WA[:], False, True, r=["WIM", "WA"])
-        for a in range(16):
-            mm(1, B[1][:, 256:272], T.SK[:, 128 * a:128 * a + 128], T.WA[:, a:256:16], a == 0, a == 15, r=["SK%d" % a, "WA"])
-        mm(6, B[6][:, 0:256], T.I2K[:], T.SG[:], False, False, r=["I2K", "SG"])
-        note(tag="I6")
-        mm(6, B[6][:, 0:256], T.NI[:], T.U[:], False, True, r=["NI", "U"])
-        act(T.LS[:], B[6][:, 0:256], F.Identity, w=["LS"], b=[6])
-        if last:
-            act(T.WG[:], T.WF[:], F.Identity, bias=2048.0, r=["WF"], w=["WG"])
-            dma("a", T.yw[:], T.WG[:], r=["WG"], w=["yw"])
-        scan(T.PS[:], T.PM[:], B[7][:], 1.0, A.max, A.mult, r=["PM", "PN"], w=["PS"], b=[7])
-        tt(T.OM[:], T.FW[:, 0:V].indirect(T.OC[:]), T.U[:], A.min, r=FWR + ["OC", "U"], w=["OM"])
-        ts(T.LO[:], T.PS[:, 15:512:16], 0.0, A.is_equal, 0.625, A.add, r=["PS"], w=["LO"])
-        tt(T.K2[:], T.RR[:, 0:256:16], B[1][:, 256:272], A.subtract, r=["RR"], w=["K2"], b=[1])
-        tt(T.K3[:], T.LO[:, 0:16], T.LO[:, 16:32], A.add, r=["LO"], w=["KA"])
-        tt(T.K4[:], T.K3[:], T.K2[:], A.add, r=["KA", "K2"], w=["KB"])
-        for j in range(2):
-            ts(T.OFF[:, j:16:2], T.K4[:, j:16:2], 8192.0, A.mult, dummy[j][0], A.min, r=["KB", dummy[j][1]], w=["OFF%d" % j])
-        if not last:
-            op("v", None, w=["WH%d" % (t + 1)])
-            note(src="arr%d" % (t + 1), sem="arr%d" % (t + 1), val=n_in, t=0, line="ring")
-            ts(T.WU[:], T["WH%d" % (t + 1)][:], 2048.0, A.add, r=["WH%d" % (t + 1)], w=["WU"])
-        for b in range(7, -1, -1):
-            tt(T.FW[:].indirect(T.OFF[:, 2 * b:2 * b + 2]), T.OM[:, 32 * b:32 * b + 32], T.LS[:, 32 * b:32 * b + 32], A.max,
-               r=["OFF0", "OFF1", "OM", "LS"], w=FWR)
-            note(t=180)
-
-    now[0], now[1] = NV, "end"
-    for c in range(len(OUT) - 1):
-        a, b, bk = OUT[c], OUT[c + 1], 2 + c
-        act(B[bk][:, 0:b - a], T.FW[:, H + a:H + b], F.Identity, scale=float(V), r=FWR, b=[bk])
-        note(k="w", t=60 + b - a)
-        tt(T.YO[:, a:b], T.FW[:, a:b], B[bk][:, 0:b - a], A.add, r=FWR, w=["YP%d" % c] + ["YO%d" % j for j in UNP], b=[bk])
-        note(t=60 + b - a)
-        dma("s", T.yf[:, a:b], T.YO[:, a:b], r=["YP%d" % c], w=["yf%d" % c])
-    op("s", None, r=["yw"] + ["yf%d" % c for c in range(len(OUT) - 1)])
-    note(src="end")
-    emit(g, T, arrange(ops))
-    g.wait_ge(T.sem.sent, n_out * (NV - 1))
+    ops = record(T, (pid, rid, topo.mask(core, nxt), len(topo.engines(prv, core))))
+    if "order" not in _KEPT:
+        _KEPT["order"] = arrange(ops)
+    emit(g, T, ops, _KEPT["order"])
+    g.wait_ge(T.sem.sent, len(topo.engines(core, nxt)) * (NV - 1) * 2)

from concourse.mybir import AluOpType as A, ActivationFunctionType as F

V, H, K, NV = 4096, 2048, 256, 5
MAG = 1.5 * 2.0 ** 36
AL = 0.1875
CFG = {
    "IN": [0, 256, 768, 1280, 1792, 2048],
    "OUT": [0, 256, 768, 1280, 1792, 2048],
    "UNP": (1, 3),
    "PC": [(224, 32, 0, "v"), (192, 32, 0, "v"), (128, 64, 0, "v"), (64, 64, 1, "v"), (0, 64, 1, "v")],
    "WR": [(0, 128, 1), (128, 128, 0)],
    "XV": (0,),
    "KD": [0, 12],
    "GW": 32,
    "VG": 2,
    "MEAN": "aa",
    "TB": [dict(eq=(0, 0), vo=(2, 256), df=(3, 0), av=(5, 384), va=(6, 0), ls=(1, 256), kk=(4, 384), pr=(7, 0), cc=(2, 384), zz=(2, 420)),
           dict(eq=(0, 256), vo=(3, 384), df=(0, 384), av=(5, 128), va=(5, 0), ls=(5, 256), kk=(3, 256), pr=(1, 0), cc=(3, 128), zz=(0, 0))],
    "TH": (2, 500),
    "WR0": [(192, 64, 0), (128, 64, 0), (64, 64, 1), (0, 64, 1)],
    "HEAD": {"v": "G0a G1a G2a IH0 IN0 G2b G3a IH1 IN1 G3b G4a IH2 IN2 G4b IX2 IH3 IN3 IX0",
             "a": "IT0 X7 X6 IT1 X5 X4 IT2 X3 M1 IT3 X1", "p": "P0 P1 P2 K1 P3 S3 S2 P4 K0"},
    "LOAD": {"v": "Ua0 Ub0 Uc0 Ua1 Ua2 Ub2 Uc1 Ua3 Uc2 Ua4 Ub4 UW Uc4 Uc3 UH", "a": "Uc0 Ua1 Ub1 Uc1 Uc2 Ua3 Ub3 Uc3 Uc4"},
    "XV0": (2, 0),
    "WAT": 4,
    "ORDER": {
        "v": "G0a G1a N0 G2a N1 G2b WU0< G3a N2 G3b G4a N3 G4b N4 V1a X0 V1f V1c V1b V1d V1e EH1 EH0 ZI1 SC1 RQ1 ZA1 PP1 QS1 ZP1 MX1 PT1 "
             "CS1 EQ1 RR1 ZI0 OC1 SC0 ZA0 RQ0 ZP0 PP0 QS0 PD1 MX0 PS1 PT0 LO1 WO1 KA1 EQ0 CS0 OM1 RR0 OC0 KB1 OM0 OF1 PS0 F7 LO0 F6 KA0 "
             "F5 KB0 F4 OF0 PD0 F3 WO0 F2 F1 WU1 F0",
        "a": "TA TB X7 X6 TC X4 X5 X3 M1 X2 X1 ET1 B1a M0 SQ1 ET0 B0b TD B0a B0d B0c SQ0 GO1 SG1 U1 U0 GO0 LS1 SG0 LS0",
        "p": "P0 K1 TM P1 K0 P2 S3 P3 S2 DX1a P4 MP1 KX1 DM1a EM1 ZM1 S1 EV1a S0 DX0b EB1a EV1c DM0b DX0a DM0a EV1b EV1f EV1e EV1d R1 "
             "DX0d DM0d DX0c DM0c EB0a EB0b ZM0 CM1 QB1 EB0d PA1 EB0c R0 SA1 BO1 SB1 DA1 PB1 DB1 PC1 AA1 PW1 AB1 KM1 PA0 SA0 LA0 QB0 CM0 "
             "KM0 PB0 BO0 LA1 LB1 LC1 LD1 PC0 PW0 AA0 LB0 DA0 DB0 SB0 LC0 LD0 AB0",
        "g": "TO1 TO0"},
}


def _sb(n, d):
    return ("sbuf", [128, n], d)


SCRATCH = {
    "PK": _sb(H, "int32"), "HI": _sb(H, "int32"), "FW": _sb(V + 96, "float32"), "REC": _sb(2 * V, "bfloat16"), "YO": _sb(H, "float32"),
    "WI": _sb(K, "int32"), "WU": _sb(K, "uint16"), "EU": _sb(K, "uint16"), "EH": _sb(K, "float16"), "ET": _sb(K, "bfloat16"),
    "G1": _sb(V, "float16"), "GF": _sb(2048, "float32"), "X": _sb(V, "bfloat16"), "AD": _sb(V, "bfloat16"), "MB": _sb(K, "bfloat16"),
    "KF": _sb(1024, "float32"), "RQ": _sb(64, "float32"), "P16": _sb(64, "float16"), "PT": _sb(64, "float16"), "QS": _sb(16, "float32"),
    "SQ": _sb(16, "float32"), "ZI": _sb(16, "int32"), "ZA": _sb(16, "int32"),
    "EQ": _sb(K, "bfloat16"), "GO": _sb(K, "bfloat16"), "PRD": _sb(K, "float32"), "SG": _sb(K, "bfloat16"),
    "ACC": _sb(4, "float32"), "TA": _sb(4, "float32"), "THR": _sb(4, "float32"),
    "CS0": _sb(512, "float32"), "CS1": _sb(512, "float32"), "RR": _sb(K, "float16"), "OC": _sb(16, "uint16"), "U": _sb(K, "bfloat16"),
    "OM": _sb(K, "float32"), "LS": _sb(K, "float32"), "PS": _sb(2 * K, "float32"), "LO": _sb(32, "float32"),
    "K3": _sb(16, "float32"), "K4": _sb(16, "float32"), "OFF": _sb(16, "uint16"), "WF": _sb(K, "float32"), "WG": _sb(K, "float32"),
    "RD": _sb(128, "bfloat16"), "RG": _sb(128, "bfloat16"), "RK": _sb(128, "bfloat16"), "CP": _sb(4, "int32"),
    "CI": _sb(4, "int32"), "CF": _sb(4, "float32"), "CC": _sb(16, "float32"), "MK": _sb(16, "float32"),
    "I": _sb(128, "bfloat16"), "SH": _sb(128, "bfloat16"), "NSH": _sb(128, "bfloat16"), "I16": _sb(128, "bfloat16"), "NI": _sb(128, "bfloat16"),
    "I2K": _sb(128, "bfloat16"), "PSH": _sb(128, "bfloat16"), "NIU": _sb(128, "bfloat16"), "BNW": _sb(768, "bfloat16"),
    "NI2": _sb(128, "bfloat16"), "WIM": _sb(128, "bfloat16"), "SK": _sb(2048, "bfloat16"), "SKF": _sb(2048, "float32"),
    "O32": _sb(128, "bfloat16"), "O32F": _sb(128, "float32"), "MVH": _sb(128, "bfloat16"), "TBH": _sb(128, "bfloat16"),
    "HDM": _sb(128, "bfloat16"), "AVM": _sb(128, "bfloat16"), "BO": _sb(128, "bfloat16"), "B8": _sb(8, "float32"),
    "BP1": _sb(24, "bfloat16"), "BP2": _sb(24, "bfloat16"), "BN": _sb(24, "bfloat16"), "WT8": _sb(8, "bfloat16"),
    "XN": _sb(512, "bfloat16"), "XC": _sb(512, "bfloat16"), "XK": _sb(512, "bfloat16"), "XH": _sb(512, "bfloat16"), "XA": _sb(512, "bfloat16"),
    "ZR": _sb(512, "bfloat16"), "CM0": _sb(160, "bfloat16"), "CM1": _sb(160, "bfloat16"),
    "MS0": _sb(128, "bfloat16"), "MSK": _sb(256, "bfloat16"), "HM": _sb(128, "bfloat16"),
    "SC": _sb(384, "bfloat16"), "PM": _sb(256, "bfloat16"), "KC": _sb(384, "bfloat16"),
}
for _t in range(NV):
    SCRATCH["WH%d" % _t] = _sb(K, "float16")
for _t in range(NV - 1):
    SCRATCH["WO%d" % _t] = _sb(K, "float16")
for _b in range(8):
    SCRATCH["B%d" % _b] = ("psum", [128, 512], "float32")
SEMAPHORES = (["sv", "sa", "sp", "sg", "sent"] + ["arr%d_%d" % (_t, _h) for _t in range(1, NV) for _h in range(2)]
              + ["d%d" % _i for _i in range(16)])

CYC, PCYC, GATHER, SCATTER, VCALL, ACALL = 0.95, 0.48, 1.5, 3.5, 50, 65
HOP, SAME, LINK, SLACK, DMA0, DMARATE = 70, 60, 2600, 60, 2000, 200.0
POOL = ("pool", (0, 128, 0, 0, 1))
_KEPT = {}


def meet(a, b):
    if a[1] <= b[0] or b[1] <= a[0] or a[3] < b[2] or b[3] < a[2]:
        return False
    return a[4] != b[4] or (a[2] - b[2]) % a[4] == 0


def depend(ops):
    seen = {}
    for i, o in enumerate(ops):
        dep = set(o["dep"])
        for name, reg in o["r"]:
            dep.update(j for j, w, q in seen.get(name, []) if w and meet(reg, q))
        for name, reg in o["w"]:
            old = seen.get(name, [])
            dep.update(j for j, w, q in old if meet(reg, q))
            seen[name] = [e for e in old if not (reg[0] <= e[2][0] and e[2][1] <= reg[1] and reg[2] <= e[2][2] and e[2][3] <= reg[3]
                                                 and (reg[4] == 1 or (reg[4] == e[2][4] and meet(reg, e[2]))))]
        for name, reg in o["r"]:
            seen.setdefault(name, []).append((i, False, reg))
        for name, reg in o["w"]:
            seen.setdefault(name, []).append((i, True, reg))
        if o["q"] != "p":
            dep.update([ops[j]["group"][-1] for j in dep if "group" in ops[j]])
        dep.discard(i)
        o["dep"] = dep


def lag(a, b):
    if a.get("line", 0) == b.get("line", 1):
        return LINK if b["fn"] is None else 0
    if a["src"] != b["src"]:
        return HOP + a["lat"]
    return SAME if b["q"] != "p" else 0


def arrange(ops):
    n = len(ops)
    back = [dict((j, lag(ops[j], o)) for j in o["dep"]) for o in ops]
    line, steps = {}, {}
    for i, o in enumerate(ops):
        if "line" in o:
            if o["line"] in line:
                back[i].setdefault(line[o["line"]], lag(ops[line[o["line"]]], o))
            line[o["line"]] = i
        steps.setdefault((o["q"], o["visit"], o["tag"]), []).append(i)
    for (q, t, s), members in steps.items():
        for i in (members[1:] if q == "p" else []):
            for j in set(ops[i]["dep"]).difference(members):
                back[members[0]].setdefault(j, -1e9)
    for q, names in CFG["ORDER"].items():
        chain = []
        for t in range(-1, NV + 1):
            head = CFG[("LOAD", "HEAD")[t + 1]].get(q, "").split() if t < 1 else []
            for s in head + [s for s in names.split() if s not in head]:
                chain += steps.get((q, t + s.count(">") - s.count("<"), s.strip("<>")), [])
        for a, b in zip(chain, chain[1:]):
            back[b].setdefault(a, 0)
    fore = [[] for _ in range(n)]
    for i in range(n):
        for j, d in back[i].items():
            fore[j].append((i, d))
    left = [len(f) for f in fore]
    todo, path = [i for i in range(n) if not left[i]], [0.0] * n
    while todo:
        i = todo.pop()
        path[i] = ops[i]["t"] + max([path[j] + d for j, d in fore[i]] + [0.0])
        for j in back[i]:
            left[j] -= 1
            if not left[j]:
                todo.append(j)
    left = [len(b) for b in back]
    ready = [i for i in range(n) if not left[i]]
    est, end, free, used, opened, order = [0.0] * n, [0.0] * n, {}, {}, set(), []

    def start(i):
        o = ops[i]
        s = max(est[i], free.get(o["q"], 0.0)) if o["fn"] is not None else est[i]
        for b in o["b"]:
            for q, e in used.get(b, {}).items():
                if q != o["q"]:
                    s = max(s, e + HOP)
        return s

    unread, owed = [0] * 8, [[] for _ in range(n)]
    for i, o in enumerate(ops):
        for b in (o["b"] if o["q"] != "p" and o["visit"] < NV else []):
            for j in sorted(j for j in o["dep"] if ops[j]["q"] == "p" and ops[j]["b"] == [b])[-1:]:
                owed[ops[j]["group"][-1]].append((b, 1))
                owed[i].append((b, -1))

    def may(i):
        o = ops[i]
        if o["q"] == "p" and o["group"][0] != i:
            return True
        return not opened.intersection(o["b"]) and not (o["q"] == "p" and o["long"][0] and unread[o["b"][0]])

    while ready:
        st = {i: start(i) for i in ready if may(i)}
        first = min(st, key=lambda i: (st[i], i))
        q = ops[first]["q"]
        i = max((j for j in st if ops[j]["q"] == q and st[j] <= st[first] + SLACK), key=lambda j: (path[j], -j))
        o = ops[i]
        end[i] = st[i] + o["t"]
        if o["fn"] is not None:
            free[q] = end[i]
        for b in o["b"]:
            used.setdefault(b, {})[q] = end[i] + o["lat"]
            if q == "p" and o["group"][0] == i:
                opened.add(b)
            if q == "p" and o["group"][-1] == i:
                opened.discard(b)
        for b, d in owed[i]:
            unread[b] += d
        ready.remove(i)
        order.append(i)
        for j, d in fore[i]:
            est[j] = max(est[j], end[i] + d)
            left[j] -= 1
            if not left[j]:
                ready.append(j)
    assert len(order) == n
    _KEPT["span"] = max(end)
    return order


def emit(g, T, ops, order):
    queues = {"v": g.vector, "a": g.scalar, "p": g.tensor, "g": g, "s": g.sync}
    place = {i: n for n, i in enumerate(order)}
    run = [ops[i] for i in order]
    bank, clock, seen = {}, {}, {}
    for i, o in enumerate(run):
        q, src = o["q"], o["src"]
        deps = set(place[j] for j in o["dep"] if q != "p" or ops[j]["q"] != "p")
        for b in o["b"]:
            deps.update(j for s, j in bank.get(b, {}).items() if s != src)
        know = seen.setdefault(q, {})
        waits = []
        for j in sorted(deps, reverse=True):
            if know.get(run[j]["src"], -1) < j:
                waits.append(j)
                run[j]["sig"] = True
                for s, n in clock[j].items():
                    know[s] = max(know.get(s, -1), n)
        o["waits"] = waits
        clock[i] = dict(know) if o["fn"] is not None else {}
        clock[i][src] = i
        for b in o["b"]:
            bank.setdefault(b, {})[src] = i
    count = {}
    for o in run:
        if o["sem"] is None and o["sig"]:
            count[o["q"]] = count.get(o["q"], 0) + 1
            o["sem"], o["val"], o["inc"] = "s" + o["q"], count[o["q"]], 1
    for o in run:
        q = queues[o["q"]]
        for j in o["waits"]:
            q.wait_ge(T.sem[run[j]["sem"]], run[j]["val"])
        if o["fn"] is not None:
            ins = o["fn"](q)
            if o["inc"]:
                ins.then_inc(T.sem[o["sem"]], o["inc"])


def record(T, route):
    pid, rid, mask_out, n_in = route
    ops, nd, lat, now, group = [], [0], [0.0], [-1, None], {}
    IN, OUT, UNP, PC, XV, KD, VG = [CFG[k] for k in ("IN", "OUT", "UNP", "PC", "XV", "KD", "VG")]
    shapes = {"fld": H, "rec": V, "wnd": K, "yf": H, "yw": K}

    def S(name, a=0, b=None, st=1, p=(0, 128)):
        where, shape, dt = SCRATCH.get(name, ("hbm", [128, shapes.get(name)], "float32"))
        b = shape[1] if b is None else b
        m = (b - a + st - 1) // st
        return {"ap": T[name][p[0]:p[1], a:b:st], "name": name, "reg": (p[0], p[1], a, a + st * (m - 1), st), "n": m, "ps": where == "psum",
                "two": dt in ("bfloat16", "float16", "uint16"), "f32": dt == "float32"}

    def B(bk, a=0, b=None, st=1):
        return S("B%d" % bk, a, b, st)

    def IND(win, off):
        return dict(win, ap=win["ap"].indirect(off["ap"]), n=16 * off["n"], off=off)

    def ap(x):
        return x["ap"] if isinstance(x, dict) else x

    def op(q, fn, r, w, t):
        r = [x for x in r if isinstance(x, dict)]
        r += [x["off"] for x in r + w if "off" in x]
        banks = sorted(set(int(x["name"][1]) for x in r + w if x["ps"]))
        ops.append({"q": q, "src": q, "fn": fn, "r": [(x["name"], x["reg"]) for x in r], "w": [(x["name"], x["reg"]) for x in w],
                    "b": banks, "sig": False, "sem": None, "val": 0, "inc": 0, "dep": [], "t": t, "lat": 0, "visit": now[0], "tag": now[1]})

    def note(**kw):
        ops[-1].update(kw)

    def step(tag):
        now[1] = tag

    def vt(out, *ins):
        x = ins[0]
        if "off" in x:
            return VCALL + CYC * GATHER * x["n"]
        if "off" in out:
            return VCALL + CYC * SCATTER * x["n"]
        return VCALL + CYC * x["n"] * (0.5 if all(y["two"] for y in (out,) + ins) else 1)

    def dma(q, out, in_, size):
        s = "d%d" % nd[0]
        nd[0] += 1
        op(q, lambda e: e.dma_start(out["ap"], in_["ap"]), [in_], [out], 50)
        lat[0] += 128 * size * out["n"] / DMARATE
        note(src=s, sem=s, val=16, inc=16, lat=DMA0 + lat[0], line="dma" + q)

    def ts(out, in0, s1, op0, s2=None, op1=None):
        if op1 is None:
            op("v", lambda e: e.tensor_scalar(out["ap"], in0["ap"], ap(s1), None, op0), [in0, s1], [out], vt(out, in0))
        else:
            op("v", lambda e: e.tensor_scalar(out["ap"], in0["ap"], ap(s1), ap(s2), op0, op1), [in0, s1, s2], [out], vt(out, in0))

    def tt(out, in0, in1, o):
        plain = "off" not in in0 and "off" not in out
        t = VCALL + CYC * in0["n"] * (1 if in0["ps"] or in1["ps"] else 2) if plain else vt(out, in0)
        op("v", lambda e: e.tensor_tensor(out["ap"], in0["ap"], in1["ap"], o), [in0, in1], [out], t)

    def cp(out, in_):
        op("v", lambda e: e.tensor_copy(out["ap"], in_["ap"]), [in_], [out], vt(out, in_))

    def turn(out, in_):
        op("v", lambda e: e.transpose(out["ap"], in_["ap"]), [in_], [out], vt(out, in_))

    def fill(out, c):
        op("v", lambda e: e.memset(out["ap"], c), [], [out], vt(out, out))

    def scan(out, d0, d1, init, o0, o1):
        op("v", lambda e: e.tensor_tensor_scan(out["ap"], d0["ap"], d1["ap"], init, o0, o1), [d0, d1], [out], vt(out, d0, d1))

    def act(out, in_, f, bias=0.0, scale=1.0, acc=None):
        op("a", lambda e: e.activation(out["ap"], in_["ap"], f, bias=ap(bias), scale=ap(scale), accum_out=ap(acc)),
           [in_, bias, scale], [out] + ([acc] if acc else []), ACALL + CYC * in_["n"] * (GATHER if "off" in in_ else 1))

    def mm(out, lhsT, rhs, start, stop):
        op("p", lambda e: e.matmul(out["ap"], lhsT["ap"], rhs["ap"], start, stop), [lhsT, rhs], [out],
           PCYC * max(min(64, lhsT["n"]), rhs["n"]) * (4 if lhsT["f32"] else 1))
        if start:
            group[out["name"]] = ([], [False])
        members, long = group[out["name"]]
        long[0] = long[0] or bool(members) and ops[members[0]]["tag"] != now[1]
        note(lat=60, group=members, long=long, dep=(list(members) if stop else members[:1]))
        members.append(len(ops) - 1)

    def iota(out, pat, base, mult, flag=True):
        if flag:
            op("g", lambda e: e.iota(out["ap"], pat, base, mult, allow_small_or_imprecise_dtypes=True), [], [out], 200 + 2 * CYC * out["n"])
        else:
            op("g", lambda e: e.iota(out["ap"], pat, base, mult), [], [out], 200 + 2 * CYC * out["n"])
        ops[-1]["w"].append(POOL)

    def mark(out, pat, base, mult, value, src=None, keep=A.not_equal):
        src = src or out
        op("g", lambda e: e.affine_select(out["ap"], src["ap"], pat, keep, value, base, mult), [src], [out], 200 + 2 * CYC * out["n"])
        ops[-1]["w"].append(POOL)

    LCH = len(IN) - 1
    for c in range(LCH):
        dma("s", S("PK", IN[c], IN[c + 1]), S("fld", IN[c], IN[c + 1]), 4)
        if c == CFG["WAT"]:
            dma("s", S("WI"), S("wnd"), 4)
    dma("s", S("REC", 0, V), S("rec"), 2)
    dma("s", S("REC", V, 2 * V), S("rec"), 2)
    lat[0] = 0

    iota(S("CP", 0, 1), [[1, 1]], 0, 1, False)
    iota(S("RD"), [[1, 128]], 0, -1)
    iota(S("RK"), [[0, 8], [1, 16]], 0, 0)
    iota(S("RG"), [[1, 8], [0, 16]], 0, 0)
    if any(c[3] == "a" for c in PC):
        iota(S("SKF"), [[0, 2048]], 1, 0)
        mark(S("SKF"), [[-256, 16], [-16, 8], [255, 16]], 0, 1, 0.0, keep=A.is_equal)
    iota(S("KC", 0, 256, p=(32, 64)), [[0, 16], [8192, 16]], 0, 0)
    iota(S("KC", 256, 384, p=(32, 64)), [[0, 8], [64, 16]], 2112, 0)
    iota(S("KC", 0, 128, p=(0, 32)), [[0, 128]], -120 * 131072, 0)
    iota(S("KC", 128, 384, p=(0, 32)), [[0, 256]], 120 * 131072, 0)
    fill(S("ZR"), 0.0)
    mark(S("SC"), [[0, 24], [1, 16]], 0, 0, 1.0e8, S("ZR", 0, 384))
    every, top = [[-32, 4], [-1, 8], [0, 16]], [[-32, 4], [-1, 8], [-256, 16]]
    mark(S("XN"), every, 0, 1, 2.0 ** -11, S("ZR"))
    for j in range(2):
        mark(S("CM%d" % j), [[-2, 5], [-32, 16], [300, 2]], -6 - j, 1, 2.0 ** -13, S("ZR", 0, 160))
        iota(S("CS%d" % j, 0, 128), [[0, 128]], 0, 0)
    mark(S("HM"), [[0, 8], [1, 16]], 0, 0, 1.0, S("ZR", 0, 128), A.is_equal)
    mark(S("XK"), every, -16, 1, 2.0 ** -6, S("ZR"))
    mark(S("XC"), every, -8, 1, 2.0 ** -14, S("ZR"))
    for name, wt in (("XH", -0.5), ("XA", 0.5)):
        mark(S(name), top, 0, 1, 0.5, S("ZR"))
        mark(S(name), top, -24, 1, wt)
    iota(S("FW", V), [[0, 96]], 0, 0)
    mark(S("PM"), [[0, 16], [1, 16]], 0, 0, -2.0 ** 98, S("ZR", 0, 256), A.is_equal)
    mark(S("PM"), [[0, 16], [1, 16]], 0, 0, 2.0 ** 98)
    fill(S("O32"), 1.0 / 32)
    bits = [(0, 15), (4, 7), (0, 1)]
    for j, (sh, m) in enumerate(bits):
        ts(S("CI", j, j + 1), S("CP", 0, 1), sh, A.logical_shift_right, m, A.bitwise_and)
    cp(S("CF", 0, 3), S("CI", 0, 3))
    c16, cG, cO = [S("CF", j, j + 1) for j in range(3)]
    ident = S("I")
    ts(ident, S("RD"), 0.0, A.is_equal)
    ts(S("MK"), S("RK", 0, 16), c16, A.is_equal)
    nc = [0]

    def col(in0, s1, s2, o0=A.mult, o1=A.add):
        nc[0] += 1
        ts(S("CC", nc[0] - 1, nc[0]), in0, s1, o0, s2, o1)
        return S("CC", nc[0] - 1, nc[0])

    def eqm(name, row, c, wt):
        ts(S(name), row, c, A.is_equal, wt, A.mult)

    even = col(cO, -1.0, 1.0)
    eqm("SH", S("RD"), 1.0, even)
    for k in range(16):
        act(S("SK", 128 * k, 128 * k + 128), ident, F.Identity, scale=S("MK", k, k + 1))
    ts(S("NSH"), S("SH"), -2.0 ** -11, A.mult)
    ts(S("I16"), ident, 1.0 / 16, A.mult)
    not15 = col(S("MK", 15, 16), -0.5, 0.5)
    a15 = col(c16, -2.0, 15.0)
    odd_w = col(c16, 2.0, 1.0)
    dummy = [col(c16, 1.0, float(V)), col(c16, 1.0, float(V + 16))]
    kbias = col(c16, -8192.0, -33 * 8192.0)
    eu_add = col(cO, 2048.0, 2048.0)
    odd_tiny = col(cO, 2.0 ** -12, 0.0)
    ms_add = col(c16, 2 * AL, -AL)
    ts(S("B8"), S("RK", 0, 8), cG, A.is_equal)
    ts(S("MS0"), S("RK", 0, 128), -2 * AL, A.mult, ms_add, A.add)
    ts(S("MSK", 0, 128), S("MS0"), AL, A.min, -3 * AL, A.max)
    fill(S("MSK", 128, 144), 3 * AL)
    fill(S("MSK", 144, 256), AL)
    eqm("MVH", S("RD"), 1.0, not15)
    eqm("TBH", S("RD"), a15, not15)
    eqm("BO", S("RG", 0, 128), cG, 1.0 / 32)
    tt(S("HDM"), S("MVH"), S("TBH"), A.subtract)
    tt(S("AVM"), S("MVH"), S("TBH"), A.add)
    fill(S("THR"), -4.5)

    for c in range(LCH):
        a, b = IN[c], IN[c + 1]
        hj = B(2 + c, 0, b - a)
        if c in UNP:
            step("Ua%d" % c)
            ts(S("YO", a, b), S("PK", a, b), -2.0 ** 23, A.add, -2047.5, A.add)
            act(S("YO", a, b), S("YO", a, b), F.Identity, bias=MAG / 2)
            step("Ub%d" % c)
            act(hj, S("YO", a, b), F.Identity, bias=2.0 ** 23 - MAG / 2)
        else:
            step("Ua%d" % c)
            ts(S("HI", a, b), S("PK", a, b), 12, A.logical_shift_right)
            step("Ub%d" % c)
            ts(hj, S("HI", a, b), float(V), A.mult)
        step("Uc%d" % c)
        tt(S("FW", a, b), S("PK", a, b), hj, A.subtract)
        if c in UNP:
            act(S("FW", H + a, H + b), S("YO", a, b), F.Identity, scale=1.0 / V, bias=(2.0 ** 23 - MAG / 2) / V)
        else:
            act(S("FW", H + a, H + b), hj, F.Identity, scale=1.0 / V)
    step("UW")
    cp(S("WU"), S("WI"))
    step("UH")
    ts(S("WH0"), S("WU"), -2048.0, A.add)
    step(None)

    act(S("O32F"), S("O32"), F.Identity, scale=0.5)
    for name, wt in (("NI", -1.0), ("NI2", -0.5), ("WIM", -AL), ("I2K", 2048.0), ("NIU", -2.0 ** -11)):
        act(S(name), ident, F.Identity, scale=wt)
    act(S("PSH"), S("SH"), F.Identity, scale=2.0 ** -11)
    for h in range(2):
        if KD[h] > 6:
            for j in range(3):
                act(S("BNW", 384 * h + 128 * j, 384 * h + 128 * j + 128), S("BO"), F.Identity, scale=(-1 if j == 0 else 1) * 32 * 131072.0)
            if KD[h] < 16:
                mark(S("BNW", 384 * h, 384 * h + 384), [[0, 24], [-1, 16]], KD[h] - 1, 0, 0.0, keep=A.is_ge)
    for name, wt in (("BP1", 131072.0), ("BP2", 262144.0), ("BN", -131072.0)):
        for j in range(3):
            act(S(name, 8 * j, 8 * j + 8), S("B8"), F.Identity, scale=(wt if j == 0 else -wt))
    act(S("WT8"), S("B8"), F.Identity, scale=odd_w)

    for t in range(NV):
        last = t == NV - 1
        wh, WR = "WH%d" % t, CFG["WR" if t else "WR0"]
        now[0] = t

        def proposals(c):
            w0, m, bk, q = PC[c]
            e = B(bk, w0, w0 + m)
            if q == "a":
                step("GA%d" % c)
                gf = 1024 * ([j for j in range(len(PC)) if PC[j][3] == "a"].index(c) % 2)
                act(S("GF", gf, gf + 16 * m), IND(S("FW", 0, V), S("WU", w0, w0 + m)), F.Identity, bias=-1.0, scale=2.0 ** -11)
            else:
                for w in range(w0, w0 + m, CFG["GW"]):
                    w1 = min(w + CFG["GW"], w0 + m)
                    step("G%d%s" % (c, "abcd"[(w - w0) // CFG["GW"]]))
                    ts(S("G1", 16 * w, 16 * w1), IND(S("FW", 0, V), S("WU", w, w1)), -2048.0, A.add, 2.0 ** -11, A.mult)
            step("P%d" % c)
            mm(e, S("NSH"), S(wh, w0, w0 + m), True, False)
            for k in range(16):
                if q == "a":
                    step("P%d%s" % (c, "abcd"[k // 4]))
                    mm(e, S("SKF", 128 * k, 128 * k + 128), S("GF", gf + k, gf + 16 * m, 16), False, k == 15)
                else:
                    mm(e, S("SK", 128 * k, 128 * k + 128), S("G1", 16 * w0 + k, 16 * (w0 + m), 16), False, k == 15)
            step("N%d" % c)
            if t:
                ts(S("EU", w0, w0 + m), e, 2048.0, A.mult, eu_add, A.add)

        def wrap(c):
            w0, m, bk = WR[c]
            step(("ET%d" if t else "IT%d") % c)
            act(S("ET", w0, w0 + m), B(bk, w0, w0 + m), F.Sign, bias=odd_tiny, scale=cO)
            step(("EH%d" if t else "IH%d") % c)
            tt(S("EH", w0, w0 + m), B(bk, w0, w0 + m), S("ET", w0, w0 + m), A.subtract)
            if not t:
                step("IN%d" % c)
                ts(S("EU", w0, w0 + m), S("EH", w0, w0 + m), 2048.0, A.mult, 2048.0, A.add)

        def gather_x(j):
            step(("X%d" if t or j not in CFG["XV0"] else "IX%d") % j)
            src = IND(S("REC", 0, 2 * V if t else V), S("EU", 32 * j, 32 * j + 32))
            if j in (XV if t else CFG["XV0"]):
                ts(S("X", 512 * j, 512 * j + 512), src, 192.0, A.add)
            else:
                act(S("X", 512 * j, 512 * j + 512), src, F.Identity, bias=192.0)

        def sums(s):
            step("S%d" % s)
            bk, o = 2 + s // 2, 64 * (s % 2)
            for k in range(16):
                mm(B(bk, o, o + 64), S("I16"), S("X", 1024 * s + k, 1024 * (s + 1), 16), k == 0, k == 15)

        def xk(h, k):
            return S("X", H * h + k, H * (h + 1), 16)

        def mb(h):
            return S("MB", 128 * h, 128 * h + 128)

        def ad(h, k):
            return S("AD", H * h + 128 * k, H * h + 128 * k + 128)

        def distances(h):
            kb, kv = 4 + h, KD[h]
            step("K%d" % h)
            mm(B(kb, 0, 384), S("O32", p=(0, 64)), S("KC", p=(0, 64)), True, False)
            step("KX%d" % h)
            for k in range(kv):
                mm(B(kb, k, 384, 16), xk(h, k), S("BN"), False, False)
            step("M%d" % h)
            if CFG["MEAN"][h] == "v":
                ts(mb(h), B(2 + h, 0, 128), -0.46875, A.add)
            else:
                act(mb(h), B(2 + h, 0, 128), F.Identity, bias=-0.46875)
            step("MP%d" % h)
            if kv:
                mm(B(2 + h, 128, 256), ident, mb(h), True, True)
            step("EM%d" % h)
            if kv > 6:
                mm(B(kb, 0, 384), mb(h), S("BNW", 384 * h, 384 * h + 384), False, False)
            for k in range(kv if kv <= 6 else 0):
                mm(B(kb, k, 384, 16), mb(h), S("BN"), False, False)
            for k in range(kv):
                step("V%d%s" % (h, "abcdefghijklmnop"[k // VG]))
                tt(ad(h, k), xk(h, k), B(2 + h, 128, 256), A.max)
            for k in range(kv):
                step("EV%d%s" % (h, "abcdefghijklmnop"[k // VG]))
                mm(B(kb, k, 384, 16), ad(h, k), S("BP2"), False, False)
            for i, k0 in enumerate(range(kv, 16, 4)):
                ks, bk, c = list(range(k0, min(16, k0 + 4))), 7 - (i & 1), "abcd"[i]
                step("DX%d%s" % (h, c))
                for j, k in enumerate(ks):
                    mm(B(bk, 128 * j, 128 * j + 128), ident, xk(h, k), j == 0, False)
                step("DM%d%s" % (h, c))
                for j, k in enumerate(ks):
                    mm(B(bk, 128 * j, 128 * j + 128), S("NI"), mb(h), False, j == len(ks) - 1)
                step("B%d%s" % (h, c))
                act(S("AD", H * h + 128 * k0, H * h + 128 * (ks[-1] + 1)), B(bk, 0, 128 * len(ks)), F.Abs)
                step("EB%d%s" % (h, c))
                for k in ks:
                    mm(B(kb, k, 384, 16), ad(h, k), S("BP1"), False, False)
            step("R%d" % h)
            mm(B(kb, 0, 128), S("EH", 128 * h, 128 * h + 128), S("I2K"), False, False)
            mm(B(kb, 128, 256), S(wh, 128 * h, 128 * h + 128), ident, False, True)
            step("SC%d" % h)
            scan(S("KF", 512 * h, 512 * h + 384), S("SC"), B(kb, 0, 384), 0.0, A.add, A.min)

        def threshold():
            step("TM")
            x = B(CFG["TH"][0], CFG["TH"][1], CFG["TH"][1] + 1)
            for j in range(2):
                mm(x, S("O32F"), S("ACC", j, j + 1), j == 0, j == 1)
            step("TA")
            act(S("TA", 0, 1), x, F.Identity, bias=1.5 * 2.0 ** 23)
            step("TB")
            act(S("TA", 1, 2), S("TA", 0, 1), F.Identity, scale=-1.0, bias=1.5 * 2.0 ** 23)
            step("TC")
            act(S("TA", 2, 3), x, F.Abs, bias=S("TA", 1, 2))
            step("TD")
            act(S("THR", 0, 1), S("TA", 2, 3), F.Identity, scale=-2.0, bias=-4.5)

        def choose(h):
            tb, w0, s0, b0, cs = CFG["TB"][h], 128 * h, 32 * h, 8 * h, "CS%d" % h

            def row(name):
                return S(name, w0, w0 + 128)

            def bank(name, a=0, b=128):
                return B(tb[name][0], tb[name][1] + a, tb[name][1] + b)

            def tag(s):
                step("%s%d" % (s, h))

            def expand(to, name, start, stop, at=0, shift=0):
                for a in range(4):
                    o, m = at + 32 * a + shift, 32 - (shift if a == 3 else 0)
                    mm(bank(to, o, o + m), S(name, 128 * a, 128 * a + 128), S("PT", s0, s0 + m), start and a == 0, stop and a == 3)

            tag("ZM")
            mm(bank("zz", 0, 8), mb(h), S("WT8"), True, True)
            tag("SQ")
            act(S("SQ", b0, b0 + 8), bank("zz", 0, 8), F.Square, bias=-48560.0)
            tag("ZI")
            ts(S("ZI", b0, b0 + 8), S("SQ", b0, b0 + 8), 1.0 / 32, A.mult, -10952.375, A.add)
            tag("ZA")
            ts(S("ZA", b0, b0 + 8), S("ZI", b0, b0 + 8), V - 1, A.bitwise_and)
            tag("ZP")
            ts(S("P16", s0 + 24, s0 + 32), S("ZA", b0, b0 + 8), -2048.0, A.add)
            keys = S("KF", 512 * h + 15, 512 * h + 384, 16)
            tag("RQ")
            ts(S("RQ", s0, s0 + 24), keys, MAG, A.add, -MAG, A.add)
            tag("PP")
            tt(S("P16", s0, s0 + 24), keys, S("RQ", s0, s0 + 24), A.subtract)
            tag("QS")
            tt(S("QS", b0, b0 + 8), S("RQ", s0, s0 + 8), S("KF", 512 * h + 271, 512 * h + 384, 16), A.add)
            tag("MX")
            tt(S("P16", s0 + 8, s0 + 16), S("P16", s0 + 8, s0 + 16), S("QS", b0, b0 + 8), A.max)
            tag("PT")
            turn(S("PT", s0, s0 + 32), S("P16", s0, s0 + 32))
            tag("QB")
            expand("eq", "XN", True, True)
            tag("EQ")
            tt(row("EQ"), row("EH"), bank("eq"), A.is_equal)
            tag("CM")
            for j in range(4):
                g2, b1 = j // 2, j % 2
                mm(bank("cc", 16 * g2, 16 * g2 + 16), S("CM%d" % g2, 32 - b1, 160 - b1), S("PT", s0 + 16 * b1, s0 + 16 * b1 + 16), j == 0, j == 3)
            tag("CS")
            turn(S(cs, 0, 512, 16), bank("cc", 0, 32))
            tag("BO")
            mm(bank("vo"), S("BO"), row("EQ"), True, True)
            tag("GO")
            act(row("GO"), bank("vo"), F.Sign, bias=S("THR", 0, 1), scale=32.0, acc=(None if last else S("ACC", h, h + 1)))
            tag("RR")
            scan(row("RR"), S("HM", 0, 128), S(cs, 0, 128), 0.0, A.mult, A.add)
            tag("OC")
            ts(S("OC", b0, b0 + 8), S(cs, 0, 128, 16), 8192.0, A.mult, 2048.0, A.add)
            tag("KM")
            expand("kk", "XK", True, True)
            tag("U")
            act(row("U"), bank("kk"), F.Abs, bias=kbias, scale=8192.0)
            tag("SA")
            mm(bank("va"), S("PSH"), row(wh), True, False)
            tag("SB")
            expand("va", "XN", False, True)
            tag("SG")
            act(row("SG"), bank("va"), F.Sign, bias=odd_tiny, scale=cO)
            tag("DA")
            mm(bank("df"), S("HDM"), row(wh), True, False)
            tag("DB")
            expand("df", "XH", False, True)
            tag("PD")
            tt(row("PRD"), row("GO"), bank("df"), A.mult)
            tag("AA")
            mm(bank("av"), S("AVM"), row(wh), True, False)
            tag("AB")
            expand("av", "XA", False, True)
            tag("WO")
            if last:
                tt(row("WF"), row("PRD"), bank("av"), A.add)
                tag("WG")
                act(row("WG"), row("WF"), F.Identity, bias=2048.0)
                dma("a", row("yw"), row("WG"), 4)
            else:
                src, dst, sem = row("WO%d" % t), row("WH%d" % (t + 1)), "arr%d_%d" % (t + 1, h)
                tt(src, row("PRD"), bank("av"), A.add)
                tag("TO")
                op("g", lambda e: e.remote_dma(dst["ap"], src["ap"], T.sem[sem], T.sem.sent, pid, rid, mask_out), [src], [], 100)
                note(line="ring%d" % h)
            tag("OM")
            tt(row("OM"), IND(S("FW"), S("OC", b0, b0 + 8)), row("U"), A.min)
            tag("LA")
            mm(bank("ls"), S("PSH"), row(wh), True, False)
            tag("LB")
            expand("ls", "XN", False, False)
            tag("LC")
            mm(bank("ls"), S("NI"), row("SG"), False, False)
            tag("LD")
            mm(bank("ls"), S("NIU"), row("U"), False, True)
            tag("LS")
            act(row("LS"), bank("ls"), F.Identity, bias=2048.0, scale=2048.0)
            tag("PA")
            mm(bank("pr", 0, 256), ident, S("MSK"), True, False)
            tag("PB")
            expand("pr", "XC", False, False)
            expand("pr", "XC", False, False, 128, 16)
            tag("PC")
            mm(bank("pr"), S("NI2"), row("RR"), False, False)
            mm(bank("pr", 128, 256), S("NI2"), row("RR"), False, False)
            tag("PW")
            mm(bank("pr", 144, 256), S("WIM"), S("GO", w0, w0 + 112), False, False)
            mm(bank("pr"), S("WIM"), row("GO"), False, True)
            tag("PS")
            scan(S("PS", 2 * w0, 2 * w0 + 256), S("PM"), bank("pr", 0, 256), 1.0, A.max, A.mult)
            tag("LO")
            ts(S("LO", 2 * b0, 2 * b0 + 16), S("PS", 2 * w0 + 15, 2 * w0 + 256, 16), 0.0, A.is_equal, 0.125, A.add)
            tag("KA")
            tt(S("K3", b0, b0 + 8), S("LO", 2 * b0, 2 * b0 + 8), S("LO", 2 * b0 + 8, 2 * b0 + 16), A.add)
            tag("KB")
            tt(S("K4", b0, b0 + 8), S("K3", b0, b0 + 8), S(cs, 0, 128, 16), A.add)
            tag("OF")
            for j in range(2):
                ts(S("OFF", b0 + j, b0 + 8, 2), S("K4", b0 + j, b0 + 8, 2), 8192.0, A.mult, dummy[j], A.min)

        def arrive(h):
            sem, nx = "arr%d_%d" % (t + 1, h), S("WH%d" % (t + 1), 128 * h, 128 * h + 128)
            step("WU%d" % h)
            op("v", None, [], [nx], 0)
            note(src=sem, sem=sem, val=n_in, line="ring%d" % h)
            ts(S("WU", 128 * h, 128 * h + 128), nx, 2048.0, A.add)

        if t:
            threshold()
        for h in (1, 0):
            for c in range(len(PC)):
                if PC[c][0] // 128 == h:
                    proposals(c)
            for c in range(len(WR)):
                if WR[c][0] // 128 == h:
                    wrap(c)
            for j in range(4 * h + 3, 4 * h - 1, -1):
                gather_x(j)
            sums(2 * h + 1)
            sums(2 * h)
        for h in (1, 0):
            distances(h)
            choose(h)
        if not last:
            for h in (1, 0):
                arrive(h)
        for b in range(7, -1, -1):
            step("F%d" % b)
            tt(IND(S("FW"), S("OFF", 2 * b, 2 * b + 2)), S("OM", 32 * b, 32 * b + 32), S("LS", 32 * b, 32 * b + 32), A.max)

    now[0], now[1] = NV, "end"
    lat[0] = 0
    for c in range(len(OUT) - 1):
        a, b = OUT[c], OUT[c + 1]
        act(B(2 + c, 0, b - a), S("FW", H + a, H + b), F.Identity, scale=float(V))
        tt(S("YO", a, b), S("FW", a, b), B(2 + c, 0, b - a), A.add)
        dma("s", S("yf", a, b), S("YO", a, b), 4)
        note(t=60 + 128 * 4 * (b - a) / DMARATE, lat=DMA0)
    op("s", None, [S("yw"), S("yf")], [], 0)
    note(src="end")
    depend(ops)
    return ops


def rank_program(g, core, T, topo):
    rank = T.rank_of(core)
    if rank is None:
        return
    n = len(T.cores)
    nxt, prv = T.cores[(rank + 1) % n], T.cores[(rank - 1) % n]
    rid, pid, _ = topo.addr(nxt)
    ops = record(T, (pid, rid, topo.mask(core, nxt), len(topo.engines(prv, core))))
    if "order" not in _KEPT:
        _KEPT["order"] = arrange(ops)
    emit(g, T, ops, _KEPT["order"])
    g.wait_ge(T.sem.sent, len(topo.engines(core, nxt)) * (NV - 1) * 2)
